import numpy as np, ml_dtypes
CORES = [9,25,41,57]
N = 4
BF = ml_dtypes.bfloat16
W, A, S, RO, H = 4096, 128, 4, 6, 2
def parts(rng):
    z = rng.integers(0, 256, (N, 8, 16, W)); w = rng.integers(0, 256, (N, 8, 16, 3)); w[..., 2] = rng.integers(0, 2048, (N, 8, 16))
    return z, w, rng.choice(np.array([750, 850, 950, 1200]), (N, 8, 1, 1))
def loose(rng):
    share = rng.choice(np.array([0.06, 0.15, 0.4, 0.9]), (N, 8, 1, A))
    return np.where(rng.random((N, 8, 16, A)) < share, rng.integers(0, W, (N, 8, 16, A)), -1)
def objects(rng, z, n):
    ix = np.argsort(rng.random((N, 8, W)), axis=-1)[..., :S * 2 * n]
    base = rng.integers(40, 216, (8, 16, 1, 1, n)); dev = rng.integers(-16, 17, (8, 16, 16, 2, n))
    order = np.argsort(rng.random((8, 16, n)), axis=1); rows = np.arange(16)[None, :, None]
    up = rows == order[:, :1]; down = rows == order[:, 1:2]
    v = base + np.where(up[:, None, :, None, :], 16, np.where(down[:, None, :, None, :], -16, dev))
    for q in range(N):
        np.put_along_axis(z[q], np.broadcast_to(ix[q][:, None, :], (8, 16, S * 2 * n)), v[:, :, S * q:S * q + S].reshape(8, 16, S * 2 * n), 2)
    return np.ascontiguousarray(ix.reshape(N, 8, S, 2, n).transpose(1, 0, 2, 3, 4)).reshape(8, 16, 2, n), up | down
def follow(rng, obj, am):
    out = []
    for r in range(N):
        c = rng.integers(0, obj.shape[-1], (8, 1, A))
        one = np.take_along_axis(obj[:, :, 0], c, 2); two = np.take_along_axis(obj[:, :, 1], c, 2); anchor = np.take_along_axis(am, c, 2)
        v = (rng.random((8, 16, A)) < rng.choice(np.array([0, 0, 0.1, 0.5]), (8, 1, A))) & ~anchor
        keep = anchor | (rng.random((8, 16, A)) < rng.random((8, 1, A)))
        out.append(np.where(keep, np.where(v, two, one), -1))
    return np.stack(out)
def pack(z, w, t, p, s):
    return {"tz": np.ascontiguousarray(z.reshape(N, 128, W)).astype(np.float32).astype(BF), "tp": np.ascontiguousarray(p.reshape(N, 128, A)).astype(np.int32),
            "sd": np.ascontiguousarray(s.reshape(N, 128, A)).astype(np.int32), "hw": np.ascontiguousarray(w.reshape(N, 128, 3)).astype(np.int32),
            "th": np.repeat(t.reshape(N, 8, 1), 16, axis=1).astype(np.int32)}
def setup_inputs(rng):
    z, w, t = parts(rng); obj, am = objects(rng, z, A // 4)
    p = np.where(rng.random((N, 8, 1, A)) < 0.5, follow(rng, obj, am), loose(rng))
    s = np.where(rng.random((N, 8, 1, A)) < 0.5, follow(rng, obj, am), loose(rng))
    return pack(z, w, t, p, s)
def setup_inputs_twins(rng):
    z, w, t = parts(rng); obj, am = objects(rng, z, 4); t[:] = 4096
    p = follow(rng, obj, am); p[:, 6:] = loose(rng)[:, 6:]; p[..., A // 2:] = p[..., :A // 2].copy()
    return pack(z, w, t, p, follow(rng, obj, am))
def setup_inputs_ties(rng):
    z, w, t = parts(rng)
    z = np.take_along_axis(rng.integers(0, 256, (N, 8, 16, 6)), rng.integers(0, 6, (N, 8, 1, W)), 3)
    t = rng.choice(np.array([1000, 4096]), (N, 8, 1, 1)); p = loose(rng); s = loose(rng)
    w[:, 0, :, :2] = 0; w[:, 1, :, 2] = 0; w[:, 4, :, 2] = rng.choice(np.array([5, 1031]), (N, 16)); t[:, :2] = 4096
    z[:, 2:4] = 100; t[::2, 2] = 0; t[1::2, 2] = 1; t[:, 3] = 432; p[:, 2:4, :, ::4] = -1
    return pack(z, w, t, p, s)
def setup_inputs_ends(rng):
    z = 255 * rng.integers(0, 2, (N, 8, 16, W)); ends = np.array([-1, 0, 1, W - 2, W - 1])
    p = rng.choice(ends, (N, 8, 16, A)); s = rng.choice(ends, (N, 8, 16, A)); t = rng.choice(np.array([0, 1, 2040, 4080, 4096]), (N, 8, 1, 1))
    w = rng.choice(np.array([0, 1, 254, 255]), (N, 8, 16, 3)); w[..., 2] = rng.choice(np.array([0, 1, 1025, 2046, 2047]), (N, 8, 16))
    p[:, 4] = rng.integers(0, W, (N, 16, A)); t[:, 4] = 4096
    z[:, 5] = 255; w[:, 5, :, :2] = 0; w[:, 5, 0, :2] = 255; w[:, 5, 1, :2] = 2; w[:, 5, :, 2] = 2047; t[:, 5] = 4096
    p[:, 6] = -1; t[:, 6] = 4096
    z[::2, 7] = 255; z[1::2, 7] = 0; p[:, 7] = rng.integers(0, W, (N, 16, A)); p[:, 7, (np.arange(16) // S) % 2 == 1] = -1
    t[1::4, 7] = 4081; t[3::4, 7] = 4080
    w[1::2, 7, :, 0] = 0; w[1::2, 7, :, 1] = 254 * rng.integers(0, 2, (N // 2, 16)); w[1::2, 7, 0, 1] = 255; w[1::2, 7, 0, 2] = rng.integers(1, 2048, N // 2)
    return pack(z, w, t, p, s)
def setup_inputs_sparse(rng):
    z, w, t = parts(rng); t = rng.choice(np.array([900, 4096]), (N, 8, 1, 1)); t[:, 0] = 4096
    p = np.where(rng.random((N, 8, 16, A)) < 0.06, rng.integers(0, W, (N, 8, 16, A)), -1); p[rng.integers(0, N)] = -1
    s = loose(rng); s[:, rng.permutation(8)[:4]] = -1
    return pack(z, w, t, p, s)
def setup_inputs_spread(rng):
    z = np.minimum((np.exp2(8.0 * rng.random((N, 8, 1, W))) * rng.random((N, 8, 16, W))).astype(np.int64), 255)
    w = np.minimum(np.exp2(8.0 * rng.random((N, 8, 16, 3))).astype(np.int64), 255); w[..., 2] = np.minimum(np.exp2(11.0 * rng.random((N, 8, 16))).astype(np.int64), 2047)
    t = np.minimum(np.exp2(7.0 + 5.0 * rng.random((N, 8, 1, 1))).astype(np.int64), 4096)
    ps = []
    for i in range(2):
        nm = np.minimum((W * rng.random((N, 8, 16, A)) ** 3).astype(np.int64), W - 1)
        ps.append(np.where(rng.random((N, 8, 16, A)) < rng.random((N, 8, 1, A)), nm, -1))
    return pack(z, w, t, ps[0], ps[1])
def check_inputs(d):
    bad = []; v = np.asarray(d["tz"]).astype(np.float32)
    if not (np.min(v) >= 0 and np.max(v) <= 255 and np.all(v == np.floor(v))): bad.append("tz: whole numbers from 0 to 255")
    for k, lo, hi in (("tp", -1, W - 1), ("sd", -1, W - 1), ("th", 0, 4096)):
        if np.min(d[k]) < lo or np.max(d[k]) > hi: bad.append("range of " + k)
    w = np.asarray(d["hw"])
    if np.min(w) < 0 or np.max(w[..., :2]) > 255 or np.max(w[..., 2]) > 2047: bad.append("range of hw")
    t = np.asarray(d["th"]).reshape(-1, 16)
    if np.any(t != t[:, :1]): bad.append("th: one number a group")
    return bad
def reference(tz, tp, sd, hw, th):
    z = tz.astype(np.float32).astype(np.int32).reshape(N, 8, 16, W); w = hw.astype(np.int32).reshape(N, 8, 16, 3); lim = th.astype(np.int32).reshape(N, 8, 16)[:, :, :1]
    p = tp.astype(np.int32).reshape(N, 8, 16, A); s = sd.astype(np.int32).reshape(N, 8, 16, A); lower = np.arange(A)[None, :] < np.arange(A)[:, None]
    for t in range(RO):
        for r in range(N):
            q = (r + 1 + t) % N; x = S * q + t // N
            hi = np.zeros((8, 16, A), np.int32); lo = np.full((8, 16, A), 255, np.int32)
            for j in range(16):
                n = p[r, :, j]; on = (n >= 0)[:, None, :]; v = np.take_along_axis(z[j // S], np.maximum(n, 0)[:, None, :], 2)
                hi = np.where(on, np.maximum(hi, v), hi); lo = np.where(on, np.minimum(lo, v), lo)
            e = (hi + lo) >> 1; c = e
            best = np.full((8, A), 4097); name = np.zeros((8, A), np.int64)
            for k in range(H):
                u1 = np.add.reduce(w[q, :, :, 0:1] * c, axis=1) & (W - 1); u2 = np.add.reduce(w[q, :, :, 1:2] * c, axis=1) & (W - 1)
                h = (((u1 * u2) >> 5)[:, None, :] + w[q, :, :, 2:3] * u2[:, None, :]) & (W - 1)
                v = np.take_along_axis(z[q], h.reshape(8, 1, 16 * A), 2).reshape(8, 16, 16, A)
                d = np.add.reduce(np.abs(v - e[:, :, None, :]), axis=1)
                m = np.argmin(d, axis=1); dm = np.min(d, axis=1); n = np.take_along_axis(h, m[:, None, :], 1)[:, 0]
                less = dm < best; name = np.where(less, n, name); best = np.where(less, dm, best)
                c = (e + np.take_along_axis(z[q], n[:, None, :], 2)) >> 1
            n = np.where(best < lim[q], name, -1); p[r, :, x] = n
            low = (n[:, :, None] == n[:, None, :]) & (n >= 0)[:, :, None] & lower
            g, b = np.nonzero(np.count_nonzero(low, axis=2) == 1); a = np.argmax(low[g, b], axis=1)
            pa = p[r][g, :, a]; pb = p[r][g, :, b]; differ = (pa >= 0) & (pb >= 0) & (pa != pb); clash = np.any(differ, axis=1)[:, None]
            p[r][g, :, a] = np.where(clash, np.where(differ, -1, pa), np.where(pa >= 0, pa, pb))
            p[r][g, :, b] = np.where(clash, np.where(differ, -1, pb), s[r][g, :, b])
    return {"yp": p.reshape(N, 128, A).astype(np.float32)}

@@ -1,0 +1,452 @@
+import numpy as np
+from concourse.bass import DstId, RemoteDMATransfer
+from concourse.mybir import AluOpType as O, ActivationFunctionType as F
+
+N, W, A, S, RO = 4, 4096, 128, 4, 6
+BLK = W + 16
+M1, M4, M12 = 1.5 * 2.0 ** 24, 1.5 * 2.0 ** 27, 1.5 * 2.0 ** 35
+SPLIT_E = 72
+SPLIT_V = 64
+OWN = [(0, 1088), (1088, 2176)]
+HELP = [(2176, 3136), (3136, 4096)]
+
+SCRATCH = {}
+for _n, _c, _d in (
+        ("zall", N * BLK, "bfloat16"), ("zh", HELP[-1][1] - HELP[0][0], "bfloat16"), ("hwi", 16, "int32"), ("hwf", 16, "float32"),
+        ("tpi", 256, "int32"), ("tpf", 256, "float32"), ("P", 256, "float32"), ("Pw", 256, "float32"), ("Pm", 128, "float32"),
+        ("Q", 256, "float32"), ("offs", 128, "uint16"), ("hl", 128, "uint16"), ("l0", 8, "uint16"), ("L", 8, "uint16"),
+        ("Ve", 2048, "bfloat16"), ("Va", 2048, "bfloat16"), ("Hi", 2048, "bfloat16"), ("Lo", 2048, "bfloat16"),
+        ("V", 2048, "bfloat16"), ("Mx", 2048, "bfloat16"), ("E2", 128, "bfloat16"), ("C2", 128, "bfloat16"), ("Epl", 128, "float32"),
+        ("cs", 128, "float32"), ("uq", 256, "float32"), ("u1", 128, "float32"), ("pr", 128, "int32"), ("sh", 128, "int32"),
+        ("sm", 128, "int32"), ("hn", 128, "int32"), ("G", 256, "float16"), ("km", 128, "float32"), ("q8", 8, "float32"),
+        ("Zb", 128, "bfloat16"), ("Ze", 128, "bfloat16"), ("Zm", 128, "bfloat16"), ("kf0", 8, "float32"), ("Zf", 128, "float32"),
+        ("kfr", 128, "float32"), ("OH", 256, "bfloat16"), ("pd", 256, "float16"), ("SU", 128, "bfloat16"), ("Ux", 128, "float16"),
+        ("rs", 128, "float16"), ("nc", 8, "float32"), ("X", 1024, "bfloat16"), ("iM", 128, "bfloat16"), ("iU", 128, "bfloat16"),
+        ("vl", 128, "bfloat16"), ("mn", 128, "float32"), ("aa", 128, "float32"), ("dif", 128, "bfloat16"), ("sB", 128, "float32"),
+        ("B0", 128, "float32"), ("B1", 128, "float32"), ("y0", 128, "float32"), ("y1", 128, "float32"), ("y2", 128, "float32"),
+        ("on", 128, "bfloat16"), ("BD", 128, "bfloat16"), ("Ib", 128, "bfloat16"), ("If", 128, "float32"), ("onf", 128, "float32"),
+        ("HI", 128, "bfloat16"), ("NH", 128, "bfloat16"), ("CU", 256, "bfloat16"), ("BDE", 128, "bfloat16"), ("IV", 8, "bfloat16"),
+        ("IM", 8, "bfloat16"), ("I1", 8, "bfloat16"), ("Ih", 8, "float16"), ("I16", 8, "float32"), ("thx", 32, "float32"),
+        ("TH", 32, "float32"), ("W1", 512, "bfloat16"), ("W2", 512, "bfloat16"), ("KC", 256, "bfloat16"), ("d0h", 2048, "bfloat16"),
+        ("d0l", 2048, "bfloat16"), ("d0k", 128, "float32"), ("s1b", 128, "bfloat16"), ("s1f", 128, "float32"), ("CT1", 8, "float32"),
+        ("CT2", 8, "bfloat16"), ("CC", 384, "bfloat16"), ("Wt", 48, "bfloat16"), ("MB", 512, "bfloat16"), ("GO", 1024, "float16"),
+        ("Sx", 768, "float16"), ("zb", 768, "bfloat16"), ("N4", 128, "bfloat16"), ("C32", 128, "bfloat16"), ("CSX", 256, "bfloat16"),
+        ("IP", 128, "bfloat16"), ("IN", 128, "bfloat16"), ("CAB", 256, "bfloat16"), ("cA", 128, "bfloat16"), ("cB", 128, "bfloat16"),
+        ("Uf", 128, "float32"), ("jc", 1, "float32"), ("bc", 1, "float32"), ("rx", 8, "float32"), ("cx", 8, "float32"),
+        ("ji", 128, "int32"), ("jj", 128, "int32"), ("jk", 128, "int32"), ("mf", 128, "float32"), ("t8", 8, "float32")):
+    SCRATCH[_n] = ("sbuf", [128, _c], _d)
+BANKS = ("bV", "bA", "bB", "bE", "bK0", "bK1", "bR0", "bR1")
+for _n in BANKS:
+    SCRATCH[_n] = ("psum", [128, 512], "float32")
+SEMAPHORES = (["cV", "cS", "cT", "cG", "ldp", "ldh", "st", "lsem"] + ["ld%d" % i for i in range(4)] + ["tz%d" % i for i in range(N)]
+              + ["hw%d" % i for i in range(N)] + ["hx%d" % i for i in range(len(HELP))])
+
+
+def Tracker(g, T):
+    eng = {"V": g.vector, "S": g.scalar, "T": g.tensor, "G": g, "Y": g.sync}
+    cnt = {e: 0 for e in eng}; know = {e: {} for e in eng}; snap = {}; acc = {}
+
+    def need(e, needs):
+        while True:
+            todo = {s: n for s, n in needs.items() if know[e].get(s, 0) < n}
+            if not todo:
+                return
+            s = max(todo, key=lambda k: sum(1 for j in todo if j != k and snap.get((k, todo[k]), {}).get(j, 0) >= todo[j]))
+            n = todo[s]
+            eng[e].wait_ge(T.sem[s], n)
+            for k, v in snap.get((s, n), {}).items():
+                know[e][k] = max(know[e].get(k, 0), v)
+            know[e][s] = max(know[e].get(s, 0), n)
+
+    def conflicts(e, refs, write, needs):
+        for nm, lo, hi, st in refs:
+            bank = nm in BANKS
+            for w, ee, s, n, l2, h2, st2 in acc.get(nm, ()):
+                over = lo < h2 and l2 < hi and not (st == st2 > 1 and (lo - l2) % st)
+                if ee == e:
+                    hit = over and w and not (e == "T" and bank)
+                else:
+                    hit = bank or (over and (w or write))
+                if hit:
+                    needs[s] = max(needs.get(s, 0), n)
+
+    def note(e, s, n, refs, write):
+        for nm, lo, hi, st in refs:
+            keep = []
+            for a in acc.get(nm, ()):
+                cover = lo <= a[4] and a[5] <= hi and (st == 1 or (st == a[6] and (lo - a[4]) % st == 0))
+                if not (cover and (write or (not a[0] and a[1] == e))):
+                    keep.append(a)
+            acc[nm] = keep + [(write, e, s, n, lo, hi, st)]
+
+    def ref(r):
+        return (r[0], r[1], r[2], r[3] if len(r) > 3 else 1)
+
+    def ap(r):
+        return T[r[0]][:, r[1]:r[2]:r[3]] if len(r) > 3 else T[r[0]][:, r[1]:r[2]]
+
+    def op(e, outs, ins, call):
+        needs = {}
+        ro, ri = [ref(r) for r in outs], [ref(r) for r in ins]
+        conflicts(e, ri, False, needs)
+        conflicts(e, ro, True, needs)
+        need(e, needs)
+        cnt[e] += 1
+        s = "c" + e
+        snap[(s, cnt[e])] = dict(know[e])
+        call().then_inc(T.sem[s], 1)
+        note(e, s, cnt[e], ri, False)
+        note(e, s, cnt[e], ro, True)
+
+    def landed(sem, n, refs):
+        note("dma", sem, n, [ref(r) for r in refs], True)
+
+    def before(e, ins):
+        needs = {}
+        conflicts(e, [ref(r) for r in ins], False, needs)
+        need(e, needs)
+    return {"op": op, "ap": ap, "landed": landed, "before": before, "cnt": cnt, "need": need}
+
+
+def rank_program(g, core, T, topo):
+    rank = T.rank_of(core)
+    helpers = []
+    for c in T.cores:
+        helpers.append([k for k in topo.cores_of(c) if topo.die(k) != topo.die(c) and k not in T.cores
+                        and all(topo.may_write(k, d) for d in T.cores if d != c)][0])
+    if rank is None:
+        if core in helpers:
+            helper_program(g, core, T, topo, helpers.index(core))
+        return
+    others = [c for c in T.cores if c != core]
+    K = Tracker(g, T)
+    op, ap = K["op"], K["ap"]
+
+    def ind(win, off):
+        return ap(win).indirect(ap(off))
+
+    def tt(out, a, b, o, win=None):
+        op("V", [out], [a, b] + ([win] if win else []), lambda: g.vector.tensor_tensor(ap(out), ind(win, a) if win else ap(a), ap(b), o))
+
+    def ts(out, a, s1, o1, s2=None, o2=None):
+        ins = [a] + [s for s in (s1, s2) if isinstance(s, tuple)]
+        f = lambda s: ap(s) if isinstance(s, tuple) else s
+        if o2 is None:
+            op("V", [out], ins, lambda: g.vector.tensor_scalar(ap(out), ap(a), f(s1), None, o1))
+        else:
+            op("V", [out], ins, lambda: g.vector.tensor_scalar(ap(out), ap(a), f(s1), f(s2), o1, o2))
+
+    def cp(out, a):
+        op("V", [out], [a], lambda: g.vector.tensor_copy(ap(out), ap(a)))
+
+    def gat(out, win, off):
+        op("V", [out], [win, off], lambda: g.vector.tensor_copy(ap(out), ind(win, off)))
+
+    def sgat(out, win, off):
+        op("S", [out], [win, off], lambda: g.scalar.activation(ap(out), ind(win, off), F.Copy))
+
+    def scat(win, off, a):
+        op("V", [win], [off, a], lambda: g.vector.tensor_copy(ind(win, off), ap(a)))
+
+    def scan(out, d0, d1, o0, o1):
+        op("V", [out], [d0, d1], lambda: g.vector.tensor_tensor_scan(ap(out), ap(d0), ap(d1), 0.0, o0, o1))
+
+    def fill(out, c, p0=0, p1=128):
+        op("V", [out], [], lambda: g.vector.memset(T[out[0]][p0:p1, out[1]:out[2]] if len(out) < 4 else ap(out), c))
+
+    def mm(out, l, r, start, stop):
+        op("T", [out], [l, r], lambda: g.tensor.matmul(ap(out), ap(l), ap(r), start, stop))
+
+    def act(out, a, f, **k):
+        op("S", [out], [a], lambda: g.scalar.activation(ap(out), ap(a), f, **k))
+
+    def sel(out, a, pattern, o, base, cm):
+        op("G", [out], [a], lambda: g.affine_select(ap(out), ap(a), pattern, o, 0.0, base, cm))
+
+    def iota(out, pattern, base, cm, **k):
+        op("G", [out], [], lambda: g.iota(ap(out), pattern, base, cm, **k))
+
+    def b(n, lo=0, hi=128, *st):
+        return (n, lo, hi) + st
+    BM, PS, X1, X2 = [("bV", 128 * i, 128 * i + 128) for i in range(4)]
+    fl = {"allow_small_or_imprecise_dtypes": True}
+
+    base = rank * BLK
+    chunks = [HELP[0], OWN[0], HELP[1], OWN[1]]
+    for i, (c0, c1) in enumerate(chunks):
+        q = g.sync if i % 2 == 0 else g.scalar
+        q.dma_start(T.zall[:, base + c0:base + c1], T.tz[:, c0:c1]).then_inc(T.sem["ld%d" % i], 16)
+        K["landed"]("ld%d" % i, 16, [("zall", base + c0, base + c1)])
+    g.scalar.dma_start(T.hwi[:, 4 * rank:4 * rank + 3], T.hw[:, :]).then_inc(T.sem.ldh, 16)
+    g.scalar.dma_start(T.hwi[:, 4 * rank + 3:4 * rank + 4], T.th[:, :]).then_inc(T.sem.ldh, 16)
+    g.sync.dma_start(T.tpi[:, 0:128], T.tp[:, :]).then_inc(T.sem.ldp, 16)
+    g.sync.dma_start(T.tpi[:, 128:256], T.sd[:, :]).then_inc(T.sem.ldp, 16)
+    K["landed"]("ldh", 32, [("hwi", 4 * rank, 4 * rank + 4)])
+    K["landed"]("ldp", 32, [("tpi", 0, 256)])
+
+    fill(b("on"), 1.0)
+    fill(b("onf"), 1.0)
+    sel(b("OH"), b("on"), [[-16, 8], [0, 16]], O.is_ge, 0, 1)
+    sel(b("BD"), b("OH"), [[16, 8], [0, 16]], O.is_ge, 15, -1)
+    sel(b("If"), b("onf"), [[-1, 128]], O.is_equal, 0, 1)
+
+    h = helpers[rank]
+    spare = [e for e in topo.engines(core, h) if e not in topo.engines(core, others[0])]
+    eo = len(topo.engines(core, others[0]))
+    local = 0
+    to = [DstId(rid=topo.addr(c)[0], pnc=topo.addr(c)[1]) for c in others]
+
+    def to_others(buf, lo, hi, sem):
+        t = RemoteDMATransfer(dst_ids=to, dma_engine_mask=topo.mask(core, others[0]), remote_sem=T.sem[sem],
+                              srcs=[T[buf][:, lo:hi]], dsts=[T[buf][:, lo:hi] for _ in others])
+        g.remote_dma_fused([t], local_sem=T.sem.lsem)
+        return eo
+    for i, (c0, c1) in enumerate(chunks):
+        K["before"]("G", [("zall", base + c0, base + c1)])
+        if i % 2 == 0:
+            t = RemoteDMATransfer(dst_ids=[DstId(rid=topo.addr(h)[0], pnc=topo.addr(h)[1])], dma_engine_mask=sum(1 << e for e in spare),
+                                  remote_sem=T.sem["hx%d" % (i // 2)], srcs=[T.zall[:, base + c0:base + c1]],
+                                  dsts=[T.zh[:, c0 - HELP[0][0]:c1 - HELP[0][0]]])
+            g.remote_dma_fused([t], local_sem=T.sem.lsem)
+            local += len(spare)
+        else:
+            local += to_others("zall", base + c0, base + c1, "tz%d" % rank)
+        if i == 1:
+            K["before"]("G", [("hwi", 4 * rank, 4 * rank + 4)])
+            local += to_others("hwi", 4 * rank, 4 * rank + 4, "hw%d" % rank)
+    for q in range(N):
+        if q != rank:
+            K["landed"]("tz%d" % q, eo * (len(OWN) + len(HELP)), [("zall", q * BLK, q * BLK + W)])
+            K["landed"]("hw%d" % q, eo, [("hwi", 4 * q, 4 * q + 4)])
+
+    iota(b("ji"), [[0, 8], [-1, 16]], 128, 1)
+    iota(b("KC"), [[0, 8], [1, 16]], 0, 0, **fl)
+    iota(b("CT1", 0, 8), [[16, 8]], 0, 1, **fl)
+    iota(b("Uf"), [[16, 128]], 2050, 0, **fl)
+    iota(b("y0"), [[0, 128]], 0, 1, **fl)
+    fill(b("y1"), 8192.0)
+    sel(b("y2"), b("y1"), [[-1, 128]], O.is_ge, 0, 1)
+    for q in range(N):
+        fill(b("zall", q * BLK + W, (q + 1) * BLK), -256.0)
+    for nm, w, lo, hi in (("d0h", 2048, 255.0, 0.0), ("d0l", 2048, 0.0, 255.0), ("d0k", 128, -1.0e9, 1.0e9), ("s1b", 128, 1.0, 0.0), ("s1f", 128, 1.0, 0.0)):
+        fill(b(nm, 0, w), lo)
+        fill(b(nm, 0, w, 16), hi)
+    for nm, w in (("Zb", 128), ("Zf", 128), ("SU", 128), ("Q", 256), ("zb", 768)):
+        fill(b(nm, 0, w), 0.0)
+    fill(b("NH"), -0.5)
+    fill(b("CU", 0, 256), -16.0)
+    fill(b("CU", 0, 256), -15.5, 0, 1)
+    fill(b("C32"), 32.0)
+    fill(b("CSX"), -16384.0); fill(b("CSX", 128, 256), 16384.0)
+    fill(b("CAB"), 8192.0); fill(b("CAB", 128, 256), -8192.0)
+    cp(b("Ib"), b("If"))
+    for nm, c in (("HI", 0.5), ("IP", 32768.0), ("IN", -32768.0), ("N4", -4096.0)):
+        ts(b(nm), b("Ib"), c, O.mult)
+    bd16 = b("BD", 0, 128, 16)
+    ts(b("BDE"), b("BD"), -16.0, O.mult)
+    ts(b("cB"), b("BD"), 16384.0, O.mult)
+    for nm, c in (("IV", -32.0), ("IM", 64.0), ("I1", 1.0), ("Ih", 1.0), ("I16", 0.0625)):
+        ts(b(nm, 0, 8), bd16, c, O.mult)
+    ts(b("mn"), b("If"), 262144.0, O.mult)
+    ts(b("mf"), b("BD"), -16384.0, O.mult)
+    tt(b("cA"), b("mn"), b("mf"), O.add)
+    for i in range(8):
+        ts(b("GO", 128 * i, 128 * i + 128), b("on"), b("BD", 16 * i, 16 * i + 1), O.mult)
+    for i in range(4):
+        cp(b("MB", 128 * i, 128 * i + 128), b("y2"))
+    ts(b("jj"), b("ji"), 15, O.bitwise_and)
+    ts(BM, b("jj"), 0, O.is_equal)
+    ts(b("mf"), b("jj"), 0, O.is_equal)
+    cp(b("jc", 0, 1), b("jj", 0, 1))
+    ts(b("jk", 0, 1), b("jj", 0, 1), 2, O.arith_shift_right)
+    ts(b("bc", 0, 1), b("jk", 0, 1), float(BLK), O.mult, 2048.0, O.add)
+    xs = [S * ((rank + 1 + t) % N) + t // N for t in range(RO)]
+    cp(b("Sx", 0, 768), b("zb", 0, 768))
+    for t, x in enumerate(xs):
+        ts(b("rx", t, t + 1), b("jc", 0, 1), float(x), O.is_equal)
+        ts(b("cx", t, t + 1), b("rx", t, t + 1), 8192.0, O.mult, -4096.0, O.add)
+        cp(b("Sx", 128 * t + x, 128 * t + 128, 16), b("BD", x, 128, 16))
+    ts(b("KC", 128, 256), b("KC"), 8.5, O.add)
+    ts(b("KC"), b("KC"), -7.5, O.add)
+    tt(b("t8", 0, 1), b("y0", 0, 1), b("jc", 0, 1), O.subtract)
+    ts(b("q8", 0, 8), b("CT1", 0, 8), b("t8", 0, 1), O.subtract)
+    ts(b("CT2", 0, 8), b("q8", 0, 8), 128.0, O.add)
+    ts(b("CT1", 0, 8), b("q8", 0, 8), 16.0, O.mult, 7.5, O.add)
+    ts(b("CC", 0, 384, 3), b("mf"), -4.0, O.mult, 4.0, O.add)
+    ts(b("CC", 1, 384, 3), b("y0"), -1.0, O.mult)
+    ts(b("CC", 2, 384, 3), b("y0"), 0.0, O.mult)
+    fill(b("Wt", 0, 48), 1.0)
+    ts(b("Wt", 1, 48, 3), b("y0", 0, 16), -128.0, O.add)
+    ts(b("tpf", 0, 256), b("tpi", 0, 256), 0, O.is_lt, 8192.0, O.mult)
+    ts(b("Pw", 0, 256), b("tpi", 0, 256), -2048, O.add)
+    tt(b("P", 0, 256), b("Pw", 0, 256), b("tpf", 0, 256), O.add)
+    SD = b("P", 128, 256)
+    for q in [rank] + [(rank + i) % N for i in range(1, N)]:
+        cp(b("hwf", 4 * q, 4 * q + 4), b("hwi", 4 * q, 4 * q + 4))
+        ts(b("W1", 128 * q, 128 * q + 128), b("BD"), b("hwf", 4 * q, 4 * q + 1), O.mult, 0.5, O.mult)
+        ts(b("W2", 128 * q, 128 * q + 128), b("BD"), b("hwf", 4 * q + 1, 4 * q + 2), O.mult, 0.5, O.mult)
+        ts(b("thx", 8 * q, 8 * q + 8), b("I16", 0, 8), b("hwf", 4 * q + 3, 4 * q + 4), O.mult)
+    mm(b("bA", 0, 32), b("onf"), b("thx", 0, 32), True, True)
+    ts(b("TH", 0, 32), b("bA", 0, 32), 32.0, O.mult, -7.75, O.add)
+
+    def hash_mm(C, q):
+        mm(b("bA", 0, 256), b("on"), b("CU", 0, 256), True, False)
+        w1, w2 = b("W1", 128 * q, 128 * q + 128), b("W2", 128 * q, 128 * q + 128)
+        mm(b("bA", 0, 128), w1, b(C), False, False)
+        mm(b("bA", 128, 256), w2, b(C), False, True)
+        mm(b("bB", 0, 128), w1, b(C), True, True)
+        mm(b("bB", 128, 256), w2, b(C), True, True)
+
+    def hash_v(q):
+        ts(b("uq", 0, 256), b("bA", 0, 256), M12, O.add, -M12, O.add)
+        tt(b("u1"), b("bB", 0, 128), b("uq", 0, 128), O.subtract)
+        tt(X1, b("bB", 128, 256), b("uq", 128, 256), O.subtract)
+        tt(b("pr"), b("u1"), X1, O.mult)
+        ts(X2, X1, b("hwf", 4 * q + 2, 4 * q + 3), O.mult)
+        ts(b("sh"), b("pr"), 5, O.arith_shift_right)
+        tt(b("sm"), b("sh"), X2, O.add)
+        ts(b("hn"), b("sm"), 4095, O.bitwise_and)
+        cp(b("hl"), b("hn"))
+
+    def search(q, p):
+        win = b("zall", q * BLK, q * BLK + W)
+        c = 16 * SPLIT_V
+        sgat(b("V", c, 2048), win, b("hl", SPLIT_V, 128))
+        gat(b("V", 0, c), win, b("hl", 0, SPLIT_V))
+        ts(b("G", 128 * p, 128 * p + 128), b("hn"), -2048.0, O.add)
+        bk = "bK%d" % p
+
+        def vm(m):
+            mm(b(bk, m, 128, 16), b("V", m, 2048, 16), b("IV", 0, 8), False, False)
+        vm(0)
+        vm(1)
+        for m in range(16):
+            tt(b("Mx", m, 2048, 16), b("V", m, 2048, 16), b("bE"), O.max)
+            mm(b(bk, m, 128, 16), b("Mx", m, 2048, 16), b("IM", 0, 8), False, m == 15)
+            if m < 14:
+                vm(m + 2)
+
+    def key_mm(p):
+        mm(b("bK%d" % p), b("Ib"), b("KC", 128 * p, 128 * p + 128), True, False)
+        mm(b("bK%d" % p), b("E2"), b("BDE"), False, False)
+
+    for t in range(RO):
+        q = (rank + 1 + t) % N
+        x = xs[t]
+        km8, th8, z16 = b("km", 15, 128, 16), b("TH", 8 * q, 8 * q + 8), b("Zf", 0, 128, 16)
+        ts(b("offs"), b("P"), 2048.0, O.min, b("bc", 0, 1), O.add)
+        c, h2 = 16 * SPLIT_E, 8 * SPLIT_E
+        sgat(b("Ve", c, 2048), b("zall", 0, N * BLK), b("offs", SPLIT_E, 128))
+        gat(b("Ve", 0, c), b("zall", 0, N * BLK), b("offs", 0, SPLIT_E))
+        mm(b("bE", 128, 256), b("Ib"), b("NH"), True, False)
+        pieces = [(c, 2048), (0, h2), (h2, c)]
+        for lo, hi in pieces:
+            act(b("Va", lo, hi), b("Ve", lo, hi), F.Abs)
+        for lo, hi in ((0, c), (c, 2048)):
+            scan(b("Hi", lo, hi), b("d0h", lo, hi), b("Ve", lo, hi), O.min, O.max)
+        for lo, hi in pieces:
+            scan(b("Lo", lo, hi), b("d0l", lo, hi), b("Va", lo, hi), O.max, O.min)
+        mm(b("bE", 128, 256), b("Ib"), b("Hi", 15, 2048, 16), False, False)
+        mm(b("bE", 128, 256), b("Ib"), b("Lo", 15, 2048, 16), False, True)
+        ts(b("E2"), b("bE", 128, 256), M1, O.add, -M1, O.add)
+        act(b("Epl"), b("E2"), F.Identity, scale=0.5, bias=-0.5)
+        hash_mm("E2", q)
+        mm(b("bE"), b("HI"), b("E2"), True, True)
+        key_mm(0)
+        ts(b("Pm"), b("P"), b("cx", t, t + 1), O.max)
+        hash_v(q)
+        search(q, 0)
+        scan(b("km"), b("d0k"), b("bK0"), O.max, O.min)
+        ts(b("q8", 0, 8), km8, M4, O.add, -M4, O.add)
+        tt(b("Zb", 0, 128, 16), km8, b("q8", 0, 8), O.subtract)
+        scan(b("Ze"), b("s1b"), b("Zb"), O.mult, O.add)
+        tt(b("Zm"), b("Ze"), BM, O.mult)
+        mm(b("bA", 256, 264), b("If"), b("CT1", 0, 8), True, False)
+        mm(b("bA", 256, 264), b("Zm"), b("I1", 0, 8), False, True)
+        key_mm(1)
+        mm(b("bR0", 0, 512), b("Ib"), b("MB", 0, 512), True, False)
+        mm(b("bR1", 0, 512), b("Ib"), b("MB", 0, 512), True, False)
+        tt(b("kf0", 0, 8), km8, th8, O.min)
+        cp(b("l0", 0, 8), b("bA", 256, 264))
+        tt(b("cs"), b("l0", 0, 8), b("Epl"), O.add, win=b("V", 0, 2048))
+        ts(b("C2"), b("cs"), M1, O.add, -M1, O.add)
+        hash_mm("C2", q)
+        fill(b("SU"), 0.0)
+        ts(b("Ux"), b("Uf"), b("rx", t, t + 1), O.mult)
+        hash_v(q)
+        search(q, 1)
+        scan(b("km"), b("d0k"), b("bK1"), O.max, O.min)
+        tt(z16, km8, b("kf0", 0, 8), O.min)
+        scan(b("kfr"), b("s1f"), b("Zf"), O.mult, O.add)
+        tt(b("OH"), b("kfr"), b("bK0"), O.is_equal)
+        tt(b("OH", 128, 256), b("kfr"), b("bK1"), O.is_equal)
+        tt(b("SU", x, 128, 16), z16, th8, O.is_lt)
+        mm(b("bA", 0, 128), b("OH"), b("Ib"), True, True)
+        mm(b("bE"), b("OH", 128, 256), b("Ib"), True, True)
+        tt(b("pd"), b("bA"), b("G"), O.mult)
+        tt(b("pd", 128, 256), b("bE"), b("G", 128, 256), O.mult)
+        sx = b("Sx", 128 * t, 128 * t + 128)
+        mm(b("bB"), b("on"), b("C32"), True, False)
+        mm(b("bB"), b("SU"), b("N4"), False, False)
+        mm(b("bB"), sx, b("pd"), False, False)
+        mm(b("bB"), sx, b("pd", 128, 256), False, True)
+        mm(b("bK0", 0, 384), b("Ib"), b("CC", 0, 384), True, False)
+        tt(b("rs"), b("bB"), b("Ux"), O.min)
+        mm(b("bA", 0, 8), b("rs"), b("Ih", 0, 8), True, True)
+        for i in range(8):
+            mm(b("bR%d" % (i // 4), 128 * (i % 4), 128 * (i % 4) + 128), b("GO", 128 * i, 128 * i + 128), b("rs"), False, i % 4 == 3)
+        tt(b("Pw"), b("Pm"), b("bB"), O.min)
+        tt(b("Pw", 128, 256), b("Pm"), b("bB"), O.min)
+        tt(PS, b("Pm"), b("bB"), O.min)
+        cp(b("nc", 0, 8), b("bA", 0, 8))
+        for i in range(8):
+            xg = b("X", 128 * i, 128 * i + 128)
+            ts(xg, b("bR%d" % (i // 4), 128 * (i % 4), 128 * (i % 4) + 128), b("nc", i, i + 1), O.is_equal)
+            mm(b("bK0", 48 * i, 48 * i + 48), xg, b("Wt", 0, 48), False, i == 7)
+        mm(b("bA", 256, 264), b("Ib"), b("CT2", 0, 8), True, False)
+        ts(b("iM"), b("bK0", 0, 384, 3), 1.0, O.is_equal)
+        tt(b("vl"), b("iM"), b("bK0", 1, 384, 3), O.mult)
+        mm(b("bA", 256, 264), b("vl"), b("I1", 0, 8), False, True)
+        ts(b("iU"), b("bK0", 2, 384, 3), 1.0, O.is_equal)
+        mm(b("bK1", 0, 256), b("Ib"), b("CSX", 0, 256), True, False)
+        mm(b("bK1", 0, 128), b("iU"), b("IP"), False, False)
+        mm(b("bK1", 128, 256), b("iU"), b("IN"), False, True)
+        mm(b("bB", 0, 256), b("Ib"), b("CAB", 0, 256), True, False)
+        cp(b("L", 0, 8), b("bA", 256, 264))
+        gat(b("Q"), b("Pw", 0, 256), b("L", 0, 8))
+        scat(b("Q", 0, 256), b("L", 0, 8), b("Pw"))
+        tt(b("sB"), SD, b("bK1", 128, 256), O.max)
+        tt(X1, b("Q"), PS, O.max)
+        tt(b("mn"), b("Q"), PS, O.min)
+        ts(X2, X1, 2048.0, O.is_lt)
+        tt(b("aa"), X1, b("mn"), O.subtract)
+        tt(b("dif"), b("aa"), X2, O.min)
+        mm(b("bB", 0, 128), b("cA"), b("dif"), False, False)
+        mm(b("bB", 128, 256), b("cB"), b("dif"), False, True)
+        tt(X1, b("mn"), b("bK1", 0, 128), O.max)
+        tt(b("B0"), b("sB"), X1, O.min)
+        tt(X2, b("Pw"), b("bB", 0, 128), O.max)
+        tt(b("B1"), b("B0"), b("bB", 128, 256), O.max)
+        tt(b("P"), b("B1"), X2, O.min)
+    ts(b("y0"), b("P"), 4096.0, O.min, 2049.0, O.add)
+    ts(b("y1"), b("P"), 2048.0, O.is_lt)
+    tt(b("y2"), b("y0"), b("y1"), O.mult)
+    ts(b("B0"), b("y2"), -1.0, O.add)
+    K["before"]("Y", [b("B0")])
+    g.sync.dma_start(T.yp[:, :], T.B0[:, :]).then_inc(T.sem.st, 16)
+    K["need"]("Y", {"c" + e: K["cnt"][e] for e in "VSTG"})
+    g.sync.wait_ge(T.sem.st, 16)
+    g.wait_ge(T.sem.lsem, local)
+
+
+def helper_program(g, core, T, topo, r):
+    dests = [c for i, c in enumerate(T.cores) if i != r]
+    n_in = len([e for e in topo.engines(T.cores[r], core) if e not in topo.engines(T.cores[r], dests[0])])
+    ids = [DstId(rid=topo.addr(c)[0], pnc=topo.addr(c)[1]) for c in dests]
+    o = HELP[0][0]
+    for i, (c0, c1) in enumerate(HELP):
+        g.wait_ge(T.sem["hx%d" % i], n_in)
+        t = RemoteDMATransfer(dst_ids=ids, dma_engine_mask=topo.mask(core, dests[0]), remote_sem=T.sem["tz%d" % r],
+                              srcs=[T.zh[:, c0 - o:c1 - o]], dsts=[T.zall[:, r * BLK + c0:r * BLK + c1] for _ in dests])
+        g.remote_dma_fused([t], local_sem=T.sem.lsem)
+    g.wait_ge(T.sem.lsem, len(HELP) * len(topo.engines(core, dests[0])))

@@ -1,50 +1,105 @@
-import numpy as np
 from concourse.bass import DstId, RemoteDMATransfer
 from concourse.mybir import AluOpType as O, ActivationFunctionType as F
 
-N, W, A, S, RO = 4, 4096, 128, 4, 6
-BLK = W + 16
-M1, M4, M12 = 1.5 * 2.0 ** 24, 1.5 * 2.0 ** 27, 1.5 * 2.0 ** 35
-SPLIT_E = 72
-SPLIT_V = 64
-OWN = [(0, 1088), (1088, 2176)]
-HELP = [(2176, 3136), (3136, 4096)]
+N, W, RO = 4, 4096, 6
+EMPTY = 6144.0
+M1, M13 = 1.5 * 2.0 ** 24, 1.5 * 2.0 ** 36
+NAT = 272
+MID = ((0, 512, "S"), (512, 1024, "S"))
+CAND = ((0, 256, "S"), (256, 512, "S"), (512, 768, "S"), (768, 1024, "S"))
 
 SCRATCH = {}
 for _n, _c, _d in (
-        ("zall", N * BLK, "bfloat16"), ("zh", HELP[-1][1] - HELP[0][0], "bfloat16"), ("hwi", 16, "int32"), ("hwf", 16, "float32"),
-        ("tpi", 256, "int32"), ("tpf", 256, "float32"), ("P", 256, "float32"), ("Pw", 256, "float32"), ("Pm", 128, "float32"),
-        ("Q", 256, "float32"), ("offs", 128, "uint16"), ("hl", 128, "uint16"), ("l0", 8, "uint16"), ("L", 8, "uint16"),
-        ("Ve", 2048, "bfloat16"), ("Va", 2048, "bfloat16"), ("Hi", 2048, "bfloat16"), ("Lo", 2048, "bfloat16"),
-        ("V", 2048, "bfloat16"), ("Mx", 2048, "bfloat16"), ("E2", 128, "bfloat16"), ("C2", 128, "bfloat16"), ("Epl", 128, "float32"),
-        ("cs", 128, "float32"), ("uq", 256, "float32"), ("u1", 128, "float32"), ("pr", 128, "int32"), ("sh", 128, "int32"),
-        ("sm", 128, "int32"), ("hn", 128, "int32"), ("G", 256, "float16"), ("km", 128, "float32"), ("q8", 8, "float32"),
-        ("Zb", 128, "bfloat16"), ("Ze", 128, "bfloat16"), ("Zm", 128, "bfloat16"), ("kf0", 8, "float32"), ("Zf", 128, "float32"),
-        ("kfr", 128, "float32"), ("OH", 256, "bfloat16"), ("pd", 256, "float16"), ("SU", 128, "bfloat16"), ("Ux", 128, "float16"),
-        ("rs", 128, "float16"), ("nc", 8, "float32"), ("X", 1024, "bfloat16"), ("iM", 128, "bfloat16"), ("iU", 128, "bfloat16"),
-        ("vl", 128, "bfloat16"), ("mn", 128, "float32"), ("aa", 128, "float32"), ("dif", 128, "bfloat16"), ("sB", 128, "float32"),
-        ("B0", 128, "float32"), ("B1", 128, "float32"), ("y0", 128, "float32"), ("y1", 128, "float32"), ("y2", 128, "float32"),
-        ("on", 128, "bfloat16"), ("BD", 128, "bfloat16"), ("Ib", 128, "bfloat16"), ("If", 128, "float32"), ("onf", 128, "float32"),
-        ("HI", 128, "bfloat16"), ("NH", 128, "bfloat16"), ("CU", 256, "bfloat16"), ("BDE", 128, "bfloat16"), ("IV", 8, "bfloat16"),
-        ("IM", 8, "bfloat16"), ("I1", 8, "bfloat16"), ("Ih", 8, "float16"), ("I16", 8, "float32"), ("thx", 32, "float32"),
-        ("TH", 32, "float32"), ("W1", 512, "bfloat16"), ("W2", 512, "bfloat16"), ("KC", 256, "bfloat16"), ("d0h", 2048, "bfloat16"),
-        ("d0l", 2048, "bfloat16"), ("d0k", 128, "float32"), ("s1b", 128, "bfloat16"), ("s1f", 128, "float32"), ("CT1", 8, "float32"),
-        ("CT2", 8, "bfloat16"), ("CC", 384, "bfloat16"), ("Wt", 48, "bfloat16"), ("MB", 512, "bfloat16"), ("GO", 1024, "float16"),
-        ("Sx", 768, "float16"), ("zb", 768, "bfloat16"), ("N4", 128, "bfloat16"), ("C32", 128, "bfloat16"), ("CSX", 256, "bfloat16"),
-        ("IP", 128, "bfloat16"), ("IN", 128, "bfloat16"), ("CAB", 256, "bfloat16"), ("cA", 128, "bfloat16"), ("cB", 128, "bfloat16"),
-        ("Uf", 128, "float32"), ("jc", 1, "float32"), ("bc", 1, "float32"), ("rx", 8, "float32"), ("cx", 8, "float32"),
-        ("ji", 128, "int32"), ("jj", 128, "int32"), ("jk", 128, "int32"), ("mf", 128, "float32"), ("t8", 8, "float32")):
+        ("tab", W + 16, "bfloat16"), ("offs", 64, "uint16"), ("Gv", 1024, "bfloat16"), ("Ga", 1024, "bfloat16"), ("Hi", 1024, "bfloat16"),
+        ("Lo", 1024, "bfloat16"), ("HL", 384, "bfloat16"), ("E2", 64, "float16"), ("ET", 128, "bfloat16"), ("Epl", 64, "float32"),
+        ("iw", 448, "int32"), ("hn", 192, "int32"), ("hl", 64, "uint16"), ("V", 1024, "bfloat16"), ("A", 1024, "bfloat16"),
+        ("km", 72, "float32"), ("ki", 16, "int32"), ("lz", 24, "uint16"), ("cs", 64, "float32"), ("C2", 64, "float16"),
+        ("hs", 64, "float16"), ("pd", 64, "float16"), ("BP", 128, "float32"), ("Pm", 64, "float16"), ("P", 64, "float16"),
+        ("Sd", 64, "float32"), ("X", 512, "bfloat16"), ("M", 512, "bfloat16"), ("fw", 384, "float32"), ("gg", 128, "bfloat16"),
+        ("Wn", 272, "float32"), ("WW", 384, "float16"), ("KT", 4, "float32"), ("hwf", 8, "float32"), ("yo", 64, "float32")):
+    for _s in range(2):
+        SCRATCH[_n + str(_s)] = ("sbuf", [128, _c], _d)
+for _n, _c, _d in (
+        ("zs", 6 * 512, "bfloat16"), ("zl", 8 * 512, "bfloat16"), ("tpi", 260, "int32"), ("nat", N * NAT, "float16"), ("yl", 512, "float32"),
+        ("t1", 256, "float32"), ("t2", 256, "float32"), ("ji", 128, "int32"), ("jf", 128, "float32"), ("j16", 128, "float32"),
+        ("i2", 128, "float32"), ("pi", 64, "int32"), ("pf", 64, "float32"), ("IW", 128, "bfloat16"), ("w2", 2, "bfloat16"),
+        ("I2", 256, "bfloat16"), ("Ih", 128, "float16"), ("If", 128, "float32"), ("HI", 128, "float16"), ("BD", 128, "bfloat16"),
+        ("BDf", 128, "float32"), ("ZV", 144, "bfloat16"), ("ZA", 144, "bfloat16"), ("ZE", 144, "float16"), ("EXP", 1024, "bfloat16"),
+        ("d0h", 1024, "bfloat16"), ("d0l", 1024, "bfloat16"), ("d0k", 64, "float32"), ("NH", 64, "bfloat16"), ("KC", 128, "float16"),
+        ("OHW", 16, "bfloat16"), ("Sx", 768, "float16"), ("nS", 48, "float16"), ("GO", 1024, "float16"), ("MB", 512, "bfloat16"),
+        ("F1", 272, "float32"), ("F2", 272, "float32"), ("PERM", 128, "float16"), ("OUTP", 128, "float16"), ("SH", 256, "float16"),
+        ("cAB", 512, "bfloat16"), ("CC", 128, "bfloat16"), ("m384", 64, "float16"), ("cx", 8, "float32"), ("Sin", 160, "float16"),
+        ("zb", 8, "bfloat16"), ("di", 128, "int32"), ("df", 128, "float32")):
     SCRATCH[_n] = ("sbuf", [128, _c], _d)
-BANKS = ("bV", "bA", "bB", "bE", "bK0", "bK1", "bR0", "bR1")
+BANKS = tuple(n + s for s in "01" for n in ("bE", "bF", "bK", "bM"))
 for _n in BANKS:
     SCRATCH[_n] = ("psum", [128, 512], "float32")
-SEMAPHORES = (["cV", "cS", "cT", "cG", "ldp", "ldh", "st", "lsem"] + ["ld%d" % i for i in range(4)] + ["tz%d" % i for i in range(N)]
-              + ["hw%d" % i for i in range(N)] + ["hx%d" % i for i in range(len(HELP))])
+SEMAPHORES = (["cV", "cS", "cT", "cG", "ldn", "tb0", "tb1", "st", "lsem"] + ["ld%d" % i for i in range(6)]
+              + ["%s%d" % (n, i) for n in ("z", "y") for i in range(2 * N)] + ["n%d" % i for i in range(N)])
+WIDE = {"float32": 4, "int32": 4, "float16": 2, "bfloat16": 2, "uint16": 2}
+LEAD = 6000.0
+WAKE, NEAR = 100.0, 60.0
 
 
-def Tracker(g, T):
+def b(n, lo=0, hi=128, st=1, p=(0, 128)):
+    return (n, lo, hi, st, p)
+
+
+def over(a, c):
+    return a[1] < c[2] and c[1] < a[2] and not (a[3] == c[3] > 1 and (a[1] - c[1]) % a[3])
+
+
+def order(ops):
+    acc = {}
+    for i, o in enumerate(ops):
+        dep = {}
+        for refs, w in ((o["ins"], False), (o["outs"], True)):
+            for r in refs:
+                bank = r[0] in BANKS
+                for j, w2, r2 in acc.get(r[0], ()):
+                    same = ops[j]["e"] == o["e"]
+                    if (bank and (not same or o["e"] == "T")) or ((w or w2) and over(r, r2)):
+                        wait = not (same and o["e"] == "T")
+                        dep[j] = dep.get(j, False) or wait
+        dep.pop(i, None)
+        o["dep"] = dep
+        for refs, w in ((o["ins"], False), (o["outs"], True)):
+            for r in refs:
+                old = acc.get(r[0], [])
+                if w and r[3] == 1 and r[4] == (0, 128) and r[0] not in BANKS:
+                    old = [a for a in old if not (r[1] <= a[2][1] and a[2][2] <= r[2])]
+                acc[r[0]] = old[-40:] + [(i, w, r)] if r[0] in BANKS else old + [(i, w, r)]
+    left = [o["ns"] + o["urge"] for o in ops]
+    users = [[] for _ in ops]
+    for i in range(len(ops) - 1, -1, -1):
+        for j, wait in ops[i]["dep"].items():
+            left[j] = max(left[j], left[i] + ((ops[j]["ns"] + WAKE) if wait else 0.0))
+            users[j].append(i)
+    left = [v + o["lead"] for v, o in zip(left, ops)]
+    miss = [len(o["dep"]) for o in ops]
+    ready = {i: 0.0 for i in range(len(ops)) if not miss[i]}
+    free, out, start = {}, [], {}
+    while ready:
+        est = {i: max(t, free.get(ops[i]["e"], 0.0)) for i, t in ready.items()}
+        first = min(est, key=lambda i: (est[i], -left[i]))
+        i = max((j for j in est if ops[j]["e"] == ops[first]["e"] and est[j] <= est[first] + NEAR), key=lambda j: (left[j], -j))
+        start[i] = est[i]
+        if ops[i]["e"] != "D":
+            free[ops[i]["e"]] = est[i] + ops[i]["ns"]
+        del ready[i]
+        out.append(i)
+        for u in users[i]:
+            miss[u] -= 1
+            if not miss[u]:
+                ready[u] = max(start[j] + ((ops[j]["ns"] + WAKE) if wait else 0.0) for j, wait in ops[u]["dep"].items())
+    for i in out:
+        ops[i]["at"] = start[i]
+    return [ops[i] for i in out]
+
+
+def issue(g, T, ops):
     eng = {"V": g.vector, "S": g.scalar, "T": g.tensor, "G": g, "Y": g.sync}
-    cnt = {e: 0 for e in eng}; know = {e: {} for e in eng}; snap = {}; acc = {}
+    cnt = {e: 0 for e in eng}; know = {e: {} for e in eng}; snap = {}
 
     def need(e, needs):
         while True:
@@ -57,396 +112,410 @@ def Tracker(g, T):
             for k, v in snap.get((s, n), {}).items():
                 know[e][k] = max(know[e].get(k, 0), v)
             know[e][s] = max(know[e].get(s, 0), n)
+    for o in ops:
+        e = o["e"]
+        if e == "D":
+            continue
+        needs = {}
+        for j, wait in o["dep"].items():
+            if wait:
+                s, n = o["all"][j]["done"]
+                needs[s] = max(needs.get(s, 0), n)
+        need(e, needs)
+        if o["raw"]:
+            o["call"]()
+        else:
+            cnt[e] += 1
+            o["done"] = ("c" + e, cnt[e])
+            snap[o["done"]] = dict(know[e])
+            o["call"]().then_inc(T.sem["c" + e], 1)
+    need("Y", {"c" + e: cnt[e] for e in "VSTG"})
 
-    def conflicts(e, refs, write, needs):
-        for nm, lo, hi, st in refs:
-            bank = nm in BANKS
-            for w, ee, s, n, l2, h2, st2 in acc.get(nm, ()):
-                over = lo < h2 and l2 < hi and not (st == st2 > 1 and (lo - l2) % st)
-                if ee == e:
-                    hit = over and w and not (e == "T" and bank)
-                else:
-                    hit = bank or (over and (w or write))
-                if hit:
-                    needs[s] = max(needs.get(s, 0), n)
 
-    def note(e, s, n, refs, write):
-        for nm, lo, hi, st in refs:
-            keep = []
-            for a in acc.get(nm, ()):
-                cover = lo <= a[4] and a[5] <= hi and (st == 1 or (st == a[6] and (lo - a[4]) % st == 0))
-                if not (cover and (write or (not a[0] and a[1] == e))):
-                    keep.append(a)
-            acc[nm] = keep + [(write, e, s, n, lo, hi, st)]
-
-    def ref(r):
-        return (r[0], r[1], r[2], r[3] if len(r) > 3 else 1)
+def rank_program(g, core, T, topo, report=None):
+    rank = T.rank_of(core)
+    if rank is None:
+        return
+    ops = []
 
     def ap(r):
-        return T[r[0]][:, r[1]:r[2]:r[3]] if len(r) > 3 else T[r[0]][:, r[1]:r[2]]
+        return T[r[0]][r[4][0]:r[4][1], r[1]:r[2]:r[3]] if r[3] > 1 else T[r[0]][r[4][0]:r[4][1], r[1]:r[2]]
 
-    def op(e, outs, ins, call):
-        needs = {}
-        ro, ri = [ref(r) for r in outs], [ref(r) for r in ins]
-        conflicts(e, ri, False, needs)
-        conflicts(e, ro, True, needs)
-        need(e, needs)
-        cnt[e] += 1
-        s = "c" + e
-        snap[(s, cnt[e])] = dict(know[e])
-        call().then_inc(T.sem[s], 1)
-        note(e, s, cnt[e], ri, False)
-        note(e, s, cnt[e], ro, True)
+    def size(r):
+        return len(range(r[1], r[2], r[3]))
 
-    def landed(sem, n, refs):
-        note("dma", sem, n, [ref(r) for r in refs], True)
+    def narrow(*rs):
+        return all(WIDE[SCRATCH[r[0]][2]] == 2 for r in rs)
 
-    def before(e, ins):
-        needs = {}
-        conflicts(e, [ref(r) for r in ins], False, needs)
-        need(e, needs)
-    return {"op": op, "ap": ap, "landed": landed, "before": before, "cnt": cnt, "need": need}
+    def op(e, outs, ins, call, ns, raw=False, urge=0.0, done=None):
+        ops.append({"e": e, "outs": outs, "ins": ins, "call": call, "ns": ns, "raw": raw, "urge": urge, "done": done, "all": ops, "lead": 0.0})
 
+    def landed(sem, n, refs, at):
+        op("D", refs, [], None, at, done=(sem, n))
 
-def rank_program(g, core, T, topo):
-    rank = T.rank_of(core)
-    helpers = []
-    for c in T.cores:
-        helpers.append([k for k in topo.cores_of(c) if topo.die(k) != topo.die(c) and k not in T.cores
-                        and all(topo.may_write(k, d) for d in T.cores if d != c)][0])
-    if rank is None:
-        if core in helpers:
-            helper_program(g, core, T, topo, helpers.index(core))
-        return
-    others = [c for c in T.cores if c != core]
-    K = Tracker(g, T)
-    op, ap = K["op"], K["ap"]
+    def src(a, win):
+        return ap(win).indirect(ap(a)) if win else ap(a)
 
-    def ind(win, off):
-        return ap(win).indirect(ap(off))
+    def vns(out, a, win, k):
+        return 50.0 + 1.56 * size(out) if win else max(64.0, k * size(out))
 
-    def tt(out, a, b, o, win=None):
-        op("V", [out], [a, b] + ([win] if win else []), lambda: g.vector.tensor_tensor(ap(out), ind(win, a) if win else ap(a), ap(b), o))
+    def tt(out, a, c, o, win=None):
+        k = 1.0 if a[0] in BANKS or c[0] in BANKS else 2.0
+        op("V", [out], [a, c] + ([win] if win else []), lambda: g.vector.tensor_tensor(ap(out), src(a, win), ap(c), o), vns(out, a, win, k))
 
-    def ts(out, a, s1, o1, s2=None, o2=None):
-        ins = [a] + [s for s in (s1, s2) if isinstance(s, tuple)]
+    def ts(out, a, s1, o1, s2=None, o2=None, win=None):
+        ins = [a] + [s for s in (s1, s2, win) if isinstance(s, tuple)]
         f = lambda s: ap(s) if isinstance(s, tuple) else s
-        if o2 is None:
-            op("V", [out], ins, lambda: g.vector.tensor_scalar(ap(out), ap(a), f(s1), None, o1))
+        rest = (o1,) if o2 is None else (o1, o2)
+        op("V", [out], ins, lambda: g.vector.tensor_scalar(ap(out), src(a, win), f(s1), f(s2), *rest), vns(out, a, win, 0.5 if narrow(out, a) else 1.0))
+
+    def cp(out, a, win=None):
+        op("V", [out], [a] + ([win] if win else []), lambda: g.vector.tensor_copy(ap(out), src(a, win)), vns(out, a, win, 0.5 if narrow(out, a) else 1.0))
+
+    def act(out, a, f, win=None, **k):
+        op("S", [out], [a] + ([win] if win else []), lambda: g.scalar.activation(ap(out), src(a, win), f, **k),
+           65.0 + 1.56 * size(out) if win else max(64.0, size(out)))
+
+    def gather(e, out, win, off):
+        if e == "S":
+            act(out, off, F.Copy, win=win)
         else:
-            op("V", [out], ins, lambda: g.vector.tensor_scalar(ap(out), ap(a), f(s1), f(s2), o1, o2))
-
-    def cp(out, a):
-        op("V", [out], [a], lambda: g.vector.tensor_copy(ap(out), ap(a)))
-
-    def gat(out, win, off):
-        op("V", [out], [win, off], lambda: g.vector.tensor_copy(ap(out), ind(win, off)))
-
-    def sgat(out, win, off):
-        op("S", [out], [win, off], lambda: g.scalar.activation(ap(out), ind(win, off), F.Copy))
-
-    def scat(win, off, a):
-        op("V", [win], [off, a], lambda: g.vector.tensor_copy(ind(win, off), ap(a)))
+            cp(out, off, win=win)
 
     def scan(out, d0, d1, o0, o1):
-        op("V", [out], [d0, d1], lambda: g.vector.tensor_tensor_scan(ap(out), ap(d0), ap(d1), 0.0, o0, o1))
+        op("V", [out], [d0, d1], lambda: g.vector.tensor_tensor_scan(ap(out), ap(d0), ap(d1), 0.0, o0, o1),
+           vns(out, d0, None, 0.5 if narrow(out, d0, d1) else 1.0))
 
-    def fill(out, c, p0=0, p1=128):
-        op("V", [out], [], lambda: g.vector.memset(T[out[0]][p0:p1, out[1]:out[2]] if len(out) < 4 else ap(out), c))
+    def fill(out, c):
+        op("V", [out], [], lambda: g.vector.memset(ap(out), c), vns(out, out, None, 0.5 if narrow(out) else 1.0))
 
-    def mm(out, l, r, start, stop):
-        op("T", [out], [l, r], lambda: g.tensor.matmul(ap(out), ap(l), ap(r), start, stop))
+    def mm(out, l, r, start=True, stop=True):
+        op("T", [out], [l, r], lambda: g.tensor.matmul(ap(out), ap(l), ap(r), start, stop),
+           0.5 * max(min(64, size(l)), size(r)) * (1 if narrow(l) else 4) + 10.0)
 
-    def act(out, a, f, **k):
-        op("S", [out], [a], lambda: g.scalar.activation(ap(out), ap(a), f, **k))
+    def iota(out, pattern, base, cm):
+        k = {} if SCRATCH[out[0]][2] == "int32" else {"allow_small_or_imprecise_dtypes": True}
+        op("G", [out], [], lambda: g.iota(ap(out), pattern, base, cm, **k), 130.0 + 2 * size(out))
 
-    def sel(out, a, pattern, o, base, cm):
-        op("G", [out], [a], lambda: g.affine_select(ap(out), ap(a), pattern, o, 0.0, base, cm))
+    local = [0]
 
-    def iota(out, pattern, base, cm, **k):
-        op("G", [out], [], lambda: g.iota(ap(out), pattern, base, cm, **k))
+    def send(ranks, a, dst, sem, urge):
+        cs = [T.cores[r] for r in ranks]
+        t = RemoteDMATransfer(dst_ids=[DstId(rid=topo.addr(c)[0], pnc=topo.addr(c)[1]) for c in cs], dma_engine_mask=topo.mask(core, cs[0]),
+                              remote_sem=T.sem[sem], srcs=[ap(a)], dsts=[ap(dst) for _ in cs])
+        op("G", [], [a], lambda: g.remote_dma_fused([t], local_sem=T.sem.lsem), 500.0, raw=True, urge=urge)
+        local[0] += len(topo.engines(core, cs[0]))
 
-    def b(n, lo=0, hi=128, *st):
-        return (n, lo, hi) + st
-    BM, PS, X1, X2 = [("bV", 128 * i, 128 * i + 128) for i in range(4)]
-    fl = {"allow_small_or_imprecise_dtypes": True}
+    others = [(rank + i) % N for i in range(1, N)]
+    eo = len(topo.engines(T.cores[others[0]], core))
 
-    base = rank * BLK
-    chunks = [HELP[0], OWN[0], HELP[1], OWN[1]]
-    for i, (c0, c1) in enumerate(chunks):
-        q = g.sync if i % 2 == 0 else g.scalar
-        q.dma_start(T.zall[:, base + c0:base + c1], T.tz[:, c0:c1]).then_inc(T.sem["ld%d" % i], 16)
-        K["landed"]("ld%d" % i, 16, [("zall", base + c0, base + c1)])
-    g.scalar.dma_start(T.hwi[:, 4 * rank:4 * rank + 3], T.hw[:, :]).then_inc(T.sem.ldh, 16)
-    g.scalar.dma_start(T.hwi[:, 4 * rank + 3:4 * rank + 4], T.th[:, :]).then_inc(T.sem.ldh, 16)
-    g.sync.dma_start(T.tpi[:, 0:128], T.tp[:, :]).then_inc(T.sem.ldp, 16)
-    g.sync.dma_start(T.tpi[:, 128:256], T.sd[:, :]).then_inc(T.sem.ldp, 16)
-    K["landed"]("ldh", 32, [("hwi", 4 * rank, 4 * rank + 4)])
-    K["landed"]("ldp", 32, [("tpi", 0, 256)])
+    def rows(t, grp):
+        return T[t][16 * grp:16 * grp + 16, :]
 
-    fill(b("on"), 1.0)
-    fill(b("onf"), 1.0)
-    sel(b("OH"), b("on"), [[-16, 8], [0, 16]], O.is_ge, 0, 1)
-    sel(b("BD"), b("OH"), [[16, 8], [0, 16]], O.is_ge, 15, -1)
-    sel(b("If"), b("onf"), [[-1, 128]], O.is_equal, 0, 1)
+    def tab(s, q, h):
+        return T["tab%d" % s][32 * q + 16 * h:32 * q + 16 * h + 16, 0:W]
+    for s in range(2):
+        for i, d in enumerate(others):
+            j = 3 * s + i
+            (g.scalar if i == 1 else g.sync).dma_start(T.zs[:, 512 * j:512 * j + 512], rows("tz", 2 * d + s)).then_inc(T.sem["ld%d" % j], 16)
+            landed("ld%d" % j, 16, [b("zs", 512 * j, 512 * j + 512)], 2200.0 + 200 * j)
+        if s == 0:
+            g.scalar.dma_start(T.tpi[:, 0:128], T.tp[:, :]).then_inc(T.sem.ldn, 16)
+            g.sync.dma_start(T.tpi[:, 128:256], T.sd[:, :]).then_inc(T.sem.ldn, 16)
+            g.scalar.dma_start(T.tpi[:, 256:259], T.hw[:, :]).then_inc(T.sem.ldn, 16)
+            g.scalar.dma_start(T.tpi[:, 259:260], T.th[:, :]).then_inc(T.sem.ldn, 16)
+            landed("ldn", 64, [b("tpi", 0, 260)], 2800.0)
+    for s in range(2):
+        for h in range(2):
+            (g.scalar if h else g.sync).dma_start(tab(s, rank, h), rows("tz", 2 * rank + s)).then_inc(T.sem["tb%d" % s], 16)
+    for s in range(2):
+        for q in others[::-1]:
+            j = 2 * q + s
+            for h in range(2):
+                e = g.scalar if (s == 0 and h) else g.sync
+                if s == 0 or h == 0:
+                    e.wait_ge(T.sem["z%d" % j], eo)
+                e.dma_start(tab(s, q, h), T.zl[:, 512 * j:512 * j + 512]).then_inc(T.sem["tb%d" % s], 16)
+        landed("tb%d" % s, 128, [b("tab%d" % s, 0, W)], 13000.0 + 6000 * s)
+    n0 = rank * NAT
+    ts(b("t1", 0, 256), b("tpi", 0, 256), 0, O.is_lt, EMPTY + 2049.0, O.mult)
+    ts(b("t2", 0, 256), b("tpi", 0, 256), -2048, O.add)
+    tt(b("nat", n0, n0 + 256), b("t1", 0, 256), b("t2", 0, 256), O.add)
+    cp(b("nat", n0 + 256, n0 + 259), b("tpi", 256, 259))
+    ts(b("nat", n0 + 259, n0 + 260), b("tpi", 259, 260), -2048, O.add)
+    for s in range(2):
+        for i, d in enumerate(others):
+            j = 2 * rank + s
+            send([d], b("zs", 512 * (3 * s + i), 512 * (3 * s + i + 1)), b("zl", 512 * j, 512 * j + 512), "z%d" % j, 1e6 - 1e3 * (4 * s + i))
+        if s == 0:
+            send(others, b("nat", n0, n0 + 260), b("nat", n0, n0 + 260), "n%d" % rank, 1e6 - 3e3)
+    for q in others:
+        landed("n%d" % q, eo, [b("nat", q * NAT, q * NAT + 260)], 9000.0)
 
-    h = helpers[rank]
-    spare = [e for e in topo.engines(core, h) if e not in topo.engines(core, others[0])]
-    eo = len(topo.engines(core, others[0]))
-    local = 0
-    to = [DstId(rid=topo.addr(c)[0], pnc=topo.addr(c)[1]) for c in others]
-
-    def to_others(buf, lo, hi, sem):
-        t = RemoteDMATransfer(dst_ids=to, dma_engine_mask=topo.mask(core, others[0]), remote_sem=T.sem[sem],
-                              srcs=[T[buf][:, lo:hi]], dsts=[T[buf][:, lo:hi] for _ in others])
-        g.remote_dma_fused([t], local_sem=T.sem.lsem)
-        return eo
-    for i, (c0, c1) in enumerate(chunks):
-        K["before"]("G", [("zall", base + c0, base + c1)])
-        if i % 2 == 0:
-            t = RemoteDMATransfer(dst_ids=[DstId(rid=topo.addr(h)[0], pnc=topo.addr(h)[1])], dma_engine_mask=sum(1 << e for e in spare),
-                                  remote_sem=T.sem["hx%d" % (i // 2)], srcs=[T.zall[:, base + c0:base + c1]],
-                                  dsts=[T.zh[:, c0 - HELP[0][0]:c1 - HELP[0][0]]])
-            g.remote_dma_fused([t], local_sem=T.sem.lsem)
-            local += len(spare)
-        else:
-            local += to_others("zall", base + c0, base + c1, "tz%d" % rank)
-        if i == 1:
-            K["before"]("G", [("hwi", 4 * rank, 4 * rank + 4)])
-            local += to_others("hwi", 4 * rank, 4 * rank + 4, "hw%d" % rank)
-    for q in range(N):
-        if q != rank:
-            K["landed"]("tz%d" % q, eo * (len(OWN) + len(HELP)), [("zall", q * BLK, q * BLK + W)])
-            K["landed"]("hw%d" % q, eo, [("hwi", 4 * q, 4 * q + 4)])
-
-    iota(b("ji"), [[0, 8], [-1, 16]], 128, 1)
-    iota(b("KC"), [[0, 8], [1, 16]], 0, 0, **fl)
-    iota(b("CT1", 0, 8), [[16, 8]], 0, 1, **fl)
-    iota(b("Uf"), [[16, 128]], 2050, 0, **fl)
-    iota(b("y0"), [[0, 128]], 0, 1, **fl)
-    fill(b("y1"), 8192.0)
-    sel(b("y2"), b("y1"), [[-1, 128]], O.is_ge, 0, 1)
-    for q in range(N):
-        fill(b("zall", q * BLK + W, (q + 1) * BLK), -256.0)
-    for nm, w, lo, hi in (("d0h", 2048, 255.0, 0.0), ("d0l", 2048, 0.0, 255.0), ("d0k", 128, -1.0e9, 1.0e9), ("s1b", 128, 1.0, 0.0), ("s1f", 128, 1.0, 0.0)):
+    iota(b("pi", 0, 8), [[0, 8]], 0, 1)
+    iota(b("ji"), [[1, 128]], 0, 0)
+    iota(b("j16"), [[1, 8], [0, 16]], 0, 0)
+    iota(b("i2"), [[32, 4], [0, 2], [1, 16]], 0, 0)
+    for h in range(2):
+        iota(b("IW", 64 * h, 64 * h + 64), [[4, 4], [1, 4], [16, 4]], 128 + 64 * h, 0)
+    iota(b("KC"), [[1024, 2], [1, 64]], 0, 0)
+    iota(b("pi", 16, 24), [[1, 8]], 0, 0)
+    cp(b("jf"), b("ji"))
+    c1 = lambda n, i: b(n, i, i + 1)
+    for i, (sh, mask) in enumerate(((0, 127), (4, 7), (0, 15), (5, 3), (4, 1), (2, 3), (0, 3))):
+        ts(c1("pi", 8 + i), c1("pi", 0), sh, O.arith_shift_right, mask, O.bitwise_and)
+    cp(b("pf", 0, 7), b("pi", 8, 15))
+    pp, pu, pl, pq, ph, pj, pr = [c1("pf", i) for i in range(7)]
+    for i in range(2):
+        ts(b("I2", 128 * i, 128 * i + 128), b("jf"), pp, O.is_equal)
+    Ib = b("I2")
+    cp(b("Ih"), Ib); cp(b("If"), Ib)
+    ts(b("HI"), Ib, 0.5, O.mult)
+    ts(b("BD"), b("j16"), pu, O.is_equal)
+    cp(b("BDf"), b("BD"))
+    for nm, c in (("ZV", 4096.0), ("ZA", -8192.0)):
+        fill(b(nm, 0, 144), 0.0)
+        ts(b(nm, 16, 144, 16), b("BD", 0, 128, 16), c, O.mult)
+    ts(b("ZE", 0, 144), b("ZV", 0, 144), -0.5, O.mult)
+    for m in range(16):
+        cp(b("EXP", m, 1024, 16), b("I2", 0, 64))
+    for nm, w, st, lo, hi in (("d0h", 1024, 4, 255.0, 0.0), ("d0l", 1024, 4, 0.0, 255.0), ("d0k", 64, 16, -1.0e9, 1.0e9)):
         fill(b(nm, 0, w), lo)
-        fill(b(nm, 0, w, 16), hi)
-    for nm, w in (("Zb", 128), ("Zf", 128), ("SU", 128), ("Q", 256), ("zb", 768)):
-        fill(b(nm, 0, w), 0.0)
-    fill(b("NH"), -0.5)
-    fill(b("CU", 0, 256), -16.0)
-    fill(b("CU", 0, 256), -15.5, 0, 1)
-    fill(b("C32"), 32.0)
-    fill(b("CSX"), -16384.0); fill(b("CSX", 128, 256), 16384.0)
-    fill(b("CAB"), 8192.0); fill(b("CAB", 128, 256), -8192.0)
-    cp(b("Ib"), b("If"))
-    for nm, c in (("HI", 0.5), ("IP", 32768.0), ("IN", -32768.0), ("N4", -4096.0)):
-        ts(b(nm), b("Ib"), c, O.mult)
-    bd16 = b("BD", 0, 128, 16)
-    ts(b("BDE"), b("BD"), -16.0, O.mult)
-    ts(b("cB"), b("BD"), 16384.0, O.mult)
-    for nm, c in (("IV", -32.0), ("IM", 64.0), ("I1", 1.0), ("Ih", 1.0), ("I16", 0.0625)):
-        ts(b(nm, 0, 8), bd16, c, O.mult)
-    ts(b("mn"), b("If"), 262144.0, O.mult)
-    ts(b("mf"), b("BD"), -16384.0, O.mult)
-    tt(b("cA"), b("mn"), b("mf"), O.add)
-    for i in range(8):
-        ts(b("GO", 128 * i, 128 * i + 128), b("on"), b("BD", 16 * i, 16 * i + 1), O.mult)
-    for i in range(4):
-        cp(b("MB", 128 * i, 128 * i + 128), b("y2"))
-    ts(b("jj"), b("ji"), 15, O.bitwise_and)
-    ts(BM, b("jj"), 0, O.is_equal)
-    ts(b("mf"), b("jj"), 0, O.is_equal)
-    cp(b("jc", 0, 1), b("jj", 0, 1))
-    ts(b("jk", 0, 1), b("jj", 0, 1), 2, O.arith_shift_right)
-    ts(b("bc", 0, 1), b("jk", 0, 1), float(BLK), O.mult, 2048.0, O.add)
-    xs = [S * ((rank + 1 + t) % N) + t // N for t in range(RO)]
-    cp(b("Sx", 0, 768), b("zb", 0, 768))
-    for t, x in enumerate(xs):
-        ts(b("rx", t, t + 1), b("jc", 0, 1), float(x), O.is_equal)
-        ts(b("cx", t, t + 1), b("rx", t, t + 1), 8192.0, O.mult, -4096.0, O.add)
-        cp(b("Sx", 128 * t + x, 128 * t + 128, 16), b("BD", x, 128, 16))
-    ts(b("KC", 128, 256), b("KC"), 8.5, O.add)
-    ts(b("KC"), b("KC"), -7.5, O.add)
-    tt(b("t8", 0, 1), b("y0", 0, 1), b("jc", 0, 1), O.subtract)
-    ts(b("q8", 0, 8), b("CT1", 0, 8), b("t8", 0, 1), O.subtract)
-    ts(b("CT2", 0, 8), b("q8", 0, 8), 128.0, O.add)
-    ts(b("CT1", 0, 8), b("q8", 0, 8), 16.0, O.mult, 7.5, O.add)
-    ts(b("CC", 0, 384, 3), b("mf"), -4.0, O.mult, 4.0, O.add)
-    ts(b("CC", 1, 384, 3), b("y0"), -1.0, O.mult)
-    ts(b("CC", 2, 384, 3), b("y0"), 0.0, O.mult)
-    fill(b("Wt", 0, 48), 1.0)
-    ts(b("Wt", 1, 48, 3), b("y0", 0, 16), -128.0, O.add)
-    ts(b("tpf", 0, 256), b("tpi", 0, 256), 0, O.is_lt, 8192.0, O.mult)
-    ts(b("Pw", 0, 256), b("tpi", 0, 256), -2048, O.add)
-    tt(b("P", 0, 256), b("Pw", 0, 256), b("tpf", 0, 256), O.add)
-    SD = b("P", 128, 256)
-    for q in [rank] + [(rank + i) % N for i in range(1, N)]:
-        cp(b("hwf", 4 * q, 4 * q + 4), b("hwi", 4 * q, 4 * q + 4))
-        ts(b("W1", 128 * q, 128 * q + 128), b("BD"), b("hwf", 4 * q, 4 * q + 1), O.mult, 0.5, O.mult)
-        ts(b("W2", 128 * q, 128 * q + 128), b("BD"), b("hwf", 4 * q + 1, 4 * q + 2), O.mult, 0.5, O.mult)
-        ts(b("thx", 8 * q, 8 * q + 8), b("I16", 0, 8), b("hwf", 4 * q + 3, 4 * q + 4), O.mult)
-    mm(b("bA", 0, 32), b("onf"), b("thx", 0, 32), True, True)
-    ts(b("TH", 0, 32), b("bA", 0, 32), 32.0, O.mult, -7.75, O.add)
-
-    def hash_mm(C, q):
-        mm(b("bA", 0, 256), b("on"), b("CU", 0, 256), True, False)
-        w1, w2 = b("W1", 128 * q, 128 * q + 128), b("W2", 128 * q, 128 * q + 128)
-        mm(b("bA", 0, 128), w1, b(C), False, False)
-        mm(b("bA", 128, 256), w2, b(C), False, True)
-        mm(b("bB", 0, 128), w1, b(C), True, True)
-        mm(b("bB", 128, 256), w2, b(C), True, True)
-
-    def hash_v(q):
-        ts(b("uq", 0, 256), b("bA", 0, 256), M12, O.add, -M12, O.add)
-        tt(b("u1"), b("bB", 0, 128), b("uq", 0, 128), O.subtract)
-        tt(X1, b("bB", 128, 256), b("uq", 128, 256), O.subtract)
-        tt(b("pr"), b("u1"), X1, O.mult)
-        ts(X2, X1, b("hwf", 4 * q + 2, 4 * q + 3), O.mult)
-        ts(b("sh"), b("pr"), 5, O.arith_shift_right)
-        tt(b("sm"), b("sh"), X2, O.add)
-        ts(b("hn"), b("sm"), 4095, O.bitwise_and)
-        cp(b("hl"), b("hn"))
-
-    def search(q, p):
-        win = b("zall", q * BLK, q * BLK + W)
-        c = 16 * SPLIT_V
-        sgat(b("V", c, 2048), win, b("hl", SPLIT_V, 128))
-        gat(b("V", 0, c), win, b("hl", 0, SPLIT_V))
-        ts(b("G", 128 * p, 128 * p + 128), b("hn"), -2048.0, O.add)
-        bk = "bK%d" % p
-
-        def vm(m):
-            mm(b(bk, m, 128, 16), b("V", m, 2048, 16), b("IV", 0, 8), False, False)
-        vm(0)
-        vm(1)
-        for m in range(16):
-            tt(b("Mx", m, 2048, 16), b("V", m, 2048, 16), b("bE"), O.max)
-            mm(b(bk, m, 128, 16), b("Mx", m, 2048, 16), b("IM", 0, 8), False, m == 15)
-            if m < 14:
-                vm(m + 2)
-
-    def key_mm(p):
-        mm(b("bK%d" % p), b("Ib"), b("KC", 128 * p, 128 * p + 128), True, False)
-        mm(b("bK%d" % p), b("E2"), b("BDE"), False, False)
-
+        fill(b(nm, 0, w, st), hi)
+    fill(b("NH", 0, 64), -0.5); fill(b("zb", 0, 8), 0.0)
+    ts(b("m384", 0, 64), b("NH", 0, 64), 768.0, O.mult)
+    fill(b("CC"), -2048.0); fill(b("CC", 64, 128), EMPTY)
+    fill(b("F1", 0, 272), EMPTY); fill(b("F1", 128, 256), -4096.0)
+    fill(b("F2", 0, 272), -4096.0); fill(b("F2", 128, 256), EMPTY)
+    ts(c1("pf", 8), pl, 64.0, O.mult)
+    ts(b("KC"), b("KC"), c1("pf", 8), O.add)
+    ts(b("OHW", 0, 16), b("jf", 0, 16), pl, O.is_equal)
+    for u in range(8):
+        ts(b("GO", 128 * u, 128 * u + 128), b("BD"), 0.0, O.mult, c1("BD", 16 * u), O.add)
+    tcol, rq, xr = b("pi", 16, 22), b("pi", 24, 30), b("pi", 32, 38)
+    ts(b("pi", 40, 46), tcol, -1.0, O.mult, pq, O.add)
+    ts(b("pi", 40, 46), b("pi", 40, 46), 7, O.add)
+    ts(rq, b("pi", 40, 46), 3, O.bitwise_and)
+    ts(b("pi", 48, 54), tcol, 1, O.add, pq, O.add)
+    ts(xr, b("pi", 48, 54), 3, O.bitwise_and)
+    ts(b("pi", 56, 62), tcol, 2, O.arith_shift_right)
+    ts(b("pf", 16, 22), xr, 4.0, O.mult)
+    tt(b("pf", 16, 22), b("pf", 16, 22), b("pi", 56, 62), O.add)
+    ts(b("pf", 16, 22), b("pf", 16, 22), pl, O.is_equal)
+    ts(b("cx", 0, 6), b("pf", 16, 22), EMPTY + 4096.0, O.mult, -4096.0, O.add)
+    ts(c1("pf", 9), ph, 4.0, O.mult, pq, O.add)
+    ts(b("pf", 24, 30), rq, 8.0, O.mult, c1("pf", 9), O.add)
+    ts(b("pf", 24, 30), b("pf", 24, 30), 4.0, O.mult)
+    tt(b("pf", 24, 30), b("pf", 24, 30), b("pi", 56, 62), O.add)
+    ts(c1("pf", 10), ph, 4.0, O.mult)
+    ts(b("pf", 32, 38), rq, c1("pf", 10), O.add)
     for t in range(RO):
-        q = (rank + 1 + t) % N
-        x = xs[t]
-        km8, th8, z16 = b("km", 15, 128, 16), b("TH", 8 * q, 8 * q + 8), b("Zf", 0, 128, 16)
-        ts(b("offs"), b("P"), 2048.0, O.min, b("bc", 0, 1), O.add)
-        c, h2 = 16 * SPLIT_E, 8 * SPLIT_E
-        sgat(b("Ve", c, 2048), b("zall", 0, N * BLK), b("offs", SPLIT_E, 128))
-        gat(b("Ve", 0, c), b("zall", 0, N * BLK), b("offs", 0, SPLIT_E))
-        mm(b("bE", 128, 256), b("Ib"), b("NH"), True, False)
-        pieces = [(c, 2048), (0, h2), (h2, c)]
-        for lo, hi in pieces:
-            act(b("Va", lo, hi), b("Ve", lo, hi), F.Abs)
-        for lo, hi in ((0, c), (c, 2048)):
-            scan(b("Hi", lo, hi), b("d0h", lo, hi), b("Ve", lo, hi), O.min, O.max)
-        for lo, hi in pieces:
-            scan(b("Lo", lo, hi), b("d0l", lo, hi), b("Va", lo, hi), O.max, O.min)
-        mm(b("bE", 128, 256), b("Ib"), b("Hi", 15, 2048, 16), False, False)
-        mm(b("bE", 128, 256), b("Ib"), b("Lo", 15, 2048, 16), False, True)
-        ts(b("E2"), b("bE", 128, 256), M1, O.add, -M1, O.add)
-        act(b("Epl"), b("E2"), F.Identity, scale=0.5, bias=-0.5)
-        hash_mm("E2", q)
-        mm(b("bE"), b("HI"), b("E2"), True, True)
-        key_mm(0)
-        ts(b("Pm"), b("P"), b("cx", t, t + 1), O.max)
-        hash_v(q)
-        search(q, 0)
-        scan(b("km"), b("d0k"), b("bK0"), O.max, O.min)
-        ts(b("q8", 0, 8), km8, M4, O.add, -M4, O.add)
-        tt(b("Zb", 0, 128, 16), km8, b("q8", 0, 8), O.subtract)
-        scan(b("Ze"), b("s1b"), b("Zb"), O.mult, O.add)
-        tt(b("Zm"), b("Ze"), BM, O.mult)
-        mm(b("bA", 256, 264), b("If"), b("CT1", 0, 8), True, False)
-        mm(b("bA", 256, 264), b("Zm"), b("I1", 0, 8), False, True)
-        key_mm(1)
-        mm(b("bR0", 0, 512), b("Ib"), b("MB", 0, 512), True, False)
-        mm(b("bR1", 0, 512), b("Ib"), b("MB", 0, 512), True, False)
-        tt(b("kf0", 0, 8), km8, th8, O.min)
-        cp(b("l0", 0, 8), b("bA", 256, 264))
-        tt(b("cs"), b("l0", 0, 8), b("Epl"), O.add, win=b("V", 0, 2048))
-        ts(b("C2"), b("cs"), M1, O.add, -M1, O.add)
-        hash_mm("C2", q)
-        fill(b("SU"), 0.0)
-        ts(b("Ux"), b("Uf"), b("rx", t, t + 1), O.mult)
-        hash_v(q)
-        search(q, 1)
-        scan(b("km"), b("d0k"), b("bK1"), O.max, O.min)
-        tt(z16, km8, b("kf0", 0, 8), O.min)
-        scan(b("kfr"), b("s1f"), b("Zf"), O.mult, O.add)
-        tt(b("OH"), b("kfr"), b("bK0"), O.is_equal)
-        tt(b("OH", 128, 256), b("kfr"), b("bK1"), O.is_equal)
-        tt(b("SU", x, 128, 16), z16, th8, O.is_lt)
-        mm(b("bA", 0, 128), b("OH"), b("Ib"), True, True)
-        mm(b("bE"), b("OH", 128, 256), b("Ib"), True, True)
-        tt(b("pd"), b("bA"), b("G"), O.mult)
-        tt(b("pd", 128, 256), b("bE"), b("G", 128, 256), O.mult)
-        sx = b("Sx", 128 * t, 128 * t + 128)
-        mm(b("bB"), b("on"), b("C32"), True, False)
-        mm(b("bB"), b("SU"), b("N4"), False, False)
-        mm(b("bB"), sx, b("pd"), False, False)
-        mm(b("bB"), sx, b("pd", 128, 256), False, True)
-        mm(b("bK0", 0, 384), b("Ib"), b("CC", 0, 384), True, False)
-        tt(b("rs"), b("bB"), b("Ux"), O.min)
-        mm(b("bA", 0, 8), b("rs"), b("Ih", 0, 8), True, True)
-        for i in range(8):
-            mm(b("bR%d" % (i // 4), 128 * (i % 4), 128 * (i % 4) + 128), b("GO", 128 * i, 128 * i + 128), b("rs"), False, i % 4 == 3)
-        tt(b("Pw"), b("Pm"), b("bB"), O.min)
-        tt(b("Pw", 128, 256), b("Pm"), b("bB"), O.min)
-        tt(PS, b("Pm"), b("bB"), O.min)
-        cp(b("nc", 0, 8), b("bA", 0, 8))
-        for i in range(8):
-            xg = b("X", 128 * i, 128 * i + 128)
-            ts(xg, b("bR%d" % (i // 4), 128 * (i % 4), 128 * (i % 4) + 128), b("nc", i, i + 1), O.is_equal)
-            mm(b("bK0", 48 * i, 48 * i + 48), xg, b("Wt", 0, 48), False, i == 7)
-        mm(b("bA", 256, 264), b("Ib"), b("CT2", 0, 8), True, False)
-        ts(b("iM"), b("bK0", 0, 384, 3), 1.0, O.is_equal)
-        tt(b("vl"), b("iM"), b("bK0", 1, 384, 3), O.mult)
-        mm(b("bA", 256, 264), b("vl"), b("I1", 0, 8), False, True)
-        ts(b("iU"), b("bK0", 2, 384, 3), 1.0, O.is_equal)
-        mm(b("bK1", 0, 256), b("Ib"), b("CSX", 0, 256), True, False)
-        mm(b("bK1", 0, 128), b("iU"), b("IP"), False, False)
-        mm(b("bK1", 128, 256), b("iU"), b("IN"), False, True)
-        mm(b("bB", 0, 256), b("Ib"), b("CAB", 0, 256), True, False)
-        cp(b("L", 0, 8), b("bA", 256, 264))
-        gat(b("Q"), b("Pw", 0, 256), b("L", 0, 8))
-        scat(b("Q", 0, 256), b("L", 0, 8), b("Pw"))
-        tt(b("sB"), SD, b("bK1", 128, 256), O.max)
-        tt(X1, b("Q"), PS, O.max)
-        tt(b("mn"), b("Q"), PS, O.min)
-        ts(X2, X1, 2048.0, O.is_lt)
-        tt(b("aa"), X1, b("mn"), O.subtract)
-        tt(b("dif"), b("aa"), X2, O.min)
-        mm(b("bB", 0, 128), b("cA"), b("dif"), False, False)
-        mm(b("bB", 128, 256), b("cB"), b("dif"), False, True)
-        tt(X1, b("mn"), b("bK1", 0, 128), O.max)
-        tt(b("B0"), b("sB"), X1, O.min)
-        tt(X2, b("Pw"), b("bB", 0, 128), O.max)
-        tt(b("B1"), b("B0"), b("bB", 128, 256), O.max)
-        tt(b("P"), b("B1"), X2, O.min)
-    ts(b("y0"), b("P"), 4096.0, O.min, 2049.0, O.add)
-    ts(b("y1"), b("P"), 2048.0, O.is_lt)
-    tt(b("y2"), b("y0"), b("y1"), O.mult)
-    ts(b("B0"), b("y2"), -1.0, O.add)
-    K["before"]("Y", [b("B0")])
-    g.sync.dma_start(T.yp[:, :], T.B0[:, :]).then_inc(T.sem.st, 16)
-    K["need"]("Y", {"c" + e: K["cnt"][e] for e in "VSTG"})
-    g.sync.wait_ge(T.sem.st, 16)
-    g.wait_ge(T.sem.lsem, local)
+        ts(b("Sx", 128 * t, 128 * t + 128), b("jf"), c1("pf", 24 + t), O.is_equal)
+        ts(b("nS", 8 * t, 8 * t + 8), b("jf", 0, 8), c1("pf", 32 + t), O.is_equal)
+    tt(c1("pi", 1), c1("pi", 11), c1("pi", 13), O.subtract)
+    ts(c1("pi", 2), c1("pi", 1), 3, O.bitwise_and)
+    ts(c1("pf", 11), c1("pi", 2), 4.0, O.mult, pr, O.add)
+    ts(c1("pf", 12), pj, 2.0, O.mult, ph, O.add)
+    ts(c1("pf", 12), c1("pf", 12), 16.0, O.mult, c1("pf", 11), O.add)
+    ts(b("PERM"), b("jf"), c1("pf", 12), O.is_equal)
+    ts(c1("pf", 13), pq, 16.0, O.mult, pl, O.add)
+    ts(c1("pf", 14), c1("pf", 13), 2.0, O.mult, ph, O.add)
+    ts(b("OUTP"), b("jf"), c1("pf", 14), O.is_equal)
+    ts(c1("pf", 13), pq, 32.0, O.mult, pl, O.add)
+    ts(c1("pf", 15), ph, -1.0, O.mult, 1.0, O.add)
+    ts(b("SH", 0, 128), b("i2"), c1("pf", 13), O.is_equal, c1("pf", 15), O.mult)
+    ts(b("SH", 128, 256), b("i2"), c1("pf", 13), O.is_equal, ph, O.mult)
+    mm(b("bM1", 0, 1), b("IW"), b("I2", 0, 128, 128))
+    mm(b("bM1", 1, 2), b("IW"), b("I2", 0, 128, 128))
+    cp(b("w2", 0, 2), b("bM1", 0, 2))
+    for r in range(N):
+        ts(b("MB", 128 * r, 128 * r + 128), b("IW"), c1("w2", 0), O.is_le, 16384.0, O.mult)
+    ts(b("t1"), Ib, 15.0, O.mult)
+    tt(b("t2"), b("t1"), b("BD"), O.subtract)
+    for i, (a, c) in enumerate((("t2", 8192.0), ("t2", -8192.0), ("BD", 8192.0), ("BD", -8192.0))):
+        ts(b("cAB", 128 * i, 128 * i + 128), b(a), c, O.mult)
+    fill(b("t1", 128, 256), 0.0)
+    cp(b("Sin", 0, 128), b("t1", 128, 256))
 
+    def stream(s):
+        grp = 2 * rank + s
+        B = lambda n, *a, **k: b(n + str(s), *a, **k)
+        P, Pm, Sd, E2, B0, Pw = B("P", 0, 64), B("Pm", 0, 64), B("Sd", 0, 64), B("E2", 0, 64), B("BP", 0, 64), B("BP", 64, 128)
+        table = B("tab", 0, W + 16)
+        z0 = 48 * s
+        cp(b("Sin", z0 + 16, z0 + 32), b("Ih", 16 * grp, 16 * grp + 16))
+        for h in range(2):
+            cp(b("Sin", 96 + 32 * s + 16 * h, 112 + 32 * s + 16 * h), b("Ih", 16 * grp, 16 * grp + 16))
+        fill(B("tab", W, W + 16), -256.0)
+        fill(B("Wn", 0, 272), EMPTY)
+        ts(B("hwf", 4, 5), ph, 256.0, O.mult, EMPTY + 2048.0, O.add)
+        ts(B("hn", 128, 192), b("jf", 0, 64), 4.0, O.mult, B("hwf", 4, 5), O.add)
+        for r in range(N):
+            pr32 = (32 * r, 32 * r + 32)
+            mm(B("bM", 128, 132, p=pr32), b("Sin", 96 + 32 * s, 128 + 32 * s), b("nat", r * NAT + 256, r * NAT + 260))
+            for w in range(2):
+                for h in range(2):
+                    o = r * NAT + 128 * w + 64 * h
+                    mm(B("bM", 64 * w, 64 * w + 64, p=pr32), b("Sin", z0 + 16 - 16 * h, z0 + 48 - 16 * h), b("nat", o, o + 64), h == 0, h == 1)
+        cp(P, B("bM", 0, 64)); cp(Sd, B("bM", 64, 128)); cp(B("hwf", 0, 4), B("bM", 128, 132))
+        for i in range(2):
+            ts(B("WW", 128 * i, 128 * i + 128), b("BD"), B("hwf", i, i + 1), O.mult, 0.5, O.mult)
+        ts(b("df"), b("If"), B("hwf", 2, 3), O.mult)
+        mm(B("bK"), b("BDf"), b("df"))
+        ts(b("di"), B("bK"), B("hwf", 1, 2), O.mult, 2048.0, O.add)
+        ts(b("di"), b("di"), 4095, O.bitwise_and)
+        ts(B("WW", 256, 384), b("di"), -2048.0, O.add, 0.5, O.mult)
+        ts(B("hwf", 5, 6), B("hwf", 3, 4), 2047.5, O.add, 4096.0, O.mult)
+        ts(B("hwf", 5, 6), B("hwf", 5, 6), c1("pf", 8), O.add)
+        ts(B("KT", 0, 4), b("jf", 0, 4), 16.0, O.mult, B("hwf", 5, 6), O.add)
 
-def helper_program(g, core, T, topo, r):
-    dests = [c for i, c in enumerate(T.cores) if i != r]
-    n_in = len([e for e in topo.engines(T.cores[r], core) if e not in topo.engines(T.cores[r], dests[0])])
-    ids = [DstId(rid=topo.addr(c)[0], pnc=topo.addr(c)[1]) for c in dests]
-    o = HELP[0][0]
-    for i, (c0, c1) in enumerate(HELP):
-        g.wait_ge(T.sem["hx%d" % i], n_in)
-        t = RemoteDMATransfer(dst_ids=ids, dma_engine_mask=topo.mask(core, dests[0]), remote_sem=T.sem["tz%d" % r],
-                              srcs=[T.zh[:, c0 - o:c1 - o]], dsts=[T.zall[:, r * BLK + c0:r * BLK + c1] for _ in dests])
-        g.remote_dma_fused([t], local_sem=T.sem.lsem)
-    g.wait_ge(T.sem.lsem, len(HELP) * len(topo.engines(core, dests[0])))
+        def hashes(p):
+            iw = lambda i, n=1: B("iw", 64 * i, 64 * (i + n))
+            hn = B("hn", 64 * p, 64 * p + 64)
+            cp(iw(0, 2), B("bM", 192, 320))
+            ts(iw(2, 2), iw(0, 2), 4095, O.bitwise_and)
+            tt(iw(4), iw(2), iw(3), O.mult)
+            ts(iw(5), iw(4), 5, O.arith_shift_right)
+            tt(iw(6), iw(5), B("bM", 320, 384), O.add)
+            ts(hn, iw(6), 4095, O.bitwise_and)
+            cp(B("hl", 0, 64), hn)
+
+        def search(p):
+            key = B("bK", 64 * p, 64 * p + 64)
+            mm(key, b("Ih"), b("KC", 64 * p, 64 * p + 64), True, False)
+            for lo, hi, e in CAND:
+                gather(e, B("V", lo, hi), table, B("hl", lo // 16, hi // 16))
+                for l in range(lo // 64, hi // 64):
+                    mm(key, b("ZV", 16 - l, 144 - l), B("V", 64 * l, 64 * l + 64), False, False)
+                tt(B("A", lo, hi), B("V", lo, hi), B("bE" if lo < 512 else "bF", lo % 512, (hi - 1) % 512 + 1), O.min)
+                for l in range(lo // 64, hi // 64):
+                    mm(key, b("ZA", 16 - l, 144 - l), B("A", 64 * l, 64 * l + 64), False, l == 15)
+            scan(B("km", 0, 64), b("d0k", 0, 64), key, O.max, O.min)
+
+        for t in range(RO):
+            for d in range(4):
+                mm(B("bM", 16 * d, 16 * d + 16), b("PERM"), B("P", d, 64, 4))
+            ts(B("offs", 0, 64), B("bM", 0, 64), 2048.0, O.min, 2048.0, O.add)
+            mm(B("bM", 0, 64), Ib, b("NH", 0, 64), True, False)
+            ts(Pm, P, EMPTY, O.min, c1("cx", t), O.max)
+            for h in range(2):
+                mm(B("bK", 384 + 64 * h, 448 + 64 * h), b("SH", 128 * h, 128 * h + 128), Pm)
+            act(B("Wn", 128, 256), B("bK", 384, 512), F.Copy)
+            for lo, hi, e in MID:
+                gather(e, B("Gv", lo, hi), table, B("offs", lo // 16, hi // 16))
+            for lo, hi, e in MID:
+                act(B("Ga", lo, hi), B("Gv", lo, hi), F.Abs)
+            for nm, v, d0, bank, o0, o1, o in (("Hi", "Gv", "d0h", "bE", O.min, O.max, 0), ("Lo", "Ga", "d0l", "bF", O.max, O.min, 192)):
+                for lo, hi, e in MID:
+                    scan(B(nm, lo, hi), b(d0, lo, hi), B(v, lo, hi), o0, o1)
+                for d in range(1, 4):
+                    rr = (d - 1 - t) % N
+                    mm(B(bank, 64 * d, 64 * d + 64), b("I2", 128 - 32 * d, 256 - 32 * d), B(nm, 4 * rr + 3, 1024, 16))
+                m = B(nm, 4 * ((-1 - t) % N) + 3, 1024, 16)
+                for d in range(1, 4):
+                    m2 = B("HL", o + 64 * d - 64, o + 64 * d)
+                    tt(m2, B(bank, 64 * d, 64 * d + 64), m, o1)
+                    m = m2
+                mm(B("bM", 0, 64), Ib, m, False, o > 0)
+            ts(E2, B("bM", 0, 64), M1, O.add, -M1, O.add)
+            for i in range(3):
+                mm(B("bM", 192 + 64 * i, 256 + 64 * i), B("WW", 128 * i, 128 * i + 128), E2)
+            mm(B("bK", 256, 384, p=(0, 64)), E2, b("HI"))
+            act(B("ET", p=(0, 64)), B("bK", 256, 384, p=(0, 64)), F.Copy)
+            for i, bank in enumerate(("bE", "bF")):
+                mm(B(bank, 0, 512), B("ET", p=(0, 64)), b("EXP", 512 * i, 512 * i + 512, p=(0, 64)))
+            hashes(0)
+            for c in range(4):
+                mm(B("bM", 16 * c, 16 * c + 16), b("HI"), B("E2", c, 64, 4))
+            act(B("Epl", 0, 64), B("bM", 0, 64), F.Identity, bias=-0.5)
+            search(0)
+            th = B("bK", 128, 132)
+            mm(th, b("If"), B("KT", 0, 4), True, False)
+            for l in range(16):
+                mm(th, b("ZE", 16 - l, 144 - l), B("E2", 4 * l, 4 * l + 4), False, l == 15)
+            k4 = B("km", 15, 64, 16)
+            cp(B("ki", 0, 4), k4)
+            ts(B("ki", 4, 8), B("ki", 0, 4), 1023, O.bitwise_and)
+            cp(B("lz", 0, 4), B("ki", 4, 8))
+            tt(B("cs", 0, 64), B("lz", 0, 4), B("Epl", 0, 64), O.add, win=B("V", 0, 1024))
+            ts(B("C2", 0, 64), B("cs", 0, 64), M1, O.add, -M1, O.add)
+            tt(B("km", 64, 68), k4, th, O.min)
+            for i in range(3):
+                for c in range(4):
+                    mm(B("bM", 192 + 64 * i + c, 256 + 64 * i, 4), B("WW", 128 * i, 128 * i + 128), B("C2", 16 * c, 16 * c + 16))
+            hashes(1)
+            search(1)
+            mm(B("bE", 0, 512), Ib, b("MB", 0, 512), True, False)
+            tt(B("ki", 0, 4), k4, B("km", 64, 68), O.min)
+            ts(B("ki", 4, 8), B("ki", 0, 4), 4, O.arith_shift_right, 255, O.bitwise_and)
+            ts(B("ki", 8, 12), B("ki", 0, 4), 15, O.bitwise_and)
+            cp(B("lz", 4, 12), B("ki", 4, 12))
+            ts(B("hs", 0, 64), B("lz", 4, 8), -2048.0, O.add, win=B("hn", 0, 192))
+            pd = B("pd", 0, 64)
+            tt(pd, B("lz", 8, 12), B("hs", 0, 64), O.mult, win=b("OHW", 0, 16))
+            for h in range(2):
+                mm(B("bM", 448, 452, p=(64 * h, 64 * h + 64)), pd, b("nS", 8 * t + 4 * h, 8 * t + 4 * h + 4))
+            for r in range(N):
+                for h in range(2):
+                    u = 2 * ((r + 1 + t) % N) + h
+                    mm(B("bE", 128 * r + 64 * h, 128 * r + 64 * h + 64), b("GO", 128 * u, 128 * u + 128), pd, False, r == 3 and h == 1)
+            sx = b("Sx", 128 * t, 128 * t + 128)
+            mm(B("bF", 384, 448), sx, b("m384", 0, 64), True, False)
+            for d in range(4):
+                mm(B("bF", 384 + 16 * d, 400 + 16 * d), sx, B("pd", d, 64, 4), False, d == 3)
+            for r in range(N):
+                xr_ = B("X", 128 * r, 128 * r + 128)
+                ts(xr_, B("bE", 128 * r, 128 * r + 128), B("bM", 448 + r, 449 + r), O.is_equal)
+                mm(B("bK", 200 + r, 201 + r), xr_, c1("w2", 0))
+            tt(Pw, Pm, B("bF", 384, 448), O.add)
+            for c in range(4):
+                mm(B("bM", 452 + c, 453 + c), B("X", c, 512, 4), c1("w2", 0))
+            mm(B("bE", 0, 8), Ib, b("zb", 0, 8), True, False)
+            for c in range(4):
+                mm(B("bE", c, c + 1), B("X", c, 512, 4), c1("w2", 0), False, False)
+            mm(B("bF"), Ib, b("CC"), True, False)
+            for r in range(N):
+                ts(B("M", 128 * r, 128 * r + 128), b("IW"), B("bK", 200 + r, 201 + r), O.is_equal)
+            for c in range(4):
+                mm(B("bE", c, 8, 4), B("M", c, 512, 4), b("w2", 0, 2), False, c == 3)
+            fw = lambda i, n=1: B("fw", 64 * i, 64 * (i + n))
+            ts(B("lz", 12, 16), B("bM", 452, 456), 256.0, O.min)
+            tt(fw(0), B("lz", 12, 16), Sd, O.max, win=b("F1", 0, 272))
+            tt(fw(1), B("lz", 12, 16), Pw, O.max, win=b("F2", 0, 272))
+            tt(fw(2), fw(0), fw(1), O.min)
+            ts(B("lz", 16, 24), B("bE", 0, 8), 256.0, O.min)
+            tt(fw(3), B("lz", 16, 20), Pm, O.subtract, win=B("Wn", 0, 272))
+            ts(B("gg", 0, 64), fw(3), M13, O.add, M13, O.is_equal)
+            ts(B("gg", 64, 128), fw(3), 0.0, O.is_equal)
+            tt(B0, B("lz", 20, 24), fw(2), O.min, win=B("Wn", 0, 272))
+            for i in range(4):
+                mm(B("bF", 64 - 64 * (i // 2), 128 - 64 * (i // 2)), b("cAB", 128 * i, 128 * i + 128), B("gg", 64 * (i % 2), 64 * (i % 2) + 64), False, i == 3)
+            tt(fw(4, 2), B("BP"), B("bF"), O.max)
+            tt(P, fw(4), fw(5), O.min)
+        mm(B("bM", 0, 64), b("OUTP"), P)
+        ts(B("fw", 0, 64), B("bM", 0, 64), 2048.0, O.is_ge, -4097.0, O.mult)
+        ts(B("fw", 64, 128), B("bM", 0, 64), 2048.0, O.min, 2048.0, O.add)
+        tt(B("yo", 0, 64), B("fw", 0, 64), B("fw", 64, 128), O.add)
+        send(others, B("yo", 0, 64), b("yl", 64 * grp, 64 * grp + 64), "y%d" % grp, 0.0)
+        mine = (32 * rank, 32 * rank + 32)
+        op("Y", [], [B("yo", 0, 64)], lambda: g.sync.dma_start(rows("yp", grp), ap(B("yo", 0, 64, p=mine))).then_inc(T.sem.st, 16), 50.0, raw=True)
+        for i, q in enumerate(others[::-1]):
+            gq = 2 * q + s
+            e, en = (g.scalar, "S") if i == 1 and s == 1 else (g.sync, "Y")
+
+            def home(gq=gq, e=e):
+                e.wait_ge(T.sem["y%d" % gq], eo)
+                e.dma_start(rows("yp", gq), ap(b("yl", 64 * gq, 64 * gq + 64, p=mine))).then_inc(T.sem.st, 16)
+            op(en, [], [B("yo", 0, 64)], home, 50.0, raw=True)
+
+    for s in range(2):
+        i0 = len(ops)
+        stream(s)
+        for o in ops[i0:]:
+            o["lead"] = LEAD * (1 - s)
+    ops2 = order(ops)
+    if report is not None:
+        report.extend(ops2)
+    issue(g, T, ops2)
+    g.sync.wait_ge(T.sem.st, 128)
+    g.wait_ge(T.sem.lsem, local[0])

@@ -6,7 +6,9 @@ EMPTY = 6144.0
 M1, M13 = 1.5 * 2.0 ** 24, 1.5 * 2.0 ** 36
 NAT = 272
 MID = ((0, 512, "S"), (512, 1024, "S"))
-CAND = ((0, 256, "S"), (256, 512, "S"), (512, 768, "S"), (768, 1024, "S"))
+CAND = ((0, 192, "V", "min", "bE"), (192, 512, "S", "min", "bF"), (512, 832, "S", "min", "bE"), (832, 1024, "S", "min", "bF"))
+SENDS = (1, 0, 2, None, 5, 3, 4)
+HELP = (1, 2, 5)
 
 SCRATCH = {}
 for _n, _c, _d in (
@@ -25,20 +27,21 @@ for _n, _c, _d in (
         ("i2", 128, "float32"), ("pi", 64, "int32"), ("pf", 64, "float32"), ("IW", 128, "bfloat16"), ("w2", 2, "bfloat16"),
         ("I2", 256, "bfloat16"), ("Ih", 128, "float16"), ("If", 128, "float32"), ("HI", 128, "float16"), ("BD", 128, "bfloat16"),
         ("BDf", 128, "float32"), ("ZV", 144, "bfloat16"), ("ZA", 144, "bfloat16"), ("ZE", 144, "float16"), ("EXP", 1024, "bfloat16"),
-        ("d0h", 1024, "bfloat16"), ("d0l", 1024, "bfloat16"), ("d0k", 64, "float32"), ("NH", 64, "bfloat16"), ("KC", 128, "float16"),
+        ("d0h", 1024, "bfloat16"), ("d0l", 1024, "bfloat16"), ("d0k", 64, "float32"), ("NH", 256, "bfloat16"), ("d04", 256, "bfloat16"), ("KC", 128, "float16"),
         ("OHW", 16, "bfloat16"), ("Sx", 768, "float16"), ("nS", 48, "float16"), ("GO", 1024, "float16"), ("MB", 512, "bfloat16"),
         ("F1", 272, "float32"), ("F2", 272, "float32"), ("PERM", 128, "float16"), ("OUTP", 128, "float16"), ("SH", 256, "float16"),
         ("cAB", 512, "bfloat16"), ("CC", 128, "bfloat16"), ("m384", 64, "float16"), ("cx", 8, "float32"), ("Sin", 160, "float16"),
-        ("zb", 8, "bfloat16"), ("di", 128, "int32"), ("df", 128, "float32")):
+        ("zb", 16, "bfloat16"), ("IN", 128, "bfloat16"), ("di", 128, "int32"), ("df", 128, "float32")):
     SCRATCH[_n] = ("sbuf", [128, _c], _d)
 BANKS = tuple(n + s for s in "01" for n in ("bE", "bF", "bK", "bM"))
 for _n in BANKS:
     SCRATCH[_n] = ("psum", [128, 512], "float32")
 SEMAPHORES = (["cV", "cS", "cT", "cG", "ldn", "tb0", "tb1", "st", "lsem"] + ["ld%d" % i for i in range(6)]
-              + ["%s%d" % (n, i) for n in ("z", "y") for i in range(2 * N)] + ["n%d" % i for i in range(N)])
+              + ["%s%d" % (n, i) for n in ("z", "y") for i in range(2 * N)] + ["n%d" % i for i in range(N)]
+              + ["hx%d" % j for j in HELP])
 WIDE = {"float32": 4, "int32": 4, "float16": 2, "bfloat16": 2, "uint16": 2}
-LEAD = 6000.0
-WAKE, NEAR = 100.0, 60.0
+LEAD = 2000.0
+WAKE, SAME, NEAR = 125.0, 125.0, 0.3
 
 
 def b(n, lo=0, hi=128, st=1, p=(0, 128)):
@@ -58,6 +61,8 @@ def order(ops):
                 bank = r[0] in BANKS
                 for j, w2, r2 in acc.get(r[0], ()):
                     same = ops[j]["e"] == o["e"]
+                    if o["sum"] is not None and ops[j]["sum"] is o["sum"]:
+                        continue
                     if (bank and (not same or o["e"] == "T")) or ((w or w2) and over(r, r2)):
                         wait = not (same and o["e"] == "T")
                         dep[j] = dep.get(j, False) or wait
@@ -68,12 +73,12 @@ def order(ops):
                 old = acc.get(r[0], [])
                 if w and r[3] == 1 and r[4] == (0, 128) and r[0] not in BANKS:
                     old = [a for a in old if not (r[1] <= a[2][1] and a[2][2] <= r[2])]
-                acc[r[0]] = old[-40:] + [(i, w, r)] if r[0] in BANKS else old + [(i, w, r)]
+                acc[r[0]] = old[-48:] + [(i, w, r)] if r[0] in BANKS else old + [(i, w, r)]
     left = [o["ns"] + o["urge"] for o in ops]
     users = [[] for _ in ops]
     for i in range(len(ops) - 1, -1, -1):
         for j, wait in ops[i]["dep"].items():
-            left[j] = max(left[j], left[i] + ((ops[j]["ns"] + WAKE) if wait else 0.0))
+            left[j] = max(left[j], left[i] + ((ops[j]["ns"] + (SAME if ops[j]["e"] == ops[i]["e"] else WAKE)) if wait else 0.0))
             users[j].append(i)
     left = [v + o["lead"] for v, o in zip(left, ops)]
     miss = [len(o["dep"]) for o in ops]
@@ -82,7 +87,7 @@ def order(ops):
     while ready:
         est = {i: max(t, free.get(ops[i]["e"], 0.0)) for i, t in ready.items()}
         first = min(est, key=lambda i: (est[i], -left[i]))
-        i = max((j for j in est if ops[j]["e"] == ops[first]["e"] and est[j] <= est[first] + NEAR), key=lambda j: (left[j], -j))
+        i = max((j for j in est if ops[j]["e"] == ops[first]["e"] and est[j] <= est[first] + NEAR * ops[first]["ns"]), key=lambda j: (left[j], -j))
         start[i] = est[i]
         if ops[i]["e"] != "D":
             free[ops[i]["e"]] = est[i] + ops[i]["ns"]
@@ -91,7 +96,7 @@ def order(ops):
         for u in users[i]:
             miss[u] -= 1
             if not miss[u]:
-                ready[u] = max(start[j] + ((ops[j]["ns"] + WAKE) if wait else 0.0) for j, wait in ops[u]["dep"].items())
+                ready[u] = max(start[j] + ((ops[j]["ns"] + (SAME if ops[j]["e"] == ops[u]["e"] else WAKE)) if wait else 0.0) for j, wait in ops[u]["dep"].items())
     for i in out:
         ops[i]["at"] = start[i]
     return [ops[i] for i in out]
@@ -132,9 +137,28 @@ def issue(g, T, ops):
     need("Y", {"c" + e: cnt[e] for e in "VSTG"})
 
 
+def on_chip_only(topo, core, near, far):
+    return [e for e in topo.engines(core, near) if e not in topo.engines(core, far)]
+
+
+def helper_program(g, core, T, topo, r):
+    others = [T.cores[(r + i) % N] for i in range(1, N)]
+    for j in HELP:
+        c, x = others[j % 3], 2 * r + j // 3
+        g.wait_ge(T.sem["hx%d" % j], len(on_chip_only(topo, T.cores[r], core, c)))
+        t = RemoteDMATransfer(dst_ids=[DstId(rid=topo.addr(c)[0], pnc=topo.addr(c)[1])], dma_engine_mask=topo.mask(core, c), remote_sem=T.sem["z%d" % x],
+                              srcs=[T.zs[:, 512 * j:512 * j + 512]], dsts=[T.zl[:, 512 * x:512 * x + 512]])
+        g.remote_dma_fused([t], local_sem=T.sem.lsem)
+    g.wait_ge(T.sem.lsem, len(HELP) * len(topo.engines(core, others[0])))
+
+
 def rank_program(g, core, T, topo, report=None):
     rank = T.rank_of(core)
+    helpers = [[k for k in topo.cores_of(c) if topo.die(k) != topo.die(c) and all(topo.may_write(k, d) for d in T.cores if d != c)][0]
+               for c in T.cores]
     if rank is None:
+        if core in helpers:
+            helper_program(g, core, T, topo, helpers.index(core))
         return
     ops = []
 
@@ -148,7 +172,7 @@ def rank_program(g, core, T, topo, report=None):
         return all(WIDE[SCRATCH[r[0]][2]] == 2 for r in rs)
 
     def op(e, outs, ins, call, ns, raw=False, urge=0.0, done=None):
-        ops.append({"e": e, "outs": outs, "ins": ins, "call": call, "ns": ns, "raw": raw, "urge": urge, "done": done, "all": ops, "lead": 0.0})
+        ops.append({"e": e, "outs": outs, "ins": ins, "call": call, "ns": ns, "raw": raw, "urge": urge, "done": done, "all": ops, "lead": 0.0, "sum": None})
 
     def landed(sem, n, refs, at):
         op("D", refs, [], None, at, done=(sem, n))
@@ -190,8 +214,14 @@ def rank_program(g, core, T, topo, report=None):
         op("V", [out], [], lambda: g.vector.memset(ap(out), c), vns(out, out, None, 0.5 if narrow(out) else 1.0))
 
     def mm(out, l, r, start=True, stop=True):
-        op("T", [out], [l, r], lambda: g.tensor.matmul(ap(out), ap(l), ap(r), start, stop),
-           0.5 * max(min(64, size(l)), size(r)) * (1 if narrow(l) else 4) + 10.0)
+        def call():
+            if isinstance(stop, list):
+                stop[0] -= 1
+            return g.tensor.matmul(ap(out), ap(l), ap(r), start, stop[0] == 0 if isinstance(stop, list) else stop)
+        op("T", [out], [l, r], call, 0.5 * max(min(64, size(l)), size(r)) * (1 if narrow(l) else 4) + 10.0)
+        if isinstance(stop, list):
+            stop[0] += 1
+            ops[-1]["sum"] = stop
 
     def iota(out, pattern, base, cm):
         k = {} if SCRATCH[out[0]][2] == "int32" else {"allow_small_or_imprecise_dtypes": True}
@@ -199,15 +229,16 @@ def rank_program(g, core, T, topo, report=None):
 
     local = [0]
 
-    def send(ranks, a, dst, sem, urge):
-        cs = [T.cores[r] for r in ranks]
-        t = RemoteDMATransfer(dst_ids=[DstId(rid=topo.addr(c)[0], pnc=topo.addr(c)[1]) for c in cs], dma_engine_mask=topo.mask(core, cs[0]),
+    def send(cs, a, dst, sem, urge, engines=None):
+        engines = engines or topo.engines(core, cs[0])
+        t = RemoteDMATransfer(dst_ids=[DstId(rid=topo.addr(c)[0], pnc=topo.addr(c)[1]) for c in cs], dma_engine_mask=sum(1 << e for e in engines),
                               remote_sem=T.sem[sem], srcs=[ap(a)], dsts=[ap(dst) for _ in cs])
         op("G", [], [a], lambda: g.remote_dma_fused([t], local_sem=T.sem.lsem), 500.0, raw=True, urge=urge)
-        local[0] += len(topo.engines(core, cs[0]))
+        local[0] += len(engines)
 
     others = [(rank + i) % N for i in range(1, N)]
     eo = len(topo.engines(T.cores[others[0]], core))
+    spare = on_chip_only(topo, core, helpers[rank], T.cores[others[0]])
 
     def rows(t, grp):
         return T[t][16 * grp:16 * grp + 16, :]
@@ -243,12 +274,14 @@ def rank_program(g, core, T, topo, report=None):
     tt(b("nat", n0, n0 + 256), b("t1", 0, 256), b("t2", 0, 256), O.add)
     cp(b("nat", n0 + 256, n0 + 259), b("tpi", 256, 259))
     ts(b("nat", n0 + 259, n0 + 260), b("tpi", 259, 260), -2048, O.add)
-    for s in range(2):
-        for i, d in enumerate(others):
-            j = 2 * rank + s
-            send([d], b("zs", 512 * (3 * s + i), 512 * (3 * s + i + 1)), b("zl", 512 * j, 512 * j + 512), "z%d" % j, 1e6 - 1e3 * (4 * s + i))
-        if s == 0:
-            send(others, b("nat", n0, n0 + 260), b("nat", n0, n0 + 260), "n%d" % rank, 1e6 - 3e3)
+    for k, j in enumerate(SENDS):
+        if j is None:
+            send([T.cores[d] for d in others], b("nat", n0, n0 + 260), b("nat", n0, n0 + 260), "n%d" % rank, 1e6 - 1e3 * k)
+        elif j in HELP:
+            send([helpers[rank]], b("zs", 512 * j, 512 * j + 512), b("zs", 512 * j, 512 * j + 512), "hx%d" % j, 1e6 - 1e3 * k, spare)
+        else:
+            x = 2 * rank + j // 3
+            send([T.cores[others[j % 3]]], b("zs", 512 * j, 512 * j + 512), b("zl", 512 * x, 512 * x + 512), "z%d" % x, 1e6 - 1e3 * k)
     for q in others:
         landed("n%d" % q, eo, [b("nat", q * NAT, q * NAT + 260)], 9000.0)
 
@@ -271,6 +304,7 @@ def rank_program(g, core, T, topo, report=None):
     Ib = b("I2")
     cp(b("Ih"), Ib); cp(b("If"), Ib)
     ts(b("HI"), Ib, 0.5, O.mult)
+    ts(b("IN"), Ib, -1.0, O.mult)
     ts(b("BD"), b("j16"), pu, O.is_equal)
     cp(b("BDf"), b("BD"))
     for nm, c in (("ZV", 4096.0), ("ZA", -8192.0)):
@@ -282,7 +316,8 @@ def rank_program(g, core, T, topo, report=None):
     for nm, w, st, lo, hi in (("d0h", 1024, 4, 255.0, 0.0), ("d0l", 1024, 4, 0.0, 255.0), ("d0k", 64, 16, -1.0e9, 1.0e9)):
         fill(b(nm, 0, w), lo)
         fill(b(nm, 0, w, st), hi)
-    fill(b("NH", 0, 64), -0.5); fill(b("zb", 0, 8), 0.0)
+    ts(b("d04", 0, 256), b("d0l", 0, 256), 8.0, O.mult, -1.0, O.add)
+    fill(b("NH", 0, 256), -0.5); fill(b("zb", 0, 16), 0.0)
     ts(b("m384", 0, 64), b("NH", 0, 64), 768.0, O.mult)
     fill(b("CC"), -2048.0); fill(b("CC", 64, 128), EMPTY)
     fill(b("F1", 0, 272), EMPTY); fill(b("F1", 128, 256), -4096.0)
@@ -328,7 +363,8 @@ def rank_program(g, core, T, topo, report=None):
     mm(b("bM1", 0, 1), b("IW"), b("I2", 0, 128, 128))
     mm(b("bM1", 1, 2), b("IW"), b("I2", 0, 128, 128))
     cp(b("w2", 0, 2), b("bM1", 0, 2))
-    for r in range(N):
+    fill(b("MB", 256, 260), 0.0)
+    for r in range(2):
         ts(b("MB", 128 * r, 128 * r + 128), b("IW"), c1("w2", 0), O.is_le, 16384.0, O.mult)
     ts(b("t1"), Ib, 15.0, O.mult)
     tt(b("t2"), b("t1"), b("BD"), O.subtract)
@@ -372,7 +408,16 @@ def rank_program(g, core, T, topo, report=None):
         def hashes(p):
             iw = lambda i, n=1: B("iw", 64 * i, 64 * (i + n))
             hn = B("hn", 64 * p, 64 * p + 64)
+
+            def sums(i):
+                w = B("WW", 128 * i, 128 * i + 128)
+                if p == 0:
+                    mm(B("bM", 192 + 64 * i, 256 + 64 * i), w, E2)
+                for c in range(4 * p):
+                    mm(B("bM", 192 + 64 * i + c, 256 + 64 * i, 4), w, B("C2", 16 * c, 16 * c + 16))
+            sums(0); sums(1)
             cp(iw(0, 2), B("bM", 192, 320))
+            sums(2)
             ts(iw(2, 2), iw(0, 2), 4095, O.bitwise_and)
             tt(iw(4), iw(2), iw(3), O.mult)
             ts(iw(5), iw(4), 5, O.arith_shift_right)
@@ -383,20 +428,30 @@ def rank_program(g, core, T, topo, report=None):
         def search(p):
             key = B("bK", 64 * p, 64 * p + 64)
             mm(key, b("Ih"), b("KC", 64 * p, 64 * p + 64), True, False)
-            for lo, hi, e in CAND:
+            sums, fillp = [0], {"bE": 0, "bF": 0}
+            for lo, hi, e, how, bank in CAND:
+                e16 = B(bank, fillp[bank], fillp[bank] + hi - lo)
+                fillp[bank] += hi - lo
+                lanes = range(lo // 64, hi // 64)
+                if p == 0 or how == "abs":
+                    mm(e16, B("ET", p=(0, 64)), b("EXP", lo, hi, p=(0, 64)), True, how == "min")
                 gather(e, B("V", lo, hi), table, B("hl", lo // 16, hi // 16))
-                for l in range(lo // 64, hi // 64):
-                    mm(key, b("ZV", 16 - l, 144 - l), B("V", 64 * l, 64 * l + 64), False, False)
-                tt(B("A", lo, hi), B("V", lo, hi), B("bE" if lo < 512 else "bF", lo % 512, (hi - 1) % 512 + 1), O.min)
-                for l in range(lo // 64, hi // 64):
-                    mm(key, b("ZA", 16 - l, 144 - l), B("A", 64 * l, 64 * l + 64), False, l == 15)
+                if how == "abs":
+                    mm(e16, b("IN"), B("V", lo, hi), False, True)
+                    act(B("A", lo, hi), e16, F.Abs)
+                else:
+                    for l in lanes:
+                        mm(key, b("ZV", 16 - l, 144 - l), B("V", 64 * l, 64 * l + 64), False, sums)
+                    tt(B("A", lo, hi), B("V", lo, hi), e16, O.min)
+                for l in lanes:
+                    mm(key, b("ZV" if how == "abs" else "ZA", 16 - l, 144 - l), B("A", 64 * l, 64 * l + 64), False, sums)
             scan(B("km", 0, 64), b("d0k", 0, 64), key, O.max, O.min)
 
         for t in range(RO):
             for d in range(4):
                 mm(B("bM", 16 * d, 16 * d + 16), b("PERM"), B("P", d, 64, 4))
             ts(B("offs", 0, 64), B("bM", 0, 64), 2048.0, O.min, 2048.0, O.add)
-            mm(B("bM", 0, 64), Ib, b("NH", 0, 64), True, False)
+            mm(B("bF", 0, 256), Ib, b("NH", 0, 256), True, False)
             ts(Pm, P, EMPTY, O.min, c1("cx", t), O.max)
             for h in range(2):
                 mm(B("bK", 384 + 64 * h, 448 + 64 * h), b("SH", 128 * h, 128 * h + 128), Pm)
@@ -405,34 +460,39 @@ def rank_program(g, core, T, topo, report=None):
                 gather(e, B("Gv", lo, hi), table, B("offs", lo // 16, hi // 16))
             for lo, hi, e in MID:
                 act(B("Ga", lo, hi), B("Gv", lo, hi), F.Abs)
-            for nm, v, d0, bank, o0, o1, o in (("Hi", "Gv", "d0h", "bE", O.min, O.max, 0), ("Lo", "Ga", "d0l", "bF", O.max, O.min, 192)):
-                for lo, hi, e in MID:
-                    scan(B(nm, lo, hi), b(d0, lo, hi), B(v, lo, hi), o0, o1)
-                for d in range(1, 4):
-                    rr = (d - 1 - t) % N
-                    mm(B(bank, 64 * d, 64 * d + 64), b("I2", 128 - 32 * d, 256 - 32 * d), B(nm, 4 * rr + 3, 1024, 16))
-                m = B(nm, 4 * ((-1 - t) % N) + 3, 1024, 16)
-                for d in range(1, 4):
-                    m2 = B("HL", o + 64 * d - 64, o + 64 * d)
-                    tt(m2, B(bank, 64 * d, 64 * d + 64), m, o1)
-                    m = m2
-                mm(B("bM", 0, 64), Ib, m, False, o > 0)
-            ts(E2, B("bM", 0, 64), M1, O.add, -M1, O.add)
-            for i in range(3):
-                mm(B("bM", 192 + 64 * i, 256 + 64 * i), B("WW", 128 * i, 128 * i + 128), E2)
+            part = lambda nm, d: B(nm, 4 * ((d - 1 - t) % N) + 3, 1024, 16)
+            shift = lambda d: b("I2", 128 - 32 * d, 256 - 32 * d)
+            for lo, hi, e in MID:
+                scan(B("Hi", lo, hi), b("d0h", lo, hi), B("Gv", lo, hi), O.min, O.max)
+            m = part("Hi", 0)
+            for d in range(1, 4):
+                mm(B("bE", 64 * d, 64 * d + 64), shift(d), part("Hi", d))
+            for d in range(1, 4):
+                tt(B("HL", 64 * d - 64, 64 * d), B("bE", 64 * d, 64 * d + 64), m, O.max)
+                m = B("HL", 64 * d - 64, 64 * d)
+            for lo, hi, e in MID:
+                scan(B("Lo", lo, hi), b("d0l", lo, hi), B("Ga", lo, hi), O.max, O.min)
+            sums = [0]
+            for d in range(4):
+                mm(B("bF", d, 256, 4), Ib, m, False, sums)
+                mm(B("bF", d, 256, 4), shift(d), part("Lo", d), False, sums)
+            scan(B("fw", 0, 256), b("d04", 0, 256), B("bF", 0, 256), O.max, O.min)
+            ts(E2, B("fw", 3, 256, 4), M1, O.add, -M1, O.add)
             mm(B("bK", 256, 384, p=(0, 64)), E2, b("HI"))
             act(B("ET", p=(0, 64)), B("bK", 256, 384, p=(0, 64)), F.Copy)
-            for i, bank in enumerate(("bE", "bF")):
-                mm(B(bank, 0, 512), B("ET", p=(0, 64)), b("EXP", 512 * i, 512 * i + 512, p=(0, 64)))
             hashes(0)
             for c in range(4):
                 mm(B("bM", 16 * c, 16 * c + 16), b("HI"), B("E2", c, 64, 4))
             act(B("Epl", 0, 64), B("bM", 0, 64), F.Identity, bias=-0.5)
             search(0)
             th = B("bK", 128, 132)
-            mm(th, b("If"), B("KT", 0, 4), True, False)
-            for l in range(16):
-                mm(th, b("ZE", 16 - l, 144 - l), B("E2", 4 * l, 4 * l + 4), False, l == 15)
+            lanes = [l for lo, hi, e, how, bank in CAND if how == "min" for l in range(lo // 64, hi // 64)]
+            if lanes:
+                mm(th, b("If"), B("KT", 0, 4), True, False)
+            else:
+                th = B("KT", 0, 4)
+            for l in lanes:
+                mm(th, b("ZE", 16 - l, 144 - l), B("E2", 4 * l, 4 * l + 4), False, l == lanes[-1])
             k4 = B("km", 15, 64, 16)
             cp(B("ki", 0, 4), k4)
             ts(B("ki", 4, 8), B("ki", 0, 4), 1023, O.bitwise_and)
@@ -440,12 +500,10 @@ def rank_program(g, core, T, topo, report=None):
             tt(B("cs", 0, 64), B("lz", 0, 4), B("Epl", 0, 64), O.add, win=B("V", 0, 1024))
             ts(B("C2", 0, 64), B("cs", 0, 64), M1, O.add, -M1, O.add)
             tt(B("km", 64, 68), k4, th, O.min)
-            for i in range(3):
-                for c in range(4):
-                    mm(B("bM", 192 + 64 * i + c, 256 + 64 * i, 4), B("WW", 128 * i, 128 * i + 128), B("C2", 16 * c, 16 * c + 16))
             hashes(1)
             search(1)
-            mm(B("bE", 0, 512), Ib, b("MB", 0, 512), True, False)
+            for bank in ("bE", "bF"):
+                mm(B(bank, 0, 260), Ib, b("MB", 0, 260), True, False)
             tt(B("ki", 0, 4), k4, B("km", 64, 68), O.min)
             ts(B("ki", 4, 8), B("ki", 0, 4), 4, O.arith_shift_right, 255, O.bitwise_and)
             ts(B("ki", 8, 12), B("ki", 0, 4), 15, O.bitwise_and)
@@ -453,37 +511,39 @@ def rank_program(g, core, T, topo, report=None):
             ts(B("hs", 0, 64), B("lz", 4, 8), -2048.0, O.add, win=B("hn", 0, 192))
             pd = B("pd", 0, 64)
             tt(pd, B("lz", 8, 12), B("hs", 0, 64), O.mult, win=b("OHW", 0, 16))
-            for h in range(2):
-                mm(B("bM", 448, 452, p=(64 * h, 64 * h + 64)), pd, b("nS", 8 * t + 4 * h, 8 * t + 4 * h + 4))
-            for r in range(N):
+            for i, bank in enumerate(("bE", "bF")):
                 for h in range(2):
-                    u = 2 * ((r + 1 + t) % N) + h
-                    mm(B("bE", 128 * r + 64 * h, 128 * r + 64 * h + 64), b("GO", 128 * u, 128 * u + 128), pd, False, r == 3 and h == 1)
+                    n = 8 * t + 4 * h + 2 * i
+                    mm(B(bank, 256, 258, p=(64 * h, 64 * h + 64)), pd, b("nS", n, n + 2), False, False)
+                for j in range(4):
+                    u = 2 * ((2 * i + j // 2 + 1 + t) % N) + j % 2
+                    mm(B(bank, 64 * j, 64 * j + 64), b("GO", 128 * u, 128 * u + 128), pd, False, j == 3)
             sx = b("Sx", 128 * t, 128 * t + 128)
-            mm(B("bF", 384, 448), sx, b("m384", 0, 64), True, False)
+            mm(B("bM", 384, 448), sx, b("m384", 0, 64), True, False)
             for d in range(4):
-                mm(B("bF", 384 + 16 * d, 400 + 16 * d), sx, B("pd", d, 64, 4), False, d == 3)
+                mm(B("bM", 384 + 16 * d, 400 + 16 * d), sx, B("pd", d, 64, 4), False, d == 3)
+            ys = [B("bM" if r // 2 else "bK", 448 + r, 449 + r) for r in range(N)]
             for r in range(N):
-                xr_ = B("X", 128 * r, 128 * r + 128)
-                ts(xr_, B("bE", 128 * r, 128 * r + 128), B("bM", 448 + r, 449 + r), O.is_equal)
-                mm(B("bK", 200 + r, 201 + r), xr_, c1("w2", 0))
-            tt(Pw, Pm, B("bF", 384, 448), O.add)
+                xr_, bank = B("X", 128 * r, 128 * r + 128), "bF" if r // 2 else "bE"
+                ts(xr_, B(bank, 128 * (r % 2), 128 * (r % 2) + 128), B(bank, 256 + r % 2, 257 + r % 2), O.is_equal)
+                mm(ys[r], xr_, c1("w2", 0))
             for c in range(4):
-                mm(B("bM", 452 + c, 453 + c), B("X", c, 512, 4), c1("w2", 0))
-            mm(B("bE", 0, 8), Ib, b("zb", 0, 8), True, False)
-            for c in range(4):
-                mm(B("bE", c, c + 1), B("X", c, 512, 4), c1("w2", 0), False, False)
+                mm(B("bE", c, c + 1), B("X", c, 512, 4), c1("w2", 0))
             mm(B("bF"), Ib, b("CC"), True, False)
             for r in range(N):
-                ts(B("M", 128 * r, 128 * r + 128), b("IW"), B("bK", 200 + r, 201 + r), O.is_equal)
+                ts(B("M", 128 * r, 128 * r + 128), b("IW"), ys[r], O.is_equal)
+            mm(B("bK", 200, 208), Ib, b("zb", 0, 8), True, False)
             for c in range(4):
-                mm(B("bE", c, 8, 4), B("M", c, 512, 4), b("w2", 0, 2), False, c == 3)
+                mm(B("bK", 200 + c, 201 + c), B("X", c, 512, 4), c1("w2", 0), False, False)
+            tt(Pw, Pm, B("bM", 384, 448), O.add)
+            ts(B("lz", 12, 16), B("bE", 0, 4), 256.0, O.min)
+            for c in range(4):
+                mm(B("bK", 200 + c, 208, 4), B("M", c, 512, 4), b("w2", 0, 2), False, c == 3)
             fw = lambda i, n=1: B("fw", 64 * i, 64 * (i + n))
-            ts(B("lz", 12, 16), B("bM", 452, 456), 256.0, O.min)
             tt(fw(0), B("lz", 12, 16), Sd, O.max, win=b("F1", 0, 272))
             tt(fw(1), B("lz", 12, 16), Pw, O.max, win=b("F2", 0, 272))
             tt(fw(2), fw(0), fw(1), O.min)
-            ts(B("lz", 16, 24), B("bE", 0, 8), 256.0, O.min)
+            ts(B("lz", 16, 24), B("bK", 200, 208), 256.0, O.min)
             tt(fw(3), B("lz", 16, 20), Pm, O.subtract, win=B("Wn", 0, 272))
             ts(B("gg", 0, 64), fw(3), M13, O.add, M13, O.is_equal)
             ts(B("gg", 64, 128), fw(3), 0.0, O.is_equal)
@@ -496,7 +556,7 @@ def rank_program(g, core, T, topo, report=None):
         ts(B("fw", 0, 64), B("bM", 0, 64), 2048.0, O.is_ge, -4097.0, O.mult)
         ts(B("fw", 64, 128), B("bM", 0, 64), 2048.0, O.min, 2048.0, O.add)
         tt(B("yo", 0, 64), B("fw", 0, 64), B("fw", 64, 128), O.add)
-        send(others, B("yo", 0, 64), b("yl", 64 * grp, 64 * grp + 64), "y%d" % grp, 0.0)
+        send([T.cores[d] for d in others], B("yo", 0, 64), b("yl", 64 * grp, 64 * grp + 64), "y%d" % grp, 0.0)
         mine = (32 * rank, 32 * rank + 32)
         op("Y", [], [B("yo", 0, 64)], lambda: g.sync.dma_start(rows("yp", grp), ap(B("yo", 0, 64, p=mine))).then_inc(T.sem.st, 16), 50.0, raw=True)
         for i, q in enumerate(others[::-1]):

@@ -3,22 +3,23 @@ from concourse.mybir import AluOpType as O, ActivationFunctionType as F
 
 N, W, RO = 4, 4096, 6
 EMPTY = 6144.0
-M1, M13 = 1.5 * 2.0 ** 24, 1.5 * 2.0 ** 36
+XL = [4 * ((-1 - t) % N) + t // 4 for t in range(RO)]
 NAT = 272
-MID = ((0, 512, "S"), (512, 1024, "S"))
-CAND = ((0, 192, "V", "min", "bE"), (192, 512, "S", "min", "bF"), (512, 832, "S", "min", "bE"), (832, 1024, "S", "min", "bF"))
+MID = ((0, 256, "V"), (256, 640, "S"), (640, 1024, "S"))
+ABS = ((0, 256, False), (256, 640, False), (640, 1024, False))
+CAND = ((0, 192, "V", "bE"), (192, 512, "S", "bF"), (512, 832, "S", "bE"), (832, 1024, "S", "bF"))
 SENDS = (1, 0, 2, None, 5, 3, 4)
 HELP = (1, 2, 5)
 
 SCRATCH = {}
 for _n, _c, _d in (
         ("tab", W + 16, "bfloat16"), ("offs", 64, "uint16"), ("Gv", 1024, "bfloat16"), ("Ga", 1024, "bfloat16"), ("Hi", 1024, "bfloat16"),
-        ("Lo", 1024, "bfloat16"), ("HL", 384, "bfloat16"), ("E2", 64, "float16"), ("ET", 128, "bfloat16"), ("Epl", 64, "float32"),
+        ("Lo", 1024, "bfloat16"), ("HL", 192, "bfloat16"), ("E2", 256, "float16"), ("ET", 128, "bfloat16"), ("Epl", 64, "float32"),
         ("iw", 448, "int32"), ("hn", 192, "int32"), ("hl", 64, "uint16"), ("V", 1024, "bfloat16"), ("A", 1024, "bfloat16"),
-        ("km", 72, "float32"), ("ki", 16, "int32"), ("lz", 24, "uint16"), ("cs", 64, "float32"), ("C2", 64, "float16"),
-        ("hs", 64, "float16"), ("pd", 64, "float16"), ("BP", 128, "float32"), ("Pm", 64, "float16"), ("P", 64, "float16"),
-        ("Sd", 64, "float32"), ("X", 512, "bfloat16"), ("M", 512, "bfloat16"), ("fw", 384, "float32"), ("gg", 128, "bfloat16"),
-        ("Wn", 272, "float32"), ("WW", 384, "float16"), ("KT", 4, "float32"), ("hwf", 8, "float32"), ("yo", 64, "float32")):
+        ("km", 72, "float32"), ("ki", 16, "int32"), ("lz", 24, "uint16"), ("Pr", 128, "float32"), ("C2", 64, "float16"),
+        ("pd", 128, "float16"), ("B0", 64, "float16"), ("Pm", 64, "float16"), ("P", 64, "float32"),
+        ("Sd", 64, "float32"), ("X", 512, "bfloat16"), ("M", 512, "bfloat16"), ("fw", 192, "float32"), ("gg", 192, "bfloat16"),
+        ("Wn", 272, "float32"), ("WW", 512, "float16"), ("hwf", 12, "float32"), ("yo", 64, "float32")):
     for _s in range(2):
         SCRATCH[_n + str(_s)] = ("sbuf", [128, _c], _d)
 for _n, _c, _d in (
@@ -27,11 +28,12 @@ for _n, _c, _d in (
         ("i2", 128, "float32"), ("pi", 64, "int32"), ("pf", 64, "float32"), ("IW", 128, "bfloat16"), ("w2", 2, "bfloat16"),
         ("I2", 256, "bfloat16"), ("Ih", 128, "float16"), ("If", 128, "float32"), ("HI", 128, "float16"), ("BD", 128, "bfloat16"),
         ("BDf", 128, "float32"), ("ZV", 144, "bfloat16"), ("ZA", 144, "bfloat16"), ("ZE", 144, "float16"), ("EXP", 1024, "bfloat16"),
-        ("d0h", 1024, "bfloat16"), ("d0l", 1024, "bfloat16"), ("d0k", 64, "float32"), ("NH", 256, "bfloat16"), ("d04", 256, "bfloat16"), ("KC", 128, "float16"),
-        ("OHW", 16, "bfloat16"), ("Sx", 768, "float16"), ("nS", 48, "float16"), ("GO", 1024, "float16"), ("MB", 512, "bfloat16"),
-        ("F1", 272, "float32"), ("F2", 272, "float32"), ("PERM", 128, "float16"), ("OUTP", 128, "float16"), ("SH", 256, "float16"),
-        ("cAB", 512, "bfloat16"), ("CC", 128, "bfloat16"), ("m384", 64, "float16"), ("cx", 8, "float32"), ("Sin", 160, "float16"),
-        ("zb", 16, "bfloat16"), ("IN", 128, "bfloat16"), ("di", 128, "int32"), ("df", 128, "float32")):
+        ("d0h", 1024, "bfloat16"), ("d0l", 1024, "bfloat16"), ("d0k", 64, "float32"), ("NH", 512, "bfloat16"), ("d04", 256, "bfloat16"),
+        ("KC", 128, "float16"), ("OHW", 16, "bfloat16"), ("Z1", 144, "float16"), ("m2k", 64, "float16"), ("nS", 48, "float16"),
+        ("GO", 1024, "float16"), ("MB", 260, "bfloat16"), ("F1", 272, "float32"), ("F2", 272, "float32"), ("PERM", 128, "float16"),
+        ("OUTP", 128, "float16"), ("SH", 384, "float16"), ("SR", 384, "float16"), ("BDh", 128, "float16"), ("cAB", 640, "bfloat16"),
+        ("CC", 128, "bfloat16"), ("m384", 64, "float16"), ("cx", 8, "float32"), ("Sin", 160, "float16"), ("zb", 16, "bfloat16"),
+        ("di", 256, "int32"), ("df", 128, "float32")):
     SCRATCH[_n] = ("sbuf", [128, _c], _d)
 BANKS = tuple(n + s for s in "01" for n in ("bE", "bF", "bK", "bM"))
 for _n in BANKS:
@@ -40,8 +42,9 @@ SEMAPHORES = (["cV", "cS", "cT", "cG", "ldn", "tb0", "tb1", "st", "lsem"] + ["ld
               + ["%s%d" % (n, i) for n in ("z", "y") for i in range(2 * N)] + ["n%d" % i for i in range(N)]
               + ["hx%d" % j for j in HELP])
 WIDE = {"float32": 4, "int32": 4, "float16": 2, "bfloat16": 2, "uint16": 2}
+CYCLE, WAKE = 0.87, 195.0
 LEAD = 2000.0
-WAKE, SAME, NEAR = 125.0, 125.0, 0.3
+NEAR = 0.2
 
 
 def b(n, lo=0, hi=128, st=1, p=(0, 128)):
@@ -64,8 +67,7 @@ def order(ops):
                     if o["sum"] is not None and ops[j]["sum"] is o["sum"]:
                         continue
                     if (bank and (not same or o["e"] == "T")) or ((w or w2) and over(r, r2)):
-                        wait = not (same and o["e"] == "T")
-                        dep[j] = dep.get(j, False) or wait
+                        dep[j] = dep.get(j, False) or not (same and o["e"] == "T")
         dep.pop(i, None)
         o["dep"] = dep
         for refs, w in ((o["ins"], False), (o["outs"], True)):
@@ -74,11 +76,12 @@ def order(ops):
                 if w and r[3] == 1 and r[4] == (0, 128) and r[0] not in BANKS:
                     old = [a for a in old if not (r[1] <= a[2][1] and a[2][2] <= r[2])]
                 acc[r[0]] = old[-48:] + [(i, w, r)] if r[0] in BANKS else old + [(i, w, r)]
-    left = [o["ns"] + o["urge"] for o in ops]
+    ns = [o["ns"] * (CYCLE if o["e"] in "VS" else 1.0) for o in ops]
+    left = [ns[i] + o["urge"] for i, o in enumerate(ops)]
     users = [[] for _ in ops]
     for i in range(len(ops) - 1, -1, -1):
         for j, wait in ops[i]["dep"].items():
-            left[j] = max(left[j], left[i] + ((ops[j]["ns"] + (SAME if ops[j]["e"] == ops[i]["e"] else WAKE)) if wait else 0.0))
+            left[j] = max(left[j], left[i] + (ns[j] + WAKE if wait else 0.0))
             users[j].append(i)
     left = [v + o["lead"] for v, o in zip(left, ops)]
     miss = [len(o["dep"]) for o in ops]
@@ -87,16 +90,16 @@ def order(ops):
     while ready:
         est = {i: max(t, free.get(ops[i]["e"], 0.0)) for i, t in ready.items()}
         first = min(est, key=lambda i: (est[i], -left[i]))
-        i = max((j for j in est if ops[j]["e"] == ops[first]["e"] and est[j] <= est[first] + NEAR * ops[first]["ns"]), key=lambda j: (left[j], -j))
+        i = max((j for j in est if ops[j]["e"] == ops[first]["e"] and est[j] <= est[first] + NEAR * ns[first]), key=lambda j: (left[j], -j))
         start[i] = est[i]
         if ops[i]["e"] != "D":
-            free[ops[i]["e"]] = est[i] + ops[i]["ns"]
+            free[ops[i]["e"]] = est[i] + ns[i]
         del ready[i]
         out.append(i)
         for u in users[i]:
             miss[u] -= 1
             if not miss[u]:
-                ready[u] = max(start[j] + ((ops[j]["ns"] + (SAME if ops[j]["e"] == ops[u]["e"] else WAKE)) if wait else 0.0) for j, wait in ops[u]["dep"].items())
+                ready[u] = max(start[j] + (ns[j] + WAKE if wait else 0.0) for j, wait in ops[u]["dep"].items())
     for i in out:
         ops[i]["at"] = start[i]
     return [ops[i] for i in out]
@@ -249,7 +252,7 @@ def rank_program(g, core, T, topo, report=None):
         for i, d in enumerate(others):
             j = 3 * s + i
             (g.scalar if i == 1 else g.sync).dma_start(T.zs[:, 512 * j:512 * j + 512], rows("tz", 2 * d + s)).then_inc(T.sem["ld%d" % j], 16)
-            landed("ld%d" % j, 16, [b("zs", 512 * j, 512 * j + 512)], 2200.0 + 200 * j)
+            landed("ld%d" % j, 16, [b("zs", 512 * j, 512 * j + 512)], 2200.0 + 200 * SENDS.index(j))
         if s == 0:
             g.scalar.dma_start(T.tpi[:, 0:128], T.tp[:, :]).then_inc(T.sem.ldn, 16)
             g.sync.dma_start(T.tpi[:, 128:256], T.sd[:, :]).then_inc(T.sem.ldn, 16)
@@ -267,7 +270,7 @@ def rank_program(g, core, T, topo, report=None):
                 if s == 0 or h == 0:
                     e.wait_ge(T.sem["z%d" % j], eo)
                 e.dma_start(tab(s, q, h), T.zl[:, 512 * j:512 * j + 512]).then_inc(T.sem["tb%d" % s], 16)
-        landed("tb%d" % s, 128, [b("tab%d" % s, 0, W)], 13000.0 + 6000 * s)
+        landed("tb%d" % s, 128, [b("tab%d" % s, 0, W)], 15000.0 + 2000 * s)
     n0 = rank * NAT
     ts(b("t1", 0, 256), b("tpi", 0, 256), 0, O.is_lt, EMPTY + 2049.0, O.mult)
     ts(b("t2", 0, 256), b("tpi", 0, 256), -2048, O.add)
@@ -283,7 +286,7 @@ def rank_program(g, core, T, topo, report=None):
             x = 2 * rank + j // 3
             send([T.cores[others[j % 3]]], b("zs", 512 * j, 512 * j + 512), b("zl", 512 * x, 512 * x + 512), "z%d" % x, 1e6 - 1e3 * k)
     for q in others:
-        landed("n%d" % q, eo, [b("nat", q * NAT, q * NAT + 260)], 9000.0)
+        landed("n%d" % q, eo, [b("nat", q * NAT, q * NAT + 260)], 10000.0)
 
     iota(b("pi", 0, 8), [[0, 8]], 0, 1)
     iota(b("ji"), [[1, 128]], 0, 0)
@@ -291,7 +294,8 @@ def rank_program(g, core, T, topo, report=None):
     iota(b("i2"), [[32, 4], [0, 2], [1, 16]], 0, 0)
     for h in range(2):
         iota(b("IW", 64 * h, 64 * h + 64), [[4, 4], [1, 4], [16, 4]], 128 + 64 * h, 0)
-    iota(b("KC"), [[1024, 2], [1, 64]], 0, 0)
+    iota(b("KC", 0, 64), [[1, 64]], 0, 0)
+    iota(b("KC", 64, 128), [[256, 4], [1, 16]], 1024, 0)
     iota(b("pi", 16, 24), [[1, 8]], 0, 0)
     cp(b("jf"), b("ji"))
     c1 = lambda n, i: b(n, i, i + 1)
@@ -304,49 +308,42 @@ def rank_program(g, core, T, topo, report=None):
     Ib = b("I2")
     cp(b("Ih"), Ib); cp(b("If"), Ib)
     ts(b("HI"), Ib, 0.5, O.mult)
-    ts(b("IN"), Ib, -1.0, O.mult)
     ts(b("BD"), b("j16"), pu, O.is_equal)
     cp(b("BDf"), b("BD"))
     for nm, c in (("ZV", 4096.0), ("ZA", -8192.0)):
         fill(b(nm, 0, 144), 0.0)
         ts(b(nm, 16, 144, 16), b("BD", 0, 128, 16), c, O.mult)
     ts(b("ZE", 0, 144), b("ZV", 0, 144), -0.5, O.mult)
+    ts(b("Z1", 0, 144), b("ZV", 0, 144), 1.0 / 4096, O.mult)
     for m in range(16):
         cp(b("EXP", m, 1024, 16), b("I2", 0, 64))
     for nm, w, st, lo, hi in (("d0h", 1024, 4, 255.0, 0.0), ("d0l", 1024, 4, 0.0, 255.0), ("d0k", 64, 16, -1.0e9, 1.0e9)):
         fill(b(nm, 0, w), lo)
         fill(b(nm, 0, w, st), hi)
-    ts(b("d04", 0, 256), b("d0l", 0, 256), 8.0, O.mult, -1.0, O.add)
-    fill(b("NH", 0, 256), -0.5); fill(b("zb", 0, 16), 0.0)
+    ts(b("d04", 0, 256), b("d0l", 0, 256), 16.0, O.mult, 16.0, O.add)
+    fill(b("NH", 0, 256), -0.5); fill(b("NH", 256, 512), 2048.0); fill(b("zb", 0, 16), 0.0)
     ts(b("m384", 0, 64), b("NH", 0, 64), 768.0, O.mult)
-    fill(b("CC"), -2048.0); fill(b("CC", 64, 128), EMPTY)
+    ts(b("m2k", 0, 64), b("NH", 0, 64), 4096.0, O.mult)
+    fill(b("CC"), -2048.0); fill(b("CC", 64, 128), 0.0)
     fill(b("F1", 0, 272), EMPTY); fill(b("F1", 128, 256), -4096.0)
-    fill(b("F2", 0, 272), -4096.0); fill(b("F2", 128, 256), EMPTY)
+    fill(b("F2", 0, 272), 0.0); fill(b("F2", 128, 256), 1.0)
     ts(c1("pf", 8), pl, 64.0, O.mult)
-    ts(b("KC"), b("KC"), c1("pf", 8), O.add)
+    ts(b("KC", 0, 64), b("KC", 0, 64), c1("pf", 8), O.add)
+    ts(c1("pf", 9), pl, 16.0, O.mult)
+    ts(b("KC", 64, 128), b("KC", 64, 128), c1("pf", 9), O.add)
     ts(b("OHW", 0, 16), b("jf", 0, 16), pl, O.is_equal)
     for u in range(8):
         ts(b("GO", 128 * u, 128 * u + 128), b("BD"), 0.0, O.mult, c1("BD", 16 * u), O.add)
-    tcol, rq, xr = b("pi", 16, 22), b("pi", 24, 30), b("pi", 32, 38)
+    tcol, rq = b("pi", 16, 22), b("pi", 24, 30)
     ts(b("pi", 40, 46), tcol, -1.0, O.mult, pq, O.add)
     ts(b("pi", 40, 46), b("pi", 40, 46), 7, O.add)
     ts(rq, b("pi", 40, 46), 3, O.bitwise_and)
-    ts(b("pi", 48, 54), tcol, 1, O.add, pq, O.add)
-    ts(xr, b("pi", 48, 54), 3, O.bitwise_and)
-    ts(b("pi", 56, 62), tcol, 2, O.arith_shift_right)
-    ts(b("pf", 16, 22), xr, 4.0, O.mult)
-    tt(b("pf", 16, 22), b("pf", 16, 22), b("pi", 56, 62), O.add)
-    ts(b("pf", 16, 22), b("pf", 16, 22), pl, O.is_equal)
-    ts(b("cx", 0, 6), b("pf", 16, 22), EMPTY + 4096.0, O.mult, -4096.0, O.add)
-    ts(c1("pf", 9), ph, 4.0, O.mult, pq, O.add)
-    ts(b("pf", 24, 30), rq, 8.0, O.mult, c1("pf", 9), O.add)
-    ts(b("pf", 24, 30), b("pf", 24, 30), 4.0, O.mult)
-    tt(b("pf", 24, 30), b("pf", 24, 30), b("pi", 56, 62), O.add)
     ts(c1("pf", 10), ph, 4.0, O.mult)
     ts(b("pf", 32, 38), rq, c1("pf", 10), O.add)
     for t in range(RO):
-        ts(b("Sx", 128 * t, 128 * t + 128), b("jf"), c1("pf", 24 + t), O.is_equal)
+        ts(c1("pf", 16 + t), pl, float(XL[t]), O.is_equal)
         ts(b("nS", 8 * t, 8 * t + 8), b("jf", 0, 8), c1("pf", 32 + t), O.is_equal)
+    ts(b("cx", 0, 6), b("pf", 16, 22), EMPTY + 4096.0, O.mult, -4096.0, O.add)
     tt(c1("pi", 1), c1("pi", 11), c1("pi", 13), O.subtract)
     ts(c1("pi", 2), c1("pi", 1), 3, O.bitwise_and)
     ts(c1("pf", 11), c1("pi", 2), 4.0, O.mult, pr, O.add)
@@ -355,20 +352,25 @@ def rank_program(g, core, T, topo, report=None):
     ts(b("PERM"), b("jf"), c1("pf", 12), O.is_equal)
     ts(c1("pf", 13), pq, 16.0, O.mult, pl, O.add)
     ts(c1("pf", 14), c1("pf", 13), 2.0, O.mult, ph, O.add)
-    ts(b("OUTP"), b("jf"), c1("pf", 14), O.is_equal)
+    ts(b("SR", 256, 384), b("jf"), c1("pf", 14), O.is_equal)
     ts(c1("pf", 13), pq, 32.0, O.mult, pl, O.add)
     ts(c1("pf", 15), ph, -1.0, O.mult, 1.0, O.add)
-    ts(b("SH", 0, 128), b("i2"), c1("pf", 13), O.is_equal, c1("pf", 15), O.mult)
-    ts(b("SH", 128, 256), b("i2"), c1("pf", 13), O.is_equal, ph, O.mult)
+    ts(b("SR", 0, 128), b("i2"), c1("pf", 13), O.is_equal, c1("pf", 15), O.mult)
+    ts(b("SR", 128, 256), b("i2"), c1("pf", 13), O.is_equal, ph, O.mult)
     mm(b("bM1", 0, 1), b("IW"), b("I2", 0, 128, 128))
     mm(b("bM1", 1, 2), b("IW"), b("I2", 0, 128, 128))
     cp(b("w2", 0, 2), b("bM1", 0, 2))
     fill(b("MB", 256, 260), 0.0)
     for r in range(2):
         ts(b("MB", 128 * r, 128 * r + 128), b("IW"), c1("w2", 0), O.is_le, 16384.0, O.mult)
-    ts(b("t1"), Ib, 15.0, O.mult)
-    tt(b("t2"), b("t1"), b("BD"), O.subtract)
-    for i, (a, c) in enumerate((("t2", 8192.0), ("t2", -8192.0), ("BD", 8192.0), ("BD", -8192.0))):
+    mm(b("bE1", 0, 384), b("PERM"), b("SR", 0, 384))
+    mm(b("bE1", 384, 512), b("PERM"), b("Ih"))
+    cp(b("SH", 0, 256), b("bE1", 0, 256)); cp(b("OUTP"), b("bE1", 256, 384)); cp(b("SH", 256, 384), b("bE1", 384, 512))
+    cp(b("BDh"), b("BD"))
+    mm(b("bF1"), b("BDh"), b("PERM"))
+    ts(b("t1"), b("PERM"), 16.0, O.mult)
+    tt(b("t2"), b("t1"), b("bF1"), O.subtract)
+    for i, (a, c) in enumerate((("t2", 8192.0), ("t2", -8192.0), ("bF1", 8192.0), ("bF1", -8192.0), ("PERM", 8192.0))):
         ts(b("cAB", 128 * i, 128 * i + 128), b(a), c, O.mult)
     fill(b("t1", 128, 256), 0.0)
     cp(b("Sin", 0, 128), b("t1", 128, 256))
@@ -376,8 +378,8 @@ def rank_program(g, core, T, topo, report=None):
     def stream(s):
         grp = 2 * rank + s
         B = lambda n, *a, **k: b(n + str(s), *a, **k)
-        P, Pm, Sd, E2, B0, Pw = B("P", 0, 64), B("Pm", 0, 64), B("Sd", 0, 64), B("E2", 0, 64), B("BP", 0, 64), B("BP", 64, 128)
-        table = B("tab", 0, W + 16)
+        P, Pm, Sd, E2, B0, Pw = B("P", 0, 64), B("Pm", 0, 64), B("Sd", 0, 64), B("E2", 3, 256, 4), B("B0", 0, 64), B("fw", 128, 192)
+        table, KT = B("tab", 0, W + 16), B("hwf", 8, 12)
         z0 = 48 * s
         cp(b("Sin", z0 + 16, z0 + 32), b("Ih", 16 * grp, 16 * grp + 16))
         for h in range(2):
@@ -393,73 +395,82 @@ def rank_program(g, core, T, topo, report=None):
                 for h in range(2):
                     o = r * NAT + 128 * w + 64 * h
                     mm(B("bM", 64 * w, 64 * w + 64, p=pr32), b("Sin", z0 + 16 - 16 * h, z0 + 48 - 16 * h), b("nat", o, o + 64), h == 0, h == 1)
-        cp(P, B("bM", 0, 64)); cp(Sd, B("bM", 64, 128)); cp(B("hwf", 0, 4), B("bM", 128, 132))
+        cp(B0, B("bM", 0, 64)); cp(Sd, B("bM", 64, 128)); cp(B("hwf", 0, 4), B("bM", 128, 132))
+        mm(B("bM", 0, 64), b("PERM"), B0)
+        cp(P, B("bM", 0, 64))
         for i in range(2):
             ts(B("WW", 128 * i, 128 * i + 128), b("BD"), B("hwf", i, i + 1), O.mult, 0.5, O.mult)
+            mm(B("bK", 256 + i, 257 + i), B("WW", 128 * i, 128 * i + 128), c1("m2k", 0))
+        cp(B("hwf", 6, 8), B("bK", 256, 258))
         ts(b("df"), b("If"), B("hwf", 2, 3), O.mult)
         mm(B("bK"), b("BDf"), b("df"))
-        ts(b("di"), B("bK"), B("hwf", 1, 2), O.mult, 2048.0, O.add)
-        ts(b("di"), b("di"), 4095, O.bitwise_and)
-        ts(B("WW", 256, 384), b("di"), -2048.0, O.add, 0.5, O.mult)
-        ts(B("hwf", 5, 6), B("hwf", 3, 4), 2047.5, O.add, 4096.0, O.mult)
+        ts(b("di"), B("bK"), B("hwf", 1, 2), O.mult, 2080.0, O.add)
+        ts(b("di", 128, 256), b("di"), 63, O.bitwise_and)
+        ts(B("WW", 256, 384), b("di", 128, 256), -32.0, O.add, 0.5, O.mult)
+        ts(b("di", 128, 256), b("di"), 6, O.arith_shift_right, 63, O.bitwise_and)
+        ts(B("WW", 384, 512), b("di", 128, 256), -32.0, O.add, 32.0, O.mult)
+        ts(B("hwf", 5, 6), B("hwf", 3, 4), 2047.5 + 16384.0, O.add, 4096.0, O.mult)
         ts(B("hwf", 5, 6), B("hwf", 5, 6), c1("pf", 8), O.add)
-        ts(B("KT", 0, 4), b("jf", 0, 4), 16.0, O.mult, B("hwf", 5, 6), O.add)
+        ts(KT, b("jf", 0, 4), 16.0, O.mult, B("hwf", 5, 6), O.add)
+        lane = lambda z, l: b(z, 16 - l, 144 - l)
+        block, comb = (lambda n, d, o=0: B(n, o + 16 * d, o + 16 * d + 16)), (lambda n, d, o=0: B(n, o + d, o + 64, 4))
 
         def hashes(p):
             iw = lambda i, n=1: B("iw", 64 * i, 64 * (i + n))
             hn = B("hn", 64 * p, 64 * p + 64)
-
-            def sums(i):
-                w = B("WW", 128 * i, 128 * i + 128)
-                if p == 0:
-                    mm(B("bM", 192 + 64 * i, 256 + 64 * i), w, E2)
-                for c in range(4 * p):
-                    mm(B("bM", 192 + 64 * i + c, 256 + 64 * i, 4), w, B("C2", 16 * c, 16 * c + 16))
-            sums(0); sums(1)
-            cp(iw(0, 2), B("bM", 192, 320))
-            sums(2)
+            C, w = B("C2", 0, 64) if p else E2, lambda i: B("WW", 128 * i, 128 * i + 128)
+            for i in range(2):
+                mm(B("bM", 192 + 64 * i, 256 + 64 * i), w(i), C)
+            for i in range(2):
+                ts(iw(i), B("bM", 192 + 64 * i, 256 + 64 * i), B("hwf", 6 + i, 7 + i), O.add)
+            for j, (i, v) in enumerate(((3, b("m2k", 0, 64)), (2, b("m2k", 0, 64)), (3, C), (2, C))):
+                mm(B("bM", 320, 384), w(i), v, j == 0, j == 3)
             ts(iw(2, 2), iw(0, 2), 4095, O.bitwise_and)
             tt(iw(4), iw(2), iw(3), O.mult)
             ts(iw(5), iw(4), 5, O.arith_shift_right)
             tt(iw(6), iw(5), B("bM", 320, 384), O.add)
             ts(hn, iw(6), 4095, O.bitwise_and)
-            cp(B("hl", 0, 64), hn)
+            if p == 0:
+                cp(B("hl", 0, 64), hn)
+            for c in range(4 * p):
+                cp(comb("hl", c), block("hn", c, 64))
 
         def search(p):
             key = B("bK", 64 * p, 64 * p + 64)
             mm(key, b("Ih"), b("KC", 64 * p, 64 * p + 64), True, False)
-            sums, fillp = [0], {"bE": 0, "bF": 0}
-            for lo, hi, e, how, bank in CAND:
-                e16 = B(bank, fillp[bank], fillp[bank] + hi - lo)
+            sums, fillp, e16s = [0], {"bE": 0, "bF": 0}, []
+            for lo, hi, e, bank in CAND:
+                e16s.append(B(bank, fillp[bank], fillp[bank] + hi - lo))
                 fillp[bank] += hi - lo
-                lanes = range(lo // 64, hi // 64)
-                if p == 0 or how == "abs":
-                    mm(e16, B("ET", p=(0, 64)), b("EXP", lo, hi, p=(0, 64)), True, how == "min")
+                if p == 0:
+                    mm(e16s[-1], B("ET", p=(0, 64)), b("EXP", lo, hi, p=(0, 64)))
+            for (lo, hi, e, bank), e16 in zip(CAND, e16s):
                 gather(e, B("V", lo, hi), table, B("hl", lo // 16, hi // 16))
-                if how == "abs":
-                    mm(e16, b("IN"), B("V", lo, hi), False, True)
-                    act(B("A", lo, hi), e16, F.Abs)
-                else:
-                    for l in lanes:
-                        mm(key, b("ZV", 16 - l, 144 - l), B("V", 64 * l, 64 * l + 64), False, sums)
-                    tt(B("A", lo, hi), B("V", lo, hi), e16, O.min)
-                for l in lanes:
-                    mm(key, b("ZV" if how == "abs" else "ZA", 16 - l, 144 - l), B("A", 64 * l, 64 * l + 64), False, sums)
+                for l in range(lo // 64, hi // 64):
+                    mm(key, lane("ZV", l), B("V", 64 * l, 64 * l + 64), False, sums)
+                tt(B("A", lo, hi), B("V", lo, hi), e16, O.min)
+                for l in range(lo // 64, hi // 64):
+                    mm(key, lane("ZA", l), B("A", 64 * l, 64 * l + 64), False, sums)
             scan(B("km", 0, 64), b("d0k", 0, 64), key, O.max, O.min)
 
         for t in range(RO):
             for d in range(4):
-                mm(B("bM", 16 * d, 16 * d + 16), b("PERM"), B("P", d, 64, 4))
-            ts(B("offs", 0, 64), B("bM", 0, 64), 2048.0, O.min, 2048.0, O.add)
+                ts(block("offs", d), comb("P", d), 2048.0, O.min, 2048.0, O.add)
             mm(B("bF", 0, 256), Ib, b("NH", 0, 256), True, False)
+            mm(B("bF", 0, 256), Ib, b("NH", 256, 512), False, False)
             ts(Pm, P, EMPTY, O.min, c1("cx", t), O.max)
-            for h in range(2):
-                mm(B("bK", 384 + 64 * h, 448 + 64 * h), b("SH", 128 * h, 128 * h + 128), Pm)
-            act(B("Wn", 128, 256), B("bK", 384, 512), F.Copy)
+            for h in range(3):
+                mm(B("bK", 256 + 64 * h, 320 + 64 * h), b("SH", 128 * h, 128 * h + 128), Pm)
+            act(B("Wn", 128, 256), B("bK", 256, 384), F.Copy)
+            act(B("Pr", 0, 64), B("bK", 384, 448), F.Identity, scale=-1.0, bias=4096.0)
+            ts(B("Pr", 64, 128), B("bK", 384, 448), 3000.0, O.min)
             for lo, hi, e in MID:
                 gather(e, B("Gv", lo, hi), table, B("offs", lo // 16, hi // 16))
-            for lo, hi, e in MID:
-                act(B("Ga", lo, hi), B("Gv", lo, hi), F.Abs)
+            for lo, hi, again in ABS:
+                if again:
+                    act(B("Ga", lo, hi), B("offs", lo // 16, hi // 16), F.Abs, win=table)
+                else:
+                    act(B("Ga", lo, hi), B("Gv", lo, hi), F.Abs)
             part = lambda nm, d: B(nm, 4 * ((d - 1 - t) % N) + 3, 1024, 16)
             shift = lambda d: b("I2", 128 - 32 * d, 256 - 32 * d)
             for lo, hi, e in MID:
@@ -470,35 +481,29 @@ def rank_program(g, core, T, topo, report=None):
             for d in range(1, 4):
                 tt(B("HL", 64 * d - 64, 64 * d), B("bE", 64 * d, 64 * d + 64), m, O.max)
                 m = B("HL", 64 * d - 64, 64 * d)
-            for lo, hi, e in MID:
+            for lo, hi, again in ABS:
                 scan(B("Lo", lo, hi), b("d0l", lo, hi), B("Ga", lo, hi), O.max, O.min)
             sums = [0]
             for d in range(4):
                 mm(B("bF", d, 256, 4), Ib, m, False, sums)
                 mm(B("bF", d, 256, 4), shift(d), part("Lo", d), False, sums)
-            scan(B("fw", 0, 256), b("d04", 0, 256), B("bF", 0, 256), O.max, O.min)
-            ts(E2, B("fw", 3, 256, 4), M1, O.add, -M1, O.add)
+            scan(B("E2", 0, 256), b("d04", 0, 256), B("bF", 0, 256), O.max, O.min)
             mm(B("bK", 256, 384, p=(0, 64)), E2, b("HI"))
-            act(B("ET", p=(0, 64)), B("bK", 256, 384, p=(0, 64)), F.Copy)
+            act(B("ET", p=(0, 64)), B("bK", 256, 384, p=(0, 64)), F.Identity, bias=-1024.0)
             hashes(0)
             for c in range(4):
-                mm(B("bM", 16 * c, 16 * c + 16), b("HI"), B("E2", c, 64, 4))
-            act(B("Epl", 0, 64), B("bM", 0, 64), F.Identity, bias=-0.5)
+                mm(block("bM", c), b("HI"), B("E2", 4 * c + 3, 256, 16))
+            act(B("Epl", 0, 64), B("bM", 0, 64), F.Identity, bias=1023.5)
             search(0)
             th = B("bK", 128, 132)
-            lanes = [l for lo, hi, e, how, bank in CAND if how == "min" for l in range(lo // 64, hi // 64)]
-            if lanes:
-                mm(th, b("If"), B("KT", 0, 4), True, False)
-            else:
-                th = B("KT", 0, 4)
-            for l in lanes:
-                mm(th, b("ZE", 16 - l, 144 - l), B("E2", 4 * l, 4 * l + 4), False, l == lanes[-1])
+            mm(th, b("If"), KT, True, False)
+            for l in range(16):
+                mm(th, lane("ZE", l), B("E2", 16 * l + 3, 16 * l + 16, 4), False, l == 15)
             k4 = B("km", 15, 64, 16)
             cp(B("ki", 0, 4), k4)
             ts(B("ki", 4, 8), B("ki", 0, 4), 1023, O.bitwise_and)
             cp(B("lz", 0, 4), B("ki", 4, 8))
-            tt(B("cs", 0, 64), B("lz", 0, 4), B("Epl", 0, 64), O.add, win=B("V", 0, 1024))
-            ts(B("C2", 0, 64), B("cs", 0, 64), M1, O.add, -M1, O.add)
+            tt(B("C2", 0, 64), B("lz", 0, 4), B("Epl", 0, 64), O.add, win=B("V", 0, 1024))
             tt(B("km", 64, 68), k4, th, O.min)
             hashes(1)
             search(1)
@@ -508,9 +513,9 @@ def rank_program(g, core, T, topo, report=None):
             ts(B("ki", 4, 8), B("ki", 0, 4), 4, O.arith_shift_right, 255, O.bitwise_and)
             ts(B("ki", 8, 12), B("ki", 0, 4), 15, O.bitwise_and)
             cp(B("lz", 4, 12), B("ki", 4, 12))
-            ts(B("hs", 0, 64), B("lz", 4, 8), -2048.0, O.add, win=B("hn", 0, 192))
+            ts(B("pd", 64, 128), B("lz", 4, 8), -2048.0, O.add, win=B("hn", 0, 192))
             pd = B("pd", 0, 64)
-            tt(pd, B("lz", 8, 12), B("hs", 0, 64), O.mult, win=b("OHW", 0, 16))
+            tt(pd, B("lz", 8, 12), B("pd", 64, 128), O.mult, win=b("OHW", 0, 16))
             for i, bank in enumerate(("bE", "bF")):
                 for h in range(2):
                     n = 8 * t + 4 * h + 2 * i
@@ -518,10 +523,10 @@ def rank_program(g, core, T, topo, report=None):
                 for j in range(4):
                     u = 2 * ((2 * i + j // 2 + 1 + t) % N) + j % 2
                     mm(B(bank, 64 * j, 64 * j + 64), b("GO", 128 * u, 128 * u + 128), pd, False, j == 3)
-            sx = b("Sx", 128 * t, 128 * t + 128)
+            sx = lane("Z1", XL[t])
             mm(B("bM", 384, 448), sx, b("m384", 0, 64), True, False)
-            for d in range(4):
-                mm(B("bM", 384 + 16 * d, 400 + 16 * d), sx, B("pd", d, 64, 4), False, d == 3)
+            for c in range(4):
+                mm(block("bM", c, 384), sx, comb("pd", c), False, c == 3)
             ys = [B("bM" if r // 2 else "bK", 448 + r, 449 + r) for r in range(N)]
             for r in range(N):
                 xr_, bank = B("X", 128 * r, 128 * r + 128), "bF" if r // 2 else "bE"
@@ -529,33 +534,38 @@ def rank_program(g, core, T, topo, report=None):
                 mm(ys[r], xr_, c1("w2", 0))
             for c in range(4):
                 mm(B("bE", c, c + 1), B("X", c, 512, 4), c1("w2", 0))
-            mm(B("bF"), Ib, b("CC"), True, False)
             for r in range(N):
                 ts(B("M", 128 * r, 128 * r + 128), b("IW"), ys[r], O.is_equal)
             mm(B("bK", 200, 208), Ib, b("zb", 0, 8), True, False)
             for c in range(4):
                 mm(B("bK", 200 + c, 201 + c), B("X", c, 512, 4), c1("w2", 0), False, False)
             tt(Pw, Pm, B("bM", 384, 448), O.add)
-            ts(B("lz", 12, 16), B("bE", 0, 4), 256.0, O.min)
+            LB, L, LA = B("lz", 12, 16), B("lz", 16, 20), B("lz", 20, 24)
+            ts(LB, B("bE", 0, 4), 256.0, O.min)
             for c in range(4):
                 mm(B("bK", 200 + c, 208, 4), B("M", c, 512, 4), b("w2", 0, 2), False, c == 3)
-            fw = lambda i, n=1: B("fw", 64 * i, 64 * (i + n))
-            tt(fw(0), B("lz", 12, 16), Sd, O.max, win=b("F1", 0, 272))
-            tt(fw(1), B("lz", 12, 16), Pw, O.max, win=b("F2", 0, 272))
-            tt(fw(2), fw(0), fw(1), O.min)
+            win = B("Wn", 0, 272)
+            tt(B("fw", 0, 64), LB, Sd, O.max, win=b("F1", 0, 272))
+            act(B("gg", 128, 192), LB, F.Copy, win=b("F2", 0, 272))
             ts(B("lz", 16, 24), B("bK", 200, 208), 256.0, O.min)
-            tt(fw(3), B("lz", 16, 20), Pm, O.subtract, win=B("Wn", 0, 272))
-            ts(B("gg", 0, 64), fw(3), M13, O.add, M13, O.is_equal)
-            ts(B("gg", 64, 128), fw(3), 0.0, O.is_equal)
-            tt(B0, B("lz", 20, 24), fw(2), O.min, win=B("Wn", 0, 272))
-            for i in range(4):
-                mm(B("bF", 64 - 64 * (i // 2), 128 - 64 * (i // 2)), b("cAB", 128 * i, 128 * i + 128), B("gg", 64 * (i % 2), 64 * (i % 2) + 64), False, i == 3)
-            tt(fw(4, 2), B("BP"), B("bF"), O.max)
-            tt(P, fw(4), fw(5), O.min)
-        mm(B("bM", 0, 64), b("OUTP"), P)
-        ts(B("fw", 0, 64), B("bM", 0, 64), 2048.0, O.is_ge, -4097.0, O.mult)
-        ts(B("fw", 64, 128), B("bM", 0, 64), 2048.0, O.min, 2048.0, O.add)
-        tt(B("yo", 0, 64), B("fw", 0, 64), B("fw", 64, 128), O.add)
+            tt(B("gg", 0, 64), L, B("Pr", 0, 64), O.is_lt, win=win)
+            tt(B("gg", 64, 128), L, B("Pr", 64, 128), O.is_equal, win=win)
+            tt(B0, LA, B("fw", 0, 64), O.min, win=win)
+            mm(B("bF", 0, 64), Ib, b("CC", 0, 64), True, False)
+            mm(B("bM", 0, 64), Ib, b("CC", 64, 128), True, False)
+            for bank, terms in (("bF", (("cAB", 4, "gg", 128), ("cAB", 0, "gg", 0), ("cAB", 1, "gg", 64))),
+                                ("bM", (("cAB", 2, "gg", 0), ("cAB", 3, "gg", 64), ("PERM", 0, "B0", 0)))):
+                sums = [0]
+                for w, i, v, o in terms:
+                    mm(B(bank, 0, 64), b(w, 128 * i, 128 * i + 128), B(v, o, o + 64), False, sums)
+            tt(B("fw", 64, 128), Pw, B("bF", 0, 64), O.max)
+            tt(P, B("fw", 64, 128), B("bM", 0, 64), O.min)
+        ts(Pm, P, 2047.0, O.min)
+        ts(B("pd", 0, 64), P, 2048.0, O.is_ge, -4096.0, O.mult)
+        mm(B("bK", 0, 64), Ib, b("NH", 256, 320), True, False)
+        for v in ("Pm", "pd"):
+            mm(B("bK", 0, 64), b("OUTP"), B(v, 0, 64), False, v == "pd")
+        cp(B("yo", 0, 64), B("bK", 0, 64))
         send([T.cores[d] for d in others], B("yo", 0, 64), b("yl", 64 * grp, 64 * grp + 64), "y%d" % grp, 0.0)
         mine = (32 * rank, 32 * rank + 32)
         op("Y", [], [B("yo", 0, 64)], lambda: g.sync.dma_start(rows("yp", grp), ap(B("yo", 0, 64, p=mine))).then_inc(T.sem.st, 16), 50.0, raw=True)

@@ -5,11 +5,18 @@ N, W, RO = 4, 4096, 6
 EMPTY = 6144.0
 XL = [4 * ((-1 - t) % N) + t // 4 for t in range(RO)]
 NAT = 272
-MID = ((0, 256, "V"), (256, 640, "S"), (640, 1024, "S"))
-ABS = ((0, 256, False), (256, 640, False), (640, 1024, False))
-CAND = ((0, 192, "V", "bE"), (192, 512, "S", "bF"), (512, 832, "S", "bE"), (832, 1024, "S", "bF"))
-SENDS = (1, 0, 2, None, 5, 3, 4)
-HELP = (1, 2, 5)
+MID = ((0, 320, "V"), (320, 704, "S"), (704, 1024, "S"))
+ABS = ((0, 320, False), (320, 704, False), (704, 1024, False))
+CAND = ((0, 192, "V", "bE"), (192, 512, "S", "bF"), (512, 768, "S", "bE"), (768, 960, "S", "bF"), (960, 1024, "S", "bE"))
+SUB = 0
+TURN = "V"
+COLS, M12 = True, 1.5 * 2.0 ** 35
+LAST = 120
+FUSE, RELU = 0, False
+PACK = True
+SENDS = ((1, 2), "tp", (0,), (5,), (3, 4), "sd")
+TABLES = (14000.0, 15500.0, 10000.0, 17000.0)
+HELP = ((1, 2), (5,))
 
 SCRATCH = {}
 for _n, _c, _d in (
@@ -17,34 +24,36 @@ for _n, _c, _d in (
         ("Lo", 1024, "bfloat16"), ("HL", 192, "bfloat16"), ("E2", 256, "float16"), ("ET", 128, "bfloat16"), ("Epl", 64, "float32"),
         ("iw", 448, "int32"), ("hn", 192, "int32"), ("hl", 64, "uint16"), ("V", 1024, "bfloat16"), ("A", 1024, "bfloat16"),
         ("km", 72, "float32"), ("ki", 16, "int32"), ("lz", 24, "uint16"), ("Pr", 128, "float32"), ("C2", 64, "float16"),
-        ("pd", 128, "float16"), ("B0", 64, "float16"), ("Pm", 64, "float16"), ("P", 64, "float32"),
-        ("Sd", 64, "float32"), ("X", 512, "bfloat16"), ("M", 512, "bfloat16"), ("fw", 192, "float32"), ("gg", 192, "bfloat16"),
-        ("Wn", 272, "float32"), ("WW", 512, "float16"), ("hwf", 12, "float32"), ("yo", 64, "float32")):
+        ("pd", 128, "float16"), ("B0", 64, "float16"), ("Pm", 64, "float16"), ("P", 128, "float32"),
+        ("Sd", 192, "float32"), ("X", 512, "bfloat16"), ("M", 512, "bfloat16"), ("fw", 192, "float32"), ("gg", 192, "bfloat16"),
+        ("Wn", 272, "float32"), ("WW", 640, "float16"), ("hwf", 12, "float32"), ("yo", 64, "float32")):
     for _s in range(2):
         SCRATCH[_n + str(_s)] = ("sbuf", [128, _c], _d)
 for _n, _c, _d in (
-        ("zs", 6 * 512, "bfloat16"), ("zl", 8 * 512, "bfloat16"), ("tpi", 260, "int32"), ("nat", N * NAT, "float16"), ("yl", 512, "float32"),
+        ("tpi", 264, "int32"), ("nat", N * NAT, "float16"), ("yl", 512, "float32"),
         ("t1", 256, "float32"), ("t2", 256, "float32"), ("ji", 128, "int32"), ("jf", 128, "float32"), ("j16", 128, "float32"),
-        ("i2", 128, "float32"), ("pi", 64, "int32"), ("pf", 64, "float32"), ("IW", 128, "bfloat16"), ("w2", 2, "bfloat16"),
+        ("i2", 128, "float32"), ("pi", 64, "int32"), ("pf", 64, "float32"), ("IW", 384, "bfloat16"), ("w2", 2, "bfloat16"),
         ("I2", 256, "bfloat16"), ("Ih", 128, "float16"), ("If", 128, "float32"), ("HI", 128, "float16"), ("BD", 128, "bfloat16"),
         ("BDf", 128, "float32"), ("ZV", 144, "bfloat16"), ("ZA", 144, "bfloat16"), ("ZE", 144, "float16"), ("EXP", 1024, "bfloat16"),
         ("d0h", 1024, "bfloat16"), ("d0l", 1024, "bfloat16"), ("d0k", 64, "float32"), ("NH", 512, "bfloat16"), ("d04", 256, "bfloat16"),
-        ("KC", 128, "float16"), ("OHW", 16, "bfloat16"), ("Z1", 144, "float16"), ("m2k", 64, "float16"), ("nS", 48, "float16"),
-        ("GO", 1024, "float16"), ("MB", 260, "bfloat16"), ("F1", 272, "float32"), ("F2", 272, "float32"), ("PERM", 128, "float16"),
+        ("KC", 128, "float16"), ("OHW", 16, "bfloat16"), ("Z1", 144, "float16"), ("m2k", 128, "float16"), ("nS", 48, "float16"),
+        ("GO", 1024, "float16"), ("MB", 780, "bfloat16"), ("F1", 272, "float32"), ("F2", 272, "float32"), ("PERM", 128, "float16"),
         ("OUTP", 128, "float16"), ("SH", 384, "float16"), ("SR", 384, "float16"), ("BDh", 128, "float16"), ("cAB", 640, "bfloat16"),
-        ("CC", 128, "bfloat16"), ("m384", 64, "float16"), ("cx", 8, "float32"), ("Sin", 160, "float16"), ("zb", 16, "bfloat16"),
+        ("CC", 128, "bfloat16"), ("m384", 64, "float16"), ("cx", 8, "float32"), ("Sin", 160, "float16"), ("zb", 16, "bfloat16"), ("IN", 128, "bfloat16"),
         ("di", 256, "int32"), ("df", 128, "float32")):
     SCRATCH[_n] = ("sbuf", [128, _c], _d)
+SCRATCH["zs"] = ("dram", [6, 128, 512], "bfloat16")
+SCRATCH["zl"] = ("dram", [2 * N, 128, 512], "bfloat16")
 BANKS = tuple(n + s for s in "01" for n in ("bE", "bF", "bK", "bM"))
 for _n in BANKS:
     SCRATCH[_n] = ("psum", [128, 512], "float32")
-SEMAPHORES = (["cV", "cS", "cT", "cG", "ldn", "tb0", "tb1", "st", "lsem"] + ["ld%d" % i for i in range(6)]
-              + ["%s%d" % (n, i) for n in ("z", "y") for i in range(2 * N)] + ["n%d" % i for i in range(N)]
-              + ["hx%d" % j for j in HELP])
+SEMAPHORES = (["cV", "cS", "cT", "cG", "ldn", "lds", "tb0", "tb1", "st", "lsem"] + ["ld%d" % i for i in range(6)]
+              + ["%s%d" % (n, i) for n in ("z", "y") for i in range(2 * N)] + ["%s%d" % (n, i) for n in ("tp", "sd") for i in range(N)]
+              + ["hx%d" % j for js in HELP for j in js])
 WIDE = {"float32": 4, "int32": 4, "float16": 2, "bfloat16": 2, "uint16": 2}
-CYCLE, WAKE = 0.87, 195.0
-LEAD = 2000.0
-NEAR = 0.2
+CYCLE, WAKE = 0.9, 180.0
+LEAD = 1350.0
+NEAR = 0.25
 
 
 def b(n, lo=0, hi=128, st=1, p=(0, 128)):
@@ -67,7 +76,7 @@ def order(ops):
                     if o["sum"] is not None and ops[j]["sum"] is o["sum"]:
                         continue
                     if (bank and (not same or o["e"] == "T")) or ((w or w2) and over(r, r2)):
-                        dep[j] = dep.get(j, False) or not (same and o["e"] == "T")
+                        dep[j] = dep.get(j, False) or not (same and (o["e"] == "T" or o["raw"]))
         dep.pop(i, None)
         o["dep"] = dep
         for refs, w in ((o["ins"], False), (o["outs"], True)):
@@ -100,9 +109,46 @@ def order(ops):
             miss[u] -= 1
             if not miss[u]:
                 ready[u] = max(start[j] + (ns[j] + WAKE if wait else 0.0) for j, wait in ops[u]["dep"].items())
-    for i in out:
-        ops[i]["at"] = start[i]
-    return [ops[i] for i in out]
+    fore = [[(j, ns[j] + WAKE if wait else 1.0) for j, wait in o["dep"].items()] for o in ops]
+    back = [[(u, ns[u] + WAKE if ops[u]["dep"][j] else 1.0 - ns[j] + ns[u]) for u in users[j]] for j in range(len(ops))]
+    late = pack(ops, ns, back, [-start[i] - ns[i] for i in range(len(ops))])
+    urge = [o["urge"] for o in ops]
+    for i in range(len(ops) - 1, -1, -1):
+        for j in ops[i]["dep"]:
+            urge[j] = max(urge[j], urge[i])
+    if PACK:
+        start = pack(ops, ns, fore, [-late[i] - ns[i] - urge[i] for i in range(len(ops))])
+    for i, o in enumerate(ops):
+        o["at"] = start[i]
+    return sorted(ops, key=lambda o: o["at"]) if PACK else [ops[i] for i in out]
+
+
+def pack(ops, ns, before, rank):
+    after = [[] for _ in ops]
+    for i, js in enumerate(before):
+        for j, _ in js:
+            after[j].append(i)
+    miss = [len(js) for js in before]
+    ready = {i for i in range(len(ops)) if not miss[i]}
+    busy, start = {}, [0.0] * len(ops)
+    while ready:
+        i = min(ready, key=lambda j: (rank[j], j))
+        ready.remove(i)
+        t = max([start[j] + lag for j, lag in before[i]], default=0.0)
+        if ops[i]["e"] != "D":
+            a = busy.setdefault(ops[i]["e"], [])
+            k = len(a)
+            while k and a[k - 1][1] > t:
+                k -= 1
+            while k < len(a) and a[k][0] < t + ns[i] - 1e-6:
+                t = max(t, a[k][1]); k += 1
+            a.insert(k, (t, t + ns[i]))
+        start[i] = t
+        for u in after[i]:
+            miss[u] -= 1
+            if not miss[u]:
+                ready.add(u)
+    return start
 
 
 def issue(g, T, ops):
@@ -126,7 +172,7 @@ def issue(g, T, ops):
             continue
         needs = {}
         for j, wait in o["dep"].items():
-            if wait:
+            if wait and o["all"][j]["done"]:
                 s, n = o["all"][j]["done"]
                 needs[s] = max(needs.get(s, 0), n)
         need(e, needs)
@@ -140,19 +186,34 @@ def issue(g, T, ops):
     need("Y", {"c" + e: cnt[e] for e in "VSTG"})
 
 
+def piece(T, name, j):
+    return T[name][j] if SCRATCH[name][0] == "dram" else T[name][:, j, :]
+
+
+def share(engines, i, n):
+    if n == 3:
+        return share(engines, 0, 2) if i == 0 else share(engines, i + 1, 4)
+    return engines[i * len(engines) // n:(i + 1) * len(engines) // n]
+
+
+def transfer(T, topo, cores, engines, sem, src, dst):
+    return RemoteDMATransfer(dst_ids=[DstId(rid=topo.addr(c)[0], pnc=topo.addr(c)[1]) for c in cores], dma_engine_mask=sum(1 << e for e in engines),
+                             remote_sem=T.sem[sem], srcs=[src], dsts=[dst for _ in cores])
+
+
 def on_chip_only(topo, core, near, far):
     return [e for e in topo.engines(core, near) if e not in topo.engines(core, far)]
 
 
 def helper_program(g, core, T, topo, r):
     others = [T.cores[(r + i) % N] for i in range(1, N)]
-    for j in HELP:
-        c, x = others[j % 3], 2 * r + j // 3
-        g.wait_ge(T.sem["hx%d" % j], len(on_chip_only(topo, T.cores[r], core, c)))
-        t = RemoteDMATransfer(dst_ids=[DstId(rid=topo.addr(c)[0], pnc=topo.addr(c)[1])], dma_engine_mask=topo.mask(core, c), remote_sem=T.sem["z%d" % x],
-                              srcs=[T.zs[:, 512 * j:512 * j + 512]], dsts=[T.zl[:, 512 * x:512 * x + 512]])
-        g.remote_dma_fused([t], local_sem=T.sem.lsem)
-    g.wait_ge(T.sem.lsem, len(HELP) * len(topo.engines(core, others[0])))
+    engines = topo.engines(core, others[0])
+    for js in HELP:
+        for i, j in enumerate(js):
+            g.wait_ge(T.sem["hx%d" % j], len(share(on_chip_only(topo, T.cores[r], core, others[0]), i, len(js))))
+        g.remote_dma_fused([transfer(T, topo, [others[j % 3]], share(engines, i, len(js)), "z%d" % (2 * r + j // 3), piece(T, "zs", j),
+                                     piece(T, "zl", 2 * r + j // 3)) for i, j in enumerate(js)], local_sem=T.sem.lsem)
+    g.wait_ge(T.sem.lsem, len(HELP) * len(engines))
 
 
 def rank_program(g, core, T, topo, report=None):
@@ -166,6 +227,8 @@ def rank_program(g, core, T, topo, report=None):
     ops = []
 
     def ap(r):
+        if r[0] in ("zs", "zl"):
+            return piece(T, r[0], r[1])
         return T[r[0]][r[4][0]:r[4][1], r[1]:r[2]:r[3]] if r[3] > 1 else T[r[0]][r[4][0]:r[4][1], r[1]:r[2]]
 
     def size(r):
@@ -178,7 +241,7 @@ def rank_program(g, core, T, topo, report=None):
         ops.append({"e": e, "outs": outs, "ins": ins, "call": call, "ns": ns, "raw": raw, "urge": urge, "done": done, "all": ops, "lead": 0.0, "sum": None})
 
     def landed(sem, n, refs, at):
-        op("D", refs, [], None, at, done=(sem, n))
+        op("D", refs, [], None, at, done=(sem, n), urge=2e6)
 
     def src(a, win):
         return ap(win).indirect(ap(a)) if win else ap(a)
@@ -232,11 +295,12 @@ def rank_program(g, core, T, topo, report=None):
 
     local = [0]
 
-    def send(cs, a, dst, sem, urge, engines=None):
-        engines = engines or topo.engines(core, cs[0])
-        t = RemoteDMATransfer(dst_ids=[DstId(rid=topo.addr(c)[0], pnc=topo.addr(c)[1]) for c in cs], dma_engine_mask=sum(1 << e for e in engines),
-                              remote_sem=T.sem[sem], srcs=[ap(a)], dsts=[ap(dst) for _ in cs])
-        op("G", [], [a], lambda: g.remote_dma_fused([t], local_sem=T.sem.lsem), 500.0, raw=True, urge=urge)
+    def send(ts_, urge, engines=None):
+        engines = engines or topo.engines(core, ts_[0][0][0])
+        call = [transfer(T, topo, cs, share(engines, i, len(ts_)), sem, ap(a), ap(dst)) for i, (cs, a, dst, sem) in enumerate(ts_)]
+        op("G", [], [t[1] for t in ts_], lambda: g.remote_dma_fused(call, local_sem=T.sem.lsem), 500.0, raw=True, urge=urge)
+        if urge:
+            ops[-1]["outs"] = [b("calls")]
         local[0] += len(engines)
 
     others = [(rank + i) % N for i in range(1, N)]
@@ -248,55 +312,65 @@ def rank_program(g, core, T, topo, report=None):
 
     def tab(s, q, h):
         return T["tab%d" % s][32 * q + 16 * h:32 * q + 16 * h + 16, 0:W]
-    for s in range(2):
-        for i, d in enumerate(others):
-            j = 3 * s + i
-            (g.scalar if i == 1 else g.sync).dma_start(T.zs[:, 512 * j:512 * j + 512], rows("tz", 2 * d + s)).then_inc(T.sem["ld%d" % j], 16)
-            landed("ld%d" % j, 16, [b("zs", 512 * j, 512 * j + 512)], 2200.0 + 200 * SENDS.index(j))
-        if s == 0:
-            g.scalar.dma_start(T.tpi[:, 0:128], T.tp[:, :]).then_inc(T.sem.ldn, 16)
-            g.sync.dma_start(T.tpi[:, 128:256], T.sd[:, :]).then_inc(T.sem.ldn, 16)
-            g.scalar.dma_start(T.tpi[:, 256:259], T.hw[:, :]).then_inc(T.sem.ldn, 16)
-            g.scalar.dma_start(T.tpi[:, 259:260], T.th[:, :]).then_inc(T.sem.ldn, 16)
-            landed("ldn", 64, [b("tpi", 0, 260)], 2800.0)
+    k = 0
+    for js in SENDS:
+        if js == "tp":
+            g.sync.dma_start(T.tpi[:, 0:128], T.tp[:, :]).then_inc(T.sem.ldn, 16)
+            g.scalar.dma_start(T.tpi[:, 128:131], T.hw[:, :]).then_inc(T.sem.ldn, 16)
+            g.scalar.dma_start(T.tpi[:, 131:132], T.th[:, :]).then_inc(T.sem.ldn, 16)
+            landed("ldn", 48, [b("tpi", 0, 132)], 1900.0)
+        elif js == "sd":
+            g.sync.dma_start(T.tpi[:, 136:264], T.sd[:, :]).then_inc(T.sem.lds, 16)
+            landed("lds", 16, [b("tpi", 136, 264)], 4000.0)
+        for j in js if isinstance(js, tuple) else ():
+            k += 1
+            (g.sync if k % 2 else g.scalar).dma_start(piece(T, "zs", j), rows("tz", 2 * others[j % 3] + j // 3)).then_inc(T.sem["ld%d" % j], 16)
+            landed("ld%d" % j, 16, [b("zs", j, j + 1)], 2000.0)
+    count = {j: len(share(range(eo), i, len(js))) for js in SENDS if isinstance(js, tuple) for i, j in enumerate(js)}
     for s in range(2):
         for h in range(2):
             (g.scalar if h else g.sync).dma_start(tab(s, rank, h), rows("tz", 2 * rank + s)).then_inc(T.sem["tb%d" % s], 16)
+    op("D", [b("later")], [], None, 7500.0, raw=True)
     for s in range(2):
         for q in others[::-1]:
             j = 2 * q + s
-            for h in range(2):
-                e = g.scalar if (s == 0 and h) else g.sync
-                if s == 0 or h == 0:
-                    e.wait_ge(T.sem["z%d" % j], eo)
-                e.dma_start(tab(s, q, h), T.zl[:, 512 * j:512 * j + 512]).then_inc(T.sem["tb%d" % s], 16)
-        landed("tb%d" % s, 128, [b("tab%d" % s, 0, W)], 15000.0 + 2000 * s)
+
+            def lay(e, h, s=s, q=q, j=j):
+                e.wait_ge(T.sem["z%d" % j], count[3 * s + (rank - q - 1) % N])
+                e.dma_start(tab(s, q, h), piece(T, "zl", j)).then_inc(T.sem["tb%d" % s], 16)
+            lay(g.sync, 0)
+            if s:
+                lay(g.sync, 1)
+            else:
+                op("S", [b("lay")], [b("later")], lambda lay=lay: lay(g.scalar, 1), 64.0, raw=True, urge=1e5)
+        landed("tb%d" % s, 128, [b("tab%d" % s, 0, W)], TABLES[s])
     n0 = rank * NAT
-    ts(b("t1", 0, 256), b("tpi", 0, 256), 0, O.is_lt, EMPTY + 2049.0, O.mult)
-    ts(b("t2", 0, 256), b("tpi", 0, 256), -2048, O.add)
-    tt(b("nat", n0, n0 + 256), b("t1", 0, 256), b("t2", 0, 256), O.add)
-    cp(b("nat", n0 + 256, n0 + 259), b("tpi", 256, 259))
-    ts(b("nat", n0 + 259, n0 + 260), b("tpi", 259, 260), -2048, O.add)
-    for k, j in enumerate(SENDS):
-        if j is None:
-            send([T.cores[d] for d in others], b("nat", n0, n0 + 260), b("nat", n0, n0 + 260), "n%d" % rank, 1e6 - 1e3 * k)
-        elif j in HELP:
-            send([helpers[rank]], b("zs", 512 * j, 512 * j + 512), b("zs", 512 * j, 512 * j + 512), "hx%d" % j, 1e6 - 1e3 * k, spare)
+    for o, bank in ((0, "bK0"), (136, "bK1")):
+        ts(b("t1", (o > 0) * 128, 128 + (o > 0) * 128), b("tpi", o, o + 128), 0, O.is_lt, EMPTY + 2049.0, O.mult)
+        ts(b(bank), b("tpi", o, o + 128), -2048, O.add)
+        tt(b("nat", n0 + o, n0 + o + 128), b("t1", (o > 0) * 128, 128 + (o > 0) * 128), b(bank), O.add)
+    ts(b("nat", n0 + 128, n0 + 132), b("tpi", 128, 132), 4095.0, O.min, -2047.0, O.add)
+    for k, js in enumerate(SENDS):
+        if isinstance(js, str):
+            lo, hi = (0, 132) if js == "tp" else (136, 264)
+            send([([T.cores[d] for d in others], b("nat", n0 + lo, n0 + hi), b("nat", n0 + lo, n0 + hi), js + str(rank))], 1e6 - 1e4 * k)
+        elif js in HELP:
+            send([([helpers[rank]], b("zs", j, j + 1), b("zs", j, j + 1), "hx%d" % j) for j in js], 1e6 - 1e4 * k, spare)
         else:
-            x = 2 * rank + j // 3
-            send([T.cores[others[j % 3]]], b("zs", 512 * j, 512 * j + 512), b("zl", 512 * x, 512 * x + 512), "z%d" % x, 1e6 - 1e3 * k)
+            send([([T.cores[others[j % 3]]], b("zs", j, j + 1), b("zl", 2 * rank + j // 3, 2 * rank + j // 3 + 1), "z%d" % (2 * rank + j // 3))
+                  for j in js], 1e6 - 1e4 * k)
     for q in others:
-        landed("n%d" % q, eo, [b("nat", q * NAT, q * NAT + 260)], 10000.0)
+        landed("tp%d" % q, eo, [b("nat", q * NAT, q * NAT + 132)], TABLES[2])
+        landed("sd%d" % q, eo, [b("nat", q * NAT + 136, q * NAT + 264)], TABLES[3])
 
     iota(b("pi", 0, 8), [[0, 8]], 0, 1)
     iota(b("ji"), [[1, 128]], 0, 0)
-    iota(b("j16"), [[1, 8], [0, 16]], 0, 0)
-    iota(b("i2"), [[32, 4], [0, 2], [1, 16]], 0, 0)
+    ts(b("di"), b("ji"), 4, O.arith_shift_right)
+    ts(b("di", 128, 256), b("ji"), 111, O.bitwise_and)
+    cp(b("j16"), b("di")); cp(b("i2"), b("di", 128, 256))
     for h in range(2):
         iota(b("IW", 64 * h, 64 * h + 64), [[4, 4], [1, 4], [16, 4]], 128 + 64 * h, 0)
-    iota(b("KC", 0, 64), [[1, 64]], 0, 0)
-    iota(b("KC", 64, 128), [[256, 4], [1, 16]], 1024, 0)
-    iota(b("pi", 16, 24), [[1, 8]], 0, 0)
+        iota(b("IW", 128 + 64 * h, 192 + 64 * h), [[1, 4], [16, 4], [4, 4]], 64 * h, 0)
     cp(b("jf"), b("ji"))
     c1 = lambda n, i: b(n, i, i + 1)
     for i, (sh, mask) in enumerate(((0, 127), (4, 7), (0, 15), (5, 3), (4, 1), (2, 3), (0, 3))):
@@ -306,35 +380,48 @@ def rank_program(g, core, T, topo, report=None):
     for i in range(2):
         ts(b("I2", 128 * i, 128 * i + 128), b("jf"), pp, O.is_equal)
     Ib = b("I2")
-    cp(b("Ih"), Ib); cp(b("If"), Ib)
+
+    def sfill(out, c):
+        n = size(out)
+        act(out, b("d0h", 0, n), F.Identity, scale=0.0, bias=c)
+    cp(b("Ih"), Ib); act(b("If"), Ib, F.Copy)
     ts(b("HI"), Ib, 0.5, O.mult)
     ts(b("BD"), b("j16"), pu, O.is_equal)
-    cp(b("BDf"), b("BD"))
-    for nm, c in (("ZV", 4096.0), ("ZA", -8192.0)):
-        fill(b(nm, 0, 144), 0.0)
-        ts(b(nm, 16, 144, 16), b("BD", 0, 128, 16), c, O.mult)
+    act(b("BDf"), b("BD"), F.Copy)
+    fill(b("d0h", 0, 512), 255.0); fill(b("d0h", 0, 512, 4), 0.0)
+    act(b("d0l", 0, 512), b("d0h", 0, 512), F.Identity, scale=-1.0, bias=255.0)
+    act(b("d04", 0, 256), b("d0h", 0, 256), F.Identity, scale=-16.0, bias=4096.0)
+    sfill(b("d0k", 0, 64), -1.0e9); sfill(b("d0k", 0, 64, 16), 1.0e9)
+    sfill(b("ZV", 0, 144), 0.0)
+    act(b("ZV", 16, 144, 16), b("BD", 0, 128, 16), F.Identity, scale=4096.0)
+    act(b("ZA", 0, 144), b("ZV", 0, 144), F.Identity, scale=-2.0)
     ts(b("ZE", 0, 144), b("ZV", 0, 144), -0.5, O.mult)
     ts(b("Z1", 0, 144), b("ZV", 0, 144), 1.0 / 4096, O.mult)
     for m in range(16):
-        cp(b("EXP", m, 1024, 16), b("I2", 0, 64))
-    for nm, w, st, lo, hi in (("d0h", 1024, 4, 255.0, 0.0), ("d0l", 1024, 4, 0.0, 255.0), ("d0k", 64, 16, -1.0e9, 1.0e9)):
-        fill(b(nm, 0, w), lo)
-        fill(b(nm, 0, w, st), hi)
-    ts(b("d04", 0, 256), b("d0l", 0, 256), 16.0, O.mult, 16.0, O.add)
-    fill(b("NH", 0, 256), -0.5); fill(b("NH", 256, 512), 2048.0); fill(b("zb", 0, 16), 0.0)
-    ts(b("m384", 0, 64), b("NH", 0, 64), 768.0, O.mult)
-    ts(b("m2k", 0, 64), b("NH", 0, 64), 4096.0, O.mult)
-    fill(b("CC"), -2048.0); fill(b("CC", 64, 128), 0.0)
-    fill(b("F1", 0, 272), EMPTY); fill(b("F1", 128, 256), -4096.0)
-    fill(b("F2", 0, 272), 0.0); fill(b("F2", 128, 256), 1.0)
+        act(b("EXP", m, 1024, 16), b("I2", 0, 64), F.Copy)
+    ts(c1("pf", 40), pl, 0.0, O.is_equal, -0.5, O.mult)
+    ts(b("NH", 0, 256), b("d0h", 0, 256), 0.0, O.mult, c1("pf", 40), O.add)
+    act(b("NH", 0, 256), b("NH", 0, 256), F.Identity, bias=128.0)
+    sfill(b("NH", 256, 512), 2048.0); sfill(b("zb", 0, 16), 0.0)
+    ts(b("m384", 0, 64), b("d0h", 0, 64), 0.0, O.mult, -384.0, O.add)
+    ts(b("m2k", 0, 64), b("d0h", 0, 64), 0.0, O.mult, -2048.0, O.add)
+    for c in range(4 if FUSE else 0):
+        ts(b("m2k", 64 + 16 * c, 80 + 16 * c), b("jf", 0, 16), float(FUSE // 64), O.is_lt, -2048.0, O.mult)
+    sfill(b("CC", 0, 128, 2), -2048.0); sfill(b("CC", 1, 128, 2), 0.0)
+    sfill(b("F1", 0, 272), EMPTY); sfill(b("F1", 128, 256), -4096.0)
+    sfill(b("F2", 0, 272), 0.0); sfill(b("F2", 128, 256), 1.0)
     ts(c1("pf", 8), pl, 64.0, O.mult)
-    ts(b("KC", 0, 64), b("KC", 0, 64), c1("pf", 8), O.add)
-    ts(c1("pf", 9), pl, 16.0, O.mult)
-    ts(b("KC", 64, 128), b("KC", 64, 128), c1("pf", 9), O.add)
+    ts(c1("pf", 7), pl, float((SUB + FUSE) // 64), O.is_ge, 2.0 ** 26, O.mult)
+    if SUB:
+        ts(b("IN"), Ib, -1.0, O.mult)
+    ts(b("KC", 0, 64), b("jf", 0, 64), c1("pf", 8), O.add)
+    ts(c1("pf", 9), pl, 16.0, O.mult, 1024.0, O.add)
+    ts(b("df", 0, 64), b("j16", 0, 64), 240.0, O.mult, c1("pf", 9), O.add)
+    tt(b("KC", 64, 128), b("df", 0, 64), b("jf", 0, 64), O.add)
     ts(b("OHW", 0, 16), b("jf", 0, 16), pl, O.is_equal)
     for u in range(8):
         ts(b("GO", 128 * u, 128 * u + 128), b("BD"), 0.0, O.mult, c1("BD", 16 * u), O.add)
-    tcol, rq = b("pi", 16, 22), b("pi", 24, 30)
+    tcol, rq = b("ji", 0, 6), b("pi", 24, 30)
     ts(b("pi", 40, 46), tcol, -1.0, O.mult, pq, O.add)
     ts(b("pi", 40, 46), b("pi", 40, 46), 7, O.add)
     ts(rq, b("pi", 40, 46), 3, O.bitwise_and)
@@ -360,9 +447,12 @@ def rank_program(g, core, T, topo, report=None):
     mm(b("bM1", 0, 1), b("IW"), b("I2", 0, 128, 128))
     mm(b("bM1", 1, 2), b("IW"), b("I2", 0, 128, 128))
     cp(b("w2", 0, 2), b("bM1", 0, 2))
-    fill(b("MB", 256, 260), 0.0)
-    for r in range(2):
-        ts(b("MB", 128 * r, 128 * r + 128), b("IW"), c1("w2", 0), O.is_le, 16384.0, O.mult)
+    cp(b("IW", 256, 384), b("jf"))
+    for i, o in enumerate((128, 256, 0)):
+        mm(b("bM1", 2 + i, 3 + i), b("IW", o, o + 128), b("I2", 0, 128, 128))
+        sfill(b("MB", 260 * i + 256, 260 * i + 260), 0.0)
+        for r in range(2):
+            ts(b("MB", 260 * i + 128 * r, 260 * i + 128 * r + 128), b("IW", o, o + 128), c1("bM1", 2 + i), O.is_le, 16384.0, O.mult)
     mm(b("bE1", 0, 384), b("PERM"), b("SR", 0, 384))
     mm(b("bE1", 384, 512), b("PERM"), b("Ih"))
     cp(b("SH", 0, 256), b("bE1", 0, 256)); cp(b("OUTP"), b("bE1", 256, 384)); cp(b("SH", 256, 384), b("bE1", 384, 512))
@@ -371,33 +461,48 @@ def rank_program(g, core, T, topo, report=None):
     ts(b("t1"), b("PERM"), 16.0, O.mult)
     tt(b("t2"), b("t1"), b("bF1"), O.subtract)
     for i, (a, c) in enumerate((("t2", 8192.0), ("t2", -8192.0), ("bF1", 8192.0), ("bF1", -8192.0), ("PERM", 8192.0))):
-        ts(b("cAB", 128 * i, 128 * i + 128), b(a), c, O.mult)
-    fill(b("t1", 128, 256), 0.0)
-    cp(b("Sin", 0, 128), b("t1", 128, 256))
+        if a == "PERM":
+            ts(b("cAB", 128 * i, 128 * i + 128), b(a), c, O.mult)
+        else:
+            act(b("cAB", 128 * i, 128 * i + 128), b(a), F.Identity, scale=c)
+    ts(b("Sin", 0, 96), b("d0h", 0, 96), 0.0, O.mult)
 
     def stream(s):
         grp = 2 * rank + s
         B = lambda n, *a, **k: b(n + str(s), *a, **k)
-        P, Pm, Sd, E2, B0, Pw = B("P", 0, 64), B("Pm", 0, 64), B("Sd", 0, 64), B("E2", 3, 256, 4), B("B0", 0, 64), B("fw", 128, 192)
+        P, Pm, E2, B0, Pw = B("P", 1, 128, 2), B("Pm", 0, 64), B("E2", 3, 256, 4), B("B0", 0, 64), B("fw", 65, 192, 2)
         table, KT = B("tab", 0, W + 16), B("hwf", 8, 12)
         z0 = 48 * s
         cp(b("Sin", z0 + 16, z0 + 32), b("Ih", 16 * grp, 16 * grp + 16))
         for h in range(2):
             cp(b("Sin", 96 + 32 * s + 16 * h, 112 + 32 * s + 16 * h), b("Ih", 16 * grp, 16 * grp + 16))
         fill(B("tab", W, W + 16), -256.0)
-        fill(B("Wn", 0, 272), EMPTY)
+        ops[-1]["ins"] = [b("lay")]
+        sfill(B("Wn", 0, 272), EMPTY)
         ts(B("hwf", 4, 5), ph, 256.0, O.mult, EMPTY + 2048.0, O.add)
         ts(B("hn", 128, 192), b("jf", 0, 64), 4.0, O.mult, B("hwf", 4, 5), O.add)
-        for r in range(N):
-            pr32 = (32 * r, 32 * r + 32)
-            mm(B("bM", 128, 132, p=pr32), b("Sin", 96 + 32 * s, 128 + 32 * s), b("nat", r * NAT + 256, r * NAT + 260))
-            for w in range(2):
+        block, comb = (lambda n, d, o=0: B(n, o + 16 * d, o + 16 * d + 16)), (lambda n, d, o=0: B(n, o + d, o + 64, 4))
+
+        def by_rows(o):
+            for r in range(N):
                 for h in range(2):
-                    o = r * NAT + 128 * w + 64 * h
-                    mm(B("bM", 64 * w, 64 * w + 64, p=pr32), b("Sin", z0 + 16 - 16 * h, z0 + 48 - 16 * h), b("nat", o, o + 64), h == 0, h == 1)
-        cp(B0, B("bM", 0, 64)); cp(Sd, B("bM", 64, 128)); cp(B("hwf", 0, 4), B("bM", 128, 132))
-        mm(B("bM", 0, 64), b("PERM"), B0)
-        cp(P, B("bM", 0, 64))
+                    c = r * NAT + o + 64 * h
+                    mm(B("bM", 0, 64, p=(32 * r, 32 * r + 32)), b("Sin", z0 + 16 - 16 * h, z0 + 48 - 16 * h), b("nat", c, c + 64), h == 0, h == 1)
+            cp(B0, B("bM", 0, 64))
+
+        def seeds():
+            by_rows(136)
+            for d in range(4):
+                mm(comb("bM", d), b("Ih"), block("B0", d))
+                mm(block("bM", d, 64), b("Ih"), comb("B0", d))
+            mm(B("bM", 128, 192), b("Ih"), B0)
+            act(B("Sd", 0, 192), B("bM", 0, 192), F.Copy)
+        by_rows(0)
+        mm(B("bE", 0, 64), b("PERM"), B0)
+        for r in range(N):
+            mm(B("bM", 128, 132, p=(32 * r, 32 * r + 32)), b("Sin", 96 + 32 * s, 128 + 32 * s), b("nat", r * NAT + 128, r * NAT + 132))
+        ts(B("hwf", 0, 4), B("bM", 128, 132), 2047.0, O.add)
+        fill(B("fw", 64, 192, 2), 1.0e9)
         for i in range(2):
             ts(B("WW", 128 * i, 128 * i + 128), b("BD"), B("hwf", i, i + 1), O.mult, 0.5, O.mult)
             mm(B("bK", 256 + i, 257 + i), B("WW", 128 * i, 128 * i + 128), c1("m2k", 0))
@@ -409,11 +514,10 @@ def rank_program(g, core, T, topo, report=None):
         ts(B("WW", 256, 384), b("di", 128, 256), -32.0, O.add, 0.5, O.mult)
         ts(b("di", 128, 256), b("di"), 6, O.arith_shift_right, 63, O.bitwise_and)
         ts(B("WW", 384, 512), b("di", 128, 256), -32.0, O.add, 32.0, O.mult)
-        ts(B("hwf", 5, 6), B("hwf", 3, 4), 2047.5 + 16384.0, O.add, 4096.0, O.mult)
-        ts(B("hwf", 5, 6), B("hwf", 5, 6), c1("pf", 8), O.add)
+        ts(B("hwf", 5, 6), B("hwf", 3, 4), -0.5, O.add, 4096.0, O.mult)
+        ts(B("hwf", 5, 6), B("hwf", 5, 6), c1("pf", 8), O.add, c1("pf", 7), O.add)
         ts(KT, b("jf", 0, 4), 16.0, O.mult, B("hwf", 5, 6), O.add)
         lane = lambda z, l: b(z, 16 - l, 144 - l)
-        block, comb = (lambda n, d, o=0: B(n, o + 16 * d, o + 16 * d + 16)), (lambda n, d, o=0: B(n, o + d, o + 64, 4))
 
         def hashes(p):
             iw = lambda i, n=1: B("iw", 64 * i, 64 * (i + n))
@@ -442,10 +546,32 @@ def rank_program(g, core, T, topo, report=None):
             for lo, hi, e, bank in CAND:
                 e16s.append(B(bank, fillp[bank], fillp[bank] + hi - lo))
                 fillp[bank] += hi - lo
-                if p == 0:
+                if p == 0 and lo >= SUB:
                     mm(e16s[-1], B("ET", p=(0, 64)), b("EXP", lo, hi, p=(0, 64)))
+            if SUB:
+                mm(B("bF", 0, SUB), B("ET", p=(0, 64)), b("EXP", 0, SUB, p=(0, 64)), True, False)
             for (lo, hi, e, bank), e16 in zip(CAND, e16s):
+                if hi <= FUSE:
+                    if p == 0:
+                        act(B("Ga", lo, hi), e16, F.Copy)
+                    tt(B("V", lo, hi), B("hl", lo // 16, hi // 16), B("Ga", lo, hi), O.subtract, win=table)
+                    if RELU:
+                        ts(B("A", lo, hi), B("V", lo, hi), 0.0, O.min)
+                        for l in range(lo // 64, hi // 64):
+                            mm(key, lane("ZV", l), B("V", 64 * l, 64 * l + 64), False, sums)
+                    else:
+                        act(B("A", lo, hi), B("V", lo, hi), F.Abs)
+                    for l in range(lo // 64, hi // 64):
+                        mm(key, lane("ZA" if RELU else "ZV", l), B("A", 64 * l, 64 * l + 64), False, sums)
+                    continue
                 gather(e, B("V", lo, hi), table, B("hl", lo // 16, hi // 16))
+                if lo < SUB:
+                    mm(e16, b("IN"), B("V", lo, hi), False, hi == SUB)
+                    if hi == SUB:
+                        act(B("A", 0, SUB), B("bF", 0, SUB), F.Abs)
+                        for l in range(SUB // 64):
+                            mm(key, lane("ZV", l), B("A", 64 * l, 64 * l + 64), False, sums)
+                    continue
                 for l in range(lo // 64, hi // 64):
                     mm(key, lane("ZV", l), B("V", 64 * l, 64 * l + 64), False, sums)
                 tt(B("A", lo, hi), B("V", lo, hi), e16, O.min)
@@ -454,13 +580,19 @@ def rank_program(g, core, T, topo, report=None):
             scan(B("km", 0, 64), b("d0k", 0, 64), key, O.max, O.min)
 
         for t in range(RO):
-            for d in range(4):
-                ts(block("offs", d), comb("P", d), 2048.0, O.min, 2048.0, O.add)
-            mm(B("bF", 0, 256), Ib, b("NH", 0, 256), True, False)
-            mm(B("bF", 0, 256), Ib, b("NH", 256, 512), False, False)
-            ts(Pm, P, EMPTY, O.min, c1("cx", t), O.max)
+            now = P if t else B("bE", 0, 64)
+            ts(B("offs", 0, 64), now, 2048.0, O.min, 2048.0, O.add)
+            mm(B("bF", 0, 256), b("BD"), b("NH", 0, 256), True, False)
+            if TURN == "V":
+                for d in range(4):
+                    ts(comb("Pm", d), B(now[0][:-1], now[1] + 16 * d * now[3], now[1] + (16 * d + 15) * now[3] + 1, now[3]), EMPTY, O.min, c1("cx", t), O.max)
+            else:
+                ts(Pm, now, EMPTY, O.min, c1("cx", t), O.max)
             for h in range(3):
-                mm(B("bK", 256 + 64 * h, 320 + 64 * h), b("SH", 128 * h, 128 * h + 128), Pm)
+                if TURN == "V":
+                    mm(B("bK", 256 + 64 * h, 320 + 64 * h), b("SH", 128 * h, 128 * h + 128), Pm)
+                for d in range(4 * (TURN == "T")):
+                    mm(comb("bK", d, 256 + 64 * h), b("SH", 128 * h, 128 * h + 128), block("Pm", d))
             act(B("Wn", 128, 256), B("bK", 256, 384), F.Copy)
             act(B("Pr", 0, 64), B("bK", 384, 448), F.Identity, scale=-1.0, bias=4096.0)
             ts(B("Pr", 64, 128), B("bK", 384, 448), 3000.0, O.min)
@@ -474,7 +606,7 @@ def rank_program(g, core, T, topo, report=None):
             part = lambda nm, d: B(nm, 4 * ((d - 1 - t) % N) + 3, 1024, 16)
             shift = lambda d: b("I2", 128 - 32 * d, 256 - 32 * d)
             for lo, hi, e in MID:
-                scan(B("Hi", lo, hi), b("d0h", lo, hi), B("Gv", lo, hi), O.min, O.max)
+                scan(B("Hi", lo, hi), b("d0h", 0, hi - lo), B("Gv", lo, hi), O.min, O.max)
             m = part("Hi", 0)
             for d in range(1, 4):
                 mm(B("bE", 64 * d, 64 * d + 64), shift(d), part("Hi", d))
@@ -482,7 +614,7 @@ def rank_program(g, core, T, topo, report=None):
                 tt(B("HL", 64 * d - 64, 64 * d), B("bE", 64 * d, 64 * d + 64), m, O.max)
                 m = B("HL", 64 * d - 64, 64 * d)
             for lo, hi, again in ABS:
-                scan(B("Lo", lo, hi), b("d0l", lo, hi), B("Ga", lo, hi), O.max, O.min)
+                scan(B("Lo", lo, hi), b("d0l", 0, hi - lo), B("Ga", lo, hi), O.max, O.min)
             sums = [0]
             for d in range(4):
                 mm(B("bF", d, 256, 4), Ib, m, False, sums)
@@ -491,24 +623,35 @@ def rank_program(g, core, T, topo, report=None):
             mm(B("bK", 256, 384, p=(0, 64)), E2, b("HI"))
             act(B("ET", p=(0, 64)), B("bK", 256, 384, p=(0, 64)), F.Identity, bias=-1024.0)
             hashes(0)
+            if FUSE:
+                mm(B("bM", 0, 64), b("HI"), b("m2k", 64, 128), True, False)
+                for c in range(4):
+                    mm(B("bM", 16 * c, 16 * c + FUSE // 64), b("HI"), B("E2", 4 * c + 3, FUSE // 4, 16), False, False)
             for c in range(4):
-                mm(block("bM", c), b("HI"), B("E2", 4 * c + 3, 256, 16))
+                mm(block("bM", c), b("HI"), B("E2", 4 * c + 3, 256, 16), not FUSE, c == 3 or not FUSE)
             act(B("Epl", 0, 64), B("bM", 0, 64), F.Identity, bias=1023.5)
             search(0)
             th = B("bK", 128, 132)
             mm(th, b("If"), KT, True, False)
-            for l in range(16):
+            for l in range((SUB + FUSE) // 64, 16):
                 mm(th, lane("ZE", l), B("E2", 16 * l + 3, 16 * l + 16, 4), False, l == 15)
             k4 = B("km", 15, 64, 16)
-            cp(B("ki", 0, 4), k4)
-            ts(B("ki", 4, 8), B("ki", 0, 4), 1023, O.bitwise_and)
-            cp(B("lz", 0, 4), B("ki", 4, 8))
+            if COLS:
+                ts(B("km", 68, 72), k4, M12, O.add, -M12, O.add)
+                for c in range(4):
+                    ts(B("lz", c, c + 1), B("km", 16 * c + 15, 16 * c + 16), B("km", 68 + c, 69 + c), O.subtract)
+            else:
+                cp(B("ki", 0, 4), k4)
+                ts(B("ki", 4, 8), B("ki", 0, 4), 1023, O.bitwise_and)
+                cp(B("lz", 0, 4), B("ki", 4, 8))
             tt(B("C2", 0, 64), B("lz", 0, 4), B("Epl", 0, 64), O.add, win=B("V", 0, 1024))
             tt(B("km", 64, 68), k4, th, O.min)
             hashes(1)
+            if t == 0:
+                seeds()
             search(1)
             for bank in ("bE", "bF"):
-                mm(B(bank, 0, 260), Ib, b("MB", 0, 260), True, False)
+                mm(B(bank, 0, 260), Ib, b("MB", 260 * (t % 3), 260 * (t % 3) + 260), True, False)
             tt(B("ki", 0, 4), k4, B("km", 64, 68), O.min)
             ts(B("ki", 4, 8), B("ki", 0, 4), 4, O.arith_shift_right, 255, O.bitwise_and)
             ts(B("ki", 8, 12), B("ki", 0, 4), 15, O.bitwise_and)
@@ -525,6 +668,10 @@ def rank_program(g, core, T, topo, report=None):
                     mm(B(bank, 64 * j, 64 * j + 64), b("GO", 128 * u, 128 * u + 128), pd, False, j == 3)
             sx = lane("Z1", XL[t])
             mm(B("bM", 384, 448), sx, b("m384", 0, 64), True, False)
+            if TURN == "V":
+                mm(B("bM", 384, 448), b("Ih"), Pm, False, False)
+            for c in range(4 * (TURN == "T")):
+                mm(comb("bM", c, 384), b("Ih"), block("Pm", c), False, False)
             for c in range(4):
                 mm(block("bM", c, 384), sx, comb("pd", c), False, c == 3)
             ys = [B("bM" if r // 2 else "bK", 448 + r, 449 + r) for r in range(N)]
@@ -539,34 +686,31 @@ def rank_program(g, core, T, topo, report=None):
             mm(B("bK", 200, 208), Ib, b("zb", 0, 8), True, False)
             for c in range(4):
                 mm(B("bK", 200 + c, 201 + c), B("X", c, 512, 4), c1("w2", 0), False, False)
-            tt(Pw, Pm, B("bM", 384, 448), O.add)
+            act(Pw, B("bM", 384, 448), F.Copy)
             LB, L, LA = B("lz", 12, 16), B("lz", 16, 20), B("lz", 20, 24)
             ts(LB, B("bE", 0, 4), 256.0, O.min)
             for c in range(4):
                 mm(B("bK", 200 + c, 208, 4), B("M", c, 512, 4), b("w2", 0, 2), False, c == 3)
             win = B("Wn", 0, 272)
-            tt(B("fw", 0, 64), LB, Sd, O.max, win=b("F1", 0, 272))
+            tt(B("fw", 0, 64), LB, B("Sd", 64 * (t % 3), 64 * (t % 3) + 64), O.max, win=b("F1", 0, 272))
             act(B("gg", 128, 192), LB, F.Copy, win=b("F2", 0, 272))
             ts(B("lz", 16, 24), B("bK", 200, 208), 256.0, O.min)
             tt(B("gg", 0, 64), L, B("Pr", 0, 64), O.is_lt, win=win)
             tt(B("gg", 64, 128), L, B("Pr", 64, 128), O.is_equal, win=win)
             tt(B0, LA, B("fw", 0, 64), O.min, win=win)
-            mm(B("bF", 0, 64), Ib, b("CC", 0, 64), True, False)
-            mm(B("bM", 0, 64), Ib, b("CC", 64, 128), True, False)
-            for bank, terms in (("bF", (("cAB", 4, "gg", 128), ("cAB", 0, "gg", 0), ("cAB", 1, "gg", 64))),
-                                ("bM", (("cAB", 2, "gg", 0), ("cAB", 3, "gg", 64), ("PERM", 0, "B0", 0)))):
-                sums = [0]
-                for w, i, v, o in terms:
-                    mm(B(bank, 0, 64), b(w, 128 * i, 128 * i + 128), B(v, o, o + 64), False, sums)
-            tt(B("fw", 64, 128), Pw, B("bF", 0, 64), O.max)
-            tt(P, B("fw", 64, 128), B("bM", 0, 64), O.min)
+            mm(B("bF"), Ib, b("CC"), True, False)
+            sums = [0]
+            for c, w, i, v, o in ((0, "cAB", 4, "gg", 128), (0, "cAB", 0, "gg", 0), (1, "cAB", 2, "gg", 0), (0, "cAB", 1, "gg", 64),
+                                  (1, "cAB", 3, "gg", 64), (1, "PERM", 0, "B0", 0)):
+                mm(B("bF", c, 128, 2), b(w, 128 * i, 128 * i + 128), B(v, o, o + 64), False, sums)
+            scan(B("P"), B("fw", 64, 192), B("bF"), O.max, O.min)
         ts(Pm, P, 2047.0, O.min)
         ts(B("pd", 0, 64), P, 2048.0, O.is_ge, -4096.0, O.mult)
         mm(B("bK", 0, 64), Ib, b("NH", 256, 320), True, False)
         for v in ("Pm", "pd"):
             mm(B("bK", 0, 64), b("OUTP"), B(v, 0, 64), False, v == "pd")
         cp(B("yo", 0, 64), B("bK", 0, 64))
-        send([T.cores[d] for d in others], B("yo", 0, 64), b("yl", 64 * grp, 64 * grp + 64), "y%d" % grp, 0.0)
+        send([([T.cores[d] for d in others], B("yo", 0, 64), b("yl", 64 * grp, 64 * grp + 64), "y%d" % grp)], 0.0)
         mine = (32 * rank, 32 * rank + 32)
         op("Y", [], [B("yo", 0, 64)], lambda: g.sync.dma_start(rows("yp", grp), ap(B("yo", 0, 64, p=mine))).then_inc(T.sem.st, 16), 50.0, raw=True)
         for i, q in enumerate(others[::-1]):
@@ -581,7 +725,7 @@ def rank_program(g, core, T, topo, report=None):
     for s in range(2):
         i0 = len(ops)
         stream(s)
-        for o in ops[i0:]:
+        for o in ops[i0:len(ops) - LAST]:
             o["lead"] = LEAD * (1 - s)
     ops2 = order(ops)
     if report is not None:

from concourse.bass import DstId, RemoteDMATransfer
from concourse.mybir import AluOpType as O, ActivationFunctionType as F

N, W, RO = 4, 4096, 6
EMPTY = 6144.0
XL = [4 * ((-1 - t) % N) + t // 4 for t in range(RO)]
NAT = 272
MID = ((0, 320, "V"), (320, 704, "S"), (704, 1024, "S"))
ABS = ((0, 320, False), (320, 704, False), (704, 1024, False))
CAND = ((0, 192, "V", "bE"), (192, 512, "S", "bF"), (512, 768, "S", "bE"), (768, 960, "S", "bF"), (960, 1024, "S", "bE"))
SUB = 0
TURN = "V"
COLS, M12 = True, 1.5 * 2.0 ** 35
LAST = 120
FUSE, RELU = 0, False
PACK = True
SENDS = ((1, 2), "tp", (0,), (5,), (3, 4), "sd")
TABLES = (14000.0, 15500.0, 10000.0, 17000.0)
HELP = ((1, 2), (5,))

SCRATCH = {}
for _n, _c, _d in (
        ("tab", W + 16, "bfloat16"), ("offs", 64, "uint16"), ("Gv", 1024, "bfloat16"), ("Ga", 1024, "bfloat16"), ("Hi", 1024, "bfloat16"),
        ("Lo", 1024, "bfloat16"), ("HL", 192, "bfloat16"), ("E2", 256, "float16"), ("ET", 128, "bfloat16"), ("Epl", 64, "float32"),
        ("iw", 448, "int32"), ("hn", 192, "int32"), ("hl", 64, "uint16"), ("V", 1024, "bfloat16"), ("A", 1024, "bfloat16"),
        ("km", 72, "float32"), ("ki", 16, "int32"), ("lz", 24, "uint16"), ("Pr", 128, "float32"), ("C2", 64, "float16"),
        ("pd", 128, "float16"), ("B0", 64, "float16"), ("Pm", 64, "float16"), ("P", 128, "float32"),
        ("Sd", 192, "float32"), ("X", 512, "bfloat16"), ("M", 512, "bfloat16"), ("fw", 192, "float32"), ("gg", 192, "bfloat16"),
        ("Wn", 272, "float32"), ("WW", 640, "float16"), ("hwf", 12, "float32"), ("yo", 64, "float32")):
    for _s in range(2):
        SCRATCH[_n + str(_s)] = ("sbuf", [128, _c], _d)
for _n, _c, _d in (
        ("tpi", 264, "int32"), ("nat", N * NAT, "float16"), ("yl", 512, "float32"),
        ("t1", 256, "float32"), ("t2", 256, "float32"), ("ji", 128, "int32"), ("jf", 128, "float32"), ("j16", 128, "float32"),
        ("i2", 128, "float32"), ("pi", 64, "int32"), ("pf", 64, "float32"), ("IW", 384, "bfloat16"), ("w2", 2, "bfloat16"),
        ("I2", 256, "bfloat16"), ("Ih", 128, "float16"), ("If", 128, "float32"), ("HI", 128, "float16"), ("BD", 128, "bfloat16"),
        ("BDf", 128, "float32"), ("ZV", 144, "bfloat16"), ("ZA", 144, "bfloat16"), ("ZE", 144, "float16"), ("EXP", 1024, "bfloat16"),
        ("d0h", 1024, "bfloat16"), ("d0l", 1024, "bfloat16"), ("d0k", 64, "float32"), ("NH", 512, "bfloat16"), ("d04", 256, "bfloat16"),
        ("KC", 128, "float16"), ("OHW", 16, "bfloat16"), ("Z1", 144, "float16"), ("m2k", 128, "float16"), ("nS", 48, "float16"),
        ("GO", 1024, "float16"), ("MB", 780, "bfloat16"), ("F1", 272, "float32"), ("F2", 272, "float32"), ("PERM", 128, "float16"),
        ("OUTP", 128, "float16"), ("SH", 384, "float16"), ("SR", 384, "float16"), ("BDh", 128, "float16"), ("cAB", 640, "bfloat16"),
        ("CC", 128, "bfloat16"), ("m384", 64, "float16"), ("cx", 8, "float32"), ("Sin", 160, "float16"), ("zb", 16, "bfloat16"), ("IN", 128, "bfloat16"),
        ("di", 256, "int32"), ("df", 128, "float32")):
    SCRATCH[_n] = ("sbuf", [128, _c], _d)
SCRATCH["zs"] = ("dram", [6, 128, 512], "bfloat16")
SCRATCH["zl"] = ("dram", [2 * N, 128, 512], "bfloat16")
BANKS = tuple(n + s for s in "01" for n in ("bE", "bF", "bK", "bM"))
for _n in BANKS:
    SCRATCH[_n] = ("psum", [128, 512], "float32")
SEMAPHORES = (["cV", "cS", "cT", "cG", "ldn", "lds", "tb0", "tb1", "st", "lsem"] + ["ld%d" % i for i in range(6)]
              + ["%s%d" % (n, i) for n in ("z", "y") for i in range(2 * N)] + ["%s%d" % (n, i) for n in ("tp", "sd") for i in range(N)]
              + ["hx%d" % j for js in HELP for j in js])
WIDE = {"float32": 4, "int32": 4, "float16": 2, "bfloat16": 2, "uint16": 2}
CYCLE, WAKE = 0.9, 180.0
LEAD = 1350.0
NEAR = 0.25


def b(n, lo=0, hi=128, st=1, p=(0, 128)):
    return (n, lo, hi, st, p)


def over(a, c):
    return a[1] < c[2] and c[1] < a[2] and not (a[3] == c[3] > 1 and (a[1] - c[1]) % a[3])


def order(ops):
    acc = {}
    for i, o in enumerate(ops):
        dep = {}
        for refs, w in ((o["ins"], False), (o["outs"], True)):
            for r in refs:
                bank = r[0] in BANKS
                for j, w2, r2 in acc.get(r[0], ()):
                    same = ops[j]["e"] == o["e"]
                    if o["sum"] is not None and ops[j]["sum"] is o["sum"]:
                        continue
                    if (bank and (not same or o["e"] == "T")) or ((w or w2) and over(r, r2)):
                        dep[j] = dep.get(j, False) or not (same and (o["e"] == "T" or o["raw"]))
        dep.pop(i, None)
        o["dep"] = dep
        for refs, w in ((o["ins"], False), (o["outs"], True)):
            for r in refs:
                old = acc.get(r[0], [])
                if w and r[3] == 1 and r[4] == (0, 128) and r[0] not in BANKS:
                    old = [a for a in old if not (r[1] <= a[2][1] and a[2][2] <= r[2])]
                acc[r[0]] = old[-48:] + [(i, w, r)] if r[0] in BANKS else old + [(i, w, r)]
    ns = [o["ns"] * (CYCLE if o["e"] in "VS" else 1.0) for o in ops]
    left = [ns[i] + o["urge"] for i, o in enumerate(ops)]
    users = [[] for _ in ops]
    for i in range(len(ops) - 1, -1, -1):
        for j, wait in ops[i]["dep"].items():
            left[j] = max(left[j], left[i] + (ns[j] + WAKE if wait else 0.0))
            users[j].append(i)
    left = [v + o["lead"] for v, o in zip(left, ops)]
    miss = [len(o["dep"]) for o in ops]
    ready = {i: 0.0 for i in range(len(ops)) if not miss[i]}
    free, out, start = {}, [], {}
    while ready:
        est = {i: max(t, free.get(ops[i]["e"], 0.0)) for i, t in ready.items()}
        first = min(est, key=lambda i: (est[i], -left[i]))
        i = max((j for j in est if ops[j]["e"] == ops[first]["e"] and est[j] <= est[first] + NEAR * ns[first]), key=lambda j: (left[j], -j))
        start[i] = est[i]
        if ops[i]["e"] != "D":
            free[ops[i]["e"]] = est[i] + ns[i]
        del ready[i]
        out.append(i)
        for u in users[i]:
            miss[u] -= 1
            if not miss[u]:
                ready[u] = max(start[j] + (ns[j] + WAKE if wait else 0.0) for j, wait in ops[u]["dep"].items())
    fore = [[(j, ns[j] + WAKE if wait else 1.0) for j, wait in o["dep"].items()] for o in ops]
    back = [[(u, ns[u] + WAKE if ops[u]["dep"][j] else 1.0 - ns[j] + ns[u]) for u in users[j]] for j in range(len(ops))]
    late = pack(ops, ns, back, [-start[i] - ns[i] for i in range(len(ops))])
    urge = [o["urge"] for o in ops]
    for i in range(len(ops) - 1, -1, -1):
        for j in ops[i]["dep"]:
            urge[j] = max(urge[j], urge[i])
    if PACK:
        start = pack(ops, ns, fore, [-late[i] - ns[i] - urge[i] for i in range(len(ops))])
    for i, o in enumerate(ops):
        o["at"] = start[i]
    return sorted(ops, key=lambda o: o["at"]) if PACK else [ops[i] for i in out]


def pack(ops, ns, before, rank):
    after = [[] for _ in ops]
    for i, js in enumerate(before):
        for j, _ in js:
            after[j].append(i)
    miss = [len(js) for js in before]
    ready = {i for i in range(len(ops)) if not miss[i]}
    busy, start = {}, [0.0] * len(ops)
    while ready:
        i = min(ready, key=lambda j: (rank[j], j))
        ready.remove(i)
        t = max([start[j] + lag for j, lag in before[i]], default=0.0)
        if ops[i]["e"] != "D":
            a = busy.setdefault(ops[i]["e"], [])
            k = len(a)
            while k and a[k - 1][1] > t:
                k -= 1
            while k < len(a) and a[k][0] < t + ns[i] - 1e-6:
                t = max(t, a[k][1]); k += 1
            a.insert(k, (t, t + ns[i]))
        start[i] = t
        for u in after[i]:
            miss[u] -= 1
            if not miss[u]:
                ready.add(u)
    return start


def issue(g, T, ops):
    eng = {"V": g.vector, "S": g.scalar, "T": g.tensor, "G": g, "Y": g.sync}
    cnt = {e: 0 for e in eng}; know = {e: {} for e in eng}; snap = {}

    def need(e, needs):
        while True:
            todo = {s: n for s, n in needs.items() if know[e].get(s, 0) < n}
            if not todo:
                return
            s = max(todo, key=lambda k: sum(1 for j in todo if j != k and snap.get((k, todo[k]), {}).get(j, 0) >= todo[j]))
            n = todo[s]
            eng[e].wait_ge(T.sem[s], n)
            for k, v in snap.get((s, n), {}).items():
                know[e][k] = max(know[e].get(k, 0), v)
            know[e][s] = max(know[e].get(s, 0), n)
    for o in ops:
        e = o["e"]
        if e == "D":
            continue
        needs = {}
        for j, wait in o["dep"].items():
            if wait and o["all"][j]["done"]:
                s, n = o["all"][j]["done"]
                needs[s] = max(needs.get(s, 0), n)
        need(e, needs)
        if o["raw"]:
            o["call"]()
        else:
            cnt[e] += 1
            o["done"] = ("c" + e, cnt[e])
            snap[o["done"]] = dict(know[e])
            o["call"]().then_inc(T.sem["c" + e], 1)
    need("Y", {"c" + e: cnt[e] for e in "VSTG"})


def piece(T, name, j):
    return T[name][j] if SCRATCH[name][0] == "dram" else T[name][:, j, :]


def share(engines, i, n):
    if n == 3:
        return share(engines, 0, 2) if i == 0 else share(engines, i + 1, 4)
    return engines[i * len(engines) // n:(i + 1) * len(engines) // n]


def transfer(T, topo, cores, engines, sem, src, dst):
    return RemoteDMATransfer(dst_ids=[DstId(rid=topo.addr(c)[0], pnc=topo.addr(c)[1]) for c in cores], dma_engine_mask=sum(1 << e for e in engines),
                             remote_sem=T.sem[sem], srcs=[src], dsts=[dst for _ in cores])


def on_chip_only(topo, core, near, far):
    return [e for e in topo.engines(core, near) if e not in topo.engines(core, far)]


def helper_program(g, core, T, topo, r):
    others = [T.cores[(r + i) % N] for i in range(1, N)]
    engines = topo.engines(core, others[0])
    for js in HELP:
        for i, j in enumerate(js):
            g.wait_ge(T.sem["hx%d" % j], len(share(on_chip_only(topo, T.cores[r], core, others[0]), i, len(js))))
        g.remote_dma_fused([transfer(T, topo, [others[j % 3]], share(engines, i, len(js)), "z%d" % (2 * r + j // 3), piece(T, "zs", j),
                                     piece(T, "zl", 2 * r + j // 3)) for i, j in enumerate(js)], local_sem=T.sem.lsem)
    g.wait_ge(T.sem.lsem, len(HELP) * len(engines))


def rank_program(g, core, T, topo, report=None):
    rank = T.rank_of(core)
    helpers = [[k for k in topo.cores_of(c) if topo.die(k) != topo.die(c) and all(topo.may_write(k, d) for d in T.cores if d != c)][0]
               for c in T.cores]
    if rank is None:
        if core in helpers:
            helper_program(g, core, T, topo, helpers.index(core))
        return
    ops = []

    def ap(r):
        if r[0] in ("zs", "zl"):
            return piece(T, r[0], r[1])
        return T[r[0]][r[4][0]:r[4][1], r[1]:r[2]:r[3]] if r[3] > 1 else T[r[0]][r[4][0]:r[4][1], r[1]:r[2]]

    def size(r):
        return len(range(r[1], r[2], r[3]))

    def narrow(*rs):
        return all(WIDE[SCRATCH[r[0]][2]] == 2 for r in rs)

    def op(e, outs, ins, call, ns, raw=False, urge=0.0, done=None):
        ops.append({"e": e, "outs": outs, "ins": ins, "call": call, "ns": ns, "raw": raw, "urge": urge, "done": done, "all": ops, "lead": 0.0, "sum": None})

    def landed(sem, n, refs, at):
        op("D", refs, [], None, at, done=(sem, n), urge=2e6)

    def src(a, win):
        return ap(win).indirect(ap(a)) if win else ap(a)

    def vns(out, a, win, k):
        return 50.0 + 1.56 * size(out) if win else max(64.0, k * size(out))

    def tt(out, a, c, o, win=None):
        k = 1.0 if a[0] in BANKS or c[0] in BANKS else 2.0
        op("V", [out], [a, c] + ([win] if win else []), lambda: g.vector.tensor_tensor(ap(out), src(a, win), ap(c), o), vns(out, a, win, k))

    def ts(out, a, s1, o1, s2=None, o2=None, win=None):
        ins = [a] + [s for s in (s1, s2, win) if isinstance(s, tuple)]
        f = lambda s: ap(s) if isinstance(s, tuple) else s
        rest = (o1,) if o2 is None else (o1, o2)
        op("V", [out], ins, lambda: g.vector.tensor_scalar(ap(out), src(a, win), f(s1), f(s2), *rest), vns(out, a, win, 0.5 if narrow(out, a) else 1.0))

    def cp(out, a, win=None):
        op("V", [out], [a] + ([win] if win else []), lambda: g.vector.tensor_copy(ap(out), src(a, win)), vns(out, a, win, 0.5 if narrow(out, a) else 1.0))

    def act(out, a, f, win=None, **k):
        op("S", [out], [a] + ([win] if win else []), lambda: g.scalar.activation(ap(out), src(a, win), f, **k),
           65.0 + 1.56 * size(out) if win else max(64.0, size(out)))

    def gather(e, out, win, off):
        if e == "S":
            act(out, off, F.Copy, win=win)
        else:
            cp(out, off, win=win)

    def scan(out, d0, d1, o0, o1):
        op("V", [out], [d0, d1], lambda: g.vector.tensor_tensor_scan(ap(out), ap(d0), ap(d1), 0.0, o0, o1),
           vns(out, d0, None, 0.5 if narrow(out, d0, d1) else 1.0))

    def fill(out, c):
        op("V", [out], [], lambda: g.vector.memset(ap(out), c), vns(out, out, None, 0.5 if narrow(out) else 1.0))

    def mm(out, l, r, start=True, stop=True):
        def call():
            if isinstance(stop, list):
                stop[0] -= 1
            return g.tensor.matmul(ap(out), ap(l), ap(r), start, stop[0] == 0 if isinstance(stop, list) else stop)
        op("T", [out], [l, r], call, 0.5 * max(min(64, size(l)), size(r)) * (1 if narrow(l) else 4) + 10.0)
        if isinstance(stop, list):
            stop[0] += 1
            ops[-1]["sum"] = stop

    def iota(out, pattern, base, cm):
        k = {} if SCRATCH[out[0]][2] == "int32" else {"allow_small_or_imprecise_dtypes": True}
        op("G", [out], [], lambda: g.iota(ap(out), pattern, base, cm, **k), 130.0 + 2 * size(out))

    local = [0]

    def send(ts_, urge, engines=None):
        engines = engines or topo.engines(core, ts_[0][0][0])
        call = [transfer(T, topo, cs, share(engines, i, len(ts_)), sem, ap(a), ap(dst)) for i, (cs, a, dst, sem) in enumerate(ts_)]
        op("G", [], [t[1] for t in ts_], lambda: g.remote_dma_fused(call, local_sem=T.sem.lsem), 500.0, raw=True, urge=urge)
        if urge:
            ops[-1]["outs"] = [b("calls")]
        local[0] += len(engines)

    others = [(rank + i) % N for i in range(1, N)]
    eo = len(topo.engines(T.cores[others[0]], core))
    spare = on_chip_only(topo, core, helpers[rank], T.cores[others[0]])

    def rows(t, grp):
        return T[t][16 * grp:16 * grp + 16, :]

    def tab(s, q, h):
        return T["tab%d" % s][32 * q + 16 * h:32 * q + 16 * h + 16, 0:W]
    k = 0
    for js in SENDS:
        if js == "tp":
            g.sync.dma_start(T.tpi[:, 0:128], T.tp[:, :]).then_inc(T.sem.ldn, 16)
            g.scalar.dma_start(T.tpi[:, 128:131], T.hw[:, :]).then_inc(T.sem.ldn, 16)
            g.scalar.dma_start(T.tpi[:, 131:132], T.th[:, :]).then_inc(T.sem.ldn, 16)
            landed("ldn", 48, [b("tpi", 0, 132)], 1900.0)
        elif js == "sd":
            g.sync.dma_start(T.tpi[:, 136:264], T.sd[:, :]).then_inc(T.sem.lds, 16)
            landed("lds", 16, [b("tpi", 136, 264)], 4000.0)
        for j in js if isinstance(js, tuple) else ():
            k += 1
            (g.sync if k % 2 else g.scalar).dma_start(piece(T, "zs", j), rows("tz", 2 * others[j % 3] + j // 3)).then_inc(T.sem["ld%d" % j], 16)
            landed("ld%d" % j, 16, [b("zs", j, j + 1)], 2000.0)
    count = {j: len(share(range(eo), i, len(js))) for js in SENDS if isinstance(js, tuple) for i, j in enumerate(js)}
    for s in range(2):
        for h in range(2):
            (g.scalar if h else g.sync).dma_start(tab(s, rank, h), rows("tz", 2 * rank + s)).then_inc(T.sem["tb%d" % s], 16)
    op("D", [b("later")], [], None, 7500.0, raw=True)
    for s in range(2):
        for q in others[::-1]:
            j = 2 * q + s

            def lay(e, h, s=s, q=q, j=j):
                e.wait_ge(T.sem["z%d" % j], count[3 * s + (rank - q - 1) % N])
                e.dma_start(tab(s, q, h), piece(T, "zl", j)).then_inc(T.sem["tb%d" % s], 16)
            lay(g.sync, 0)
            if s:
                lay(g.sync, 1)
            else:
                op("S", [b("lay")], [b("later")], lambda lay=lay: lay(g.scalar, 1), 64.0, raw=True, urge=1e5)
        landed("tb%d" % s, 128, [b("tab%d" % s, 0, W)], TABLES[s])
    n0 = rank * NAT
    for o, bank in ((0, "bK0"), (136, "bK1")):
        ts(b("t1", (o > 0) * 128, 128 + (o > 0) * 128), b("tpi", o, o + 128), 0, O.is_lt, EMPTY + 2049.0, O.mult)
        ts(b(bank), b("tpi", o, o + 128), -2048, O.add)
        tt(b("nat", n0 + o, n0 + o + 128), b("t1", (o > 0) * 128, 128 + (o > 0) * 128), b(bank), O.add)
    ts(b("nat", n0 + 128, n0 + 132), b("tpi", 128, 132), 4095.0, O.min, -2047.0, O.add)
    for k, js in enumerate(SENDS):
        if isinstance(js, str):
            lo, hi = (0, 132) if js == "tp" else (136, 264)
            send([([T.cores[d] for d in others], b("nat", n0 + lo, n0 + hi), b("nat", n0 + lo, n0 + hi), js + str(rank))], 1e6 - 1e4 * k)
        elif js in HELP:
            send([([helpers[rank]], b("zs", j, j + 1), b("zs", j, j + 1), "hx%d" % j) for j in js], 1e6 - 1e4 * k, spare)
        else:
            send([([T.cores[others[j % 3]]], b("zs", j, j + 1), b("zl", 2 * rank + j // 3, 2 * rank + j // 3 + 1), "z%d" % (2 * rank + j // 3))
                  for j in js], 1e6 - 1e4 * k)
    for q in others:
        landed("tp%d" % q, eo, [b("nat", q * NAT, q * NAT + 132)], TABLES[2])
        landed("sd%d" % q, eo, [b("nat", q * NAT + 136, q * NAT + 264)], TABLES[3])

    iota(b("pi", 0, 8), [[0, 8]], 0, 1)
    iota(b("ji"), [[1, 128]], 0, 0)
    ts(b("di"), b("ji"), 4, O.arith_shift_right)
    ts(b("di", 128, 256), b("ji"), 111, O.bitwise_and)
    cp(b("j16"), b("di")); cp(b("i2"), b("di", 128, 256))
    for h in range(2):
        iota(b("IW", 64 * h, 64 * h + 64), [[4, 4], [1, 4], [16, 4]], 128 + 64 * h, 0)
        iota(b("IW", 128 + 64 * h, 192 + 64 * h), [[1, 4], [16, 4], [4, 4]], 64 * h, 0)
    cp(b("jf"), b("ji"))
    c1 = lambda n, i: b(n, i, i + 1)
    for i, (sh, mask) in enumerate(((0, 127), (4, 7), (0, 15), (5, 3), (4, 1), (2, 3), (0, 3))):
        ts(c1("pi", 8 + i), c1("pi", 0), sh, O.arith_shift_right, mask, O.bitwise_and)
    cp(b("pf", 0, 7), b("pi", 8, 15))
    pp, pu, pl, pq, ph, pj, pr = [c1("pf", i) for i in range(7)]
    for i in range(2):
        ts(b("I2", 128 * i, 128 * i + 128), b("jf"), pp, O.is_equal)
    Ib = b("I2")

    def sfill(out, c):
        n = size(out)
        act(out, b("d0h", 0, n), F.Identity, scale=0.0, bias=c)
    cp(b("Ih"), Ib); act(b("If"), Ib, F.Copy)
    ts(b("HI"), Ib, 0.5, O.mult)
    ts(b("BD"), b("j16"), pu, O.is_equal)
    act(b("BDf"), b("BD"), F.Copy)
    fill(b("d0h", 0, 512), 255.0); fill(b("d0h", 0, 512, 4), 0.0)
    act(b("d0l", 0, 512), b("d0h", 0, 512), F.Identity, scale=-1.0, bias=255.0)
    act(b("d04", 0, 256), b("d0h", 0, 256), F.Identity, scale=-16.0, bias=4096.0)
    sfill(b("d0k", 0, 64), -1.0e9); sfill(b("d0k", 0, 64, 16), 1.0e9)
    sfill(b("ZV", 0, 144), 0.0)
    act(b("ZV", 16, 144, 16), b("BD", 0, 128, 16), F.Identity, scale=4096.0)
    act(b("ZA", 0, 144), b("ZV", 0, 144), F.Identity, scale=-2.0)
    ts(b("ZE", 0, 144), b("ZV", 0, 144), -0.5, O.mult)
    ts(b("Z1", 0, 144), b("ZV", 0, 144), 1.0 / 4096, O.mult)
    for m in range(16):
        act(b("EXP", m, 1024, 16), b("I2", 0, 64), F.Copy)
    ts(c1("pf", 40), pl, 0.0, O.is_equal, -0.5, O.mult)
    ts(b("NH", 0, 256), b("d0h", 0, 256), 0.0, O.mult, c1("pf", 40), O.add)
    act(b("NH", 0, 256), b("NH", 0, 256), F.Identity, bias=128.0)
    sfill(b("NH", 256, 512), 2048.0); sfill(b("zb", 0, 16), 0.0)
    ts(b("m384", 0, 64), b("d0h", 0, 64), 0.0, O.mult, -384.0, O.add)
    ts(b("m2k", 0, 64), b("d0h", 0, 64), 0.0, O.mult, -2048.0, O.add)
    for c in range(4 if FUSE else 0):
        ts(b("m2k", 64 + 16 * c, 80 + 16 * c), b("jf", 0, 16), float(FUSE // 64), O.is_lt, -2048.0, O.mult)
    sfill(b("CC", 0, 128, 2), -2048.0); sfill(b("CC", 1, 128, 2), 0.0)
    sfill(b("F1", 0, 272), EMPTY); sfill(b("F1", 128, 256), -4096.0)
    sfill(b("F2", 0, 272), 0.0); sfill(b("F2", 128, 256), 1.0)
    ts(c1("pf", 8), pl, 64.0, O.mult)
    ts(c1("pf", 7), pl, float((SUB + FUSE) // 64), O.is_ge, 2.0 ** 26, O.mult)
    if SUB:
        ts(b("IN"), Ib, -1.0, O.mult)
    ts(b("KC", 0, 64), b("jf", 0, 64), c1("pf", 8), O.add)
    ts(c1("pf", 9), pl, 16.0, O.mult, 1024.0, O.add)
    ts(b("df", 0, 64), b("j16", 0, 64), 240.0, O.mult, c1("pf", 9), O.add)
    tt(b("KC", 64, 128), b("df", 0, 64), b("jf", 0, 64), O.add)
    ts(b("OHW", 0, 16), b("jf", 0, 16), pl, O.is_equal)
    for u in range(8):
        ts(b("GO", 128 * u, 128 * u + 128), b("BD"), 0.0, O.mult, c1("BD", 16 * u), O.add)
    tcol, rq = b("ji", 0, 6), b("pi", 24, 30)
    ts(b("pi", 40, 46), tcol, -1.0, O.mult, pq, O.add)
    ts(b("pi", 40, 46), b("pi", 40, 46), 7, O.add)
    ts(rq, b("pi", 40, 46), 3, O.bitwise_and)
    ts(c1("pf", 10), ph, 4.0, O.mult)
    ts(b("pf", 32, 38), rq, c1("pf", 10), O.add)
    for t in range(RO):
        ts(c1("pf", 16 + t), pl, float(XL[t]), O.is_equal)
        ts(b("nS", 8 * t, 8 * t + 8), b("jf", 0, 8), c1("pf", 32 + t), O.is_equal)
    ts(b("cx", 0, 6), b("pf", 16, 22), EMPTY + 4096.0, O.mult, -4096.0, O.add)
    tt(c1("pi", 1), c1("pi", 11), c1("pi", 13), O.subtract)
    ts(c1("pi", 2), c1("pi", 1), 3, O.bitwise_and)
    ts(c1("pf", 11), c1("pi", 2), 4.0, O.mult, pr, O.add)
    ts(c1("pf", 12), pj, 2.0, O.mult, ph, O.add)
    ts(c1("pf", 12), c1("pf", 12), 16.0, O.mult, c1("pf", 11), O.add)
    ts(b("PERM"), b("jf"), c1("pf", 12), O.is_equal)
    ts(c1("pf", 13), pq, 16.0, O.mult, pl, O.add)
    ts(c1("pf", 14), c1("pf", 13), 2.0, O.mult, ph, O.add)
    ts(b("SR", 256, 384), b("jf"), c1("pf", 14), O.is_equal)
    ts(c1("pf", 13), pq, 32.0, O.mult, pl, O.add)
    ts(c1("pf", 15), ph, -1.0, O.mult, 1.0, O.add)
    ts(b("SR", 0, 128), b("i2"), c1("pf", 13), O.is_equal, c1("pf", 15), O.mult)
    ts(b("SR", 128, 256), b("i2"), c1("pf", 13), O.is_equal, ph, O.mult)
    mm(b("bM1", 0, 1), b("IW"), b("I2", 0, 128, 128))
    mm(b("bM1", 1, 2), b("IW"), b("I2", 0, 128, 128))
    cp(b("w2", 0, 2), b("bM1", 0, 2))
    cp(b("IW", 256, 384), b("jf"))
    for i, o in enumerate((128, 256, 0)):
        mm(b("bM1", 2 + i, 3 + i), b("IW", o, o + 128), b("I2", 0, 128, 128))
        sfill(b("MB", 260 * i + 256, 260 * i + 260), 0.0)
        for r in range(2):
            ts(b("MB", 260 * i + 128 * r, 260 * i + 128 * r + 128), b("IW", o, o + 128), c1("bM1", 2 + i), O.is_le, 16384.0, O.mult)
    mm(b("bE1", 0, 384), b("PERM"), b("SR", 0, 384))
    mm(b("bE1", 384, 512), b("PERM"), b("Ih"))
    cp(b("SH", 0, 256), b("bE1", 0, 256)); cp(b("OUTP"), b("bE1", 256, 384)); cp(b("SH", 256, 384), b("bE1", 384, 512))
    cp(b("BDh"), b("BD"))
    mm(b("bF1"), b("BDh"), b("PERM"))
    ts(b("t1"), b("PERM"), 16.0, O.mult)
    tt(b("t2"), b("t1"), b("bF1"), O.subtract)
    for i, (a, c) in enumerate((("t2", 8192.0), ("t2", -8192.0), ("bF1", 8192.0), ("bF1", -8192.0), ("PERM", 8192.0))):
        if a == "PERM":
            ts(b("cAB", 128 * i, 128 * i + 128), b(a), c, O.mult)
        else:
            act(b("cAB", 128 * i, 128 * i + 128), b(a), F.Identity, scale=c)
    ts(b("Sin", 0, 96), b("d0h", 0, 96), 0.0, O.mult)

    def stream(s):
        grp = 2 * rank + s
        B = lambda n, *a, **k: b(n + str(s), *a, **k)
        P, Pm, E2, B0, Pw = B("P", 1, 128, 2), B("Pm", 0, 64), B("E2", 3, 256, 4), B("B0", 0, 64), B("fw", 65, 192, 2)
        table, KT = B("tab", 0, W + 16), B("hwf", 8, 12)
        z0 = 48 * s
        cp(b("Sin", z0 + 16, z0 + 32), b("Ih", 16 * grp, 16 * grp + 16))
        for h in range(2):
            cp(b("Sin", 96 + 32 * s + 16 * h, 112 + 32 * s + 16 * h), b("Ih", 16 * grp, 16 * grp + 16))
        fill(B("tab", W, W + 16), -256.0)
        ops[-1]["ins"] = [b("lay")]
        sfill(B("Wn", 0, 272), EMPTY)
        ts(B("hwf", 4, 5), ph, 256.0, O.mult, EMPTY + 2048.0, O.add)
        ts(B("hn", 128, 192), b("jf", 0, 64), 4.0, O.mult, B("hwf", 4, 5), O.add)
        block, comb = (lambda n, d, o=0: B(n, o + 16 * d, o + 16 * d + 16)), (lambda n, d, o=0: B(n, o + d, o + 64, 4))

        def by_rows(o):
            for r in range(N):
                for h in range(2):
                    c = r * NAT + o + 64 * h
                    mm(B("bM", 0, 64, p=(32 * r, 32 * r + 32)), b("Sin", z0 + 16 - 16 * h, z0 + 48 - 16 * h), b("nat", c, c + 64), h == 0, h == 1)
            cp(B0, B("bM", 0, 64))

        def seeds():
            by_rows(136)
            for d in range(4):
                mm(comb("bM", d), b("Ih"), block("B0", d))
                mm(block("bM", d, 64), b("Ih"), comb("B0", d))
            mm(B("bM", 128, 192), b("Ih"), B0)
            act(B("Sd", 0, 192), B("bM", 0, 192), F.Copy)
        by_rows(0)
        mm(B("bE", 0, 64), b("PERM"), B0)
        for r in range(N):
            mm(B("bM", 128, 132, p=(32 * r, 32 * r + 32)), b("Sin", 96 + 32 * s, 128 + 32 * s), b("nat", r * NAT + 128, r * NAT + 132))
        ts(B("hwf", 0, 4), B("bM", 128, 132), 2047.0, O.add)
        fill(B("fw", 64, 192, 2), 1.0e9)
        for i in range(2):
            ts(B("WW", 128 * i, 128 * i + 128), b("BD"), B("hwf", i, i + 1), O.mult, 0.5, O.mult)
            mm(B("bK", 256 + i, 257 + i), B("WW", 128 * i, 128 * i + 128), c1("m2k", 0))
        cp(B("hwf", 6, 8), B("bK", 256, 258))
        ts(b("df"), b("If"), B("hwf", 2, 3), O.mult)
        mm(B("bK"), b("BDf"), b("df"))
        ts(b("di"), B("bK"), B("hwf", 1, 2), O.mult, 2080.0, O.add)
        ts(b("di", 128, 256), b("di"), 63, O.bitwise_and)
        ts(B("WW", 256, 384), b("di", 128, 256), -32.0, O.add, 0.5, O.mult)
        ts(b("di", 128, 256), b("di"), 6, O.arith_shift_right, 63, O.bitwise_and)
        ts(B("WW", 384, 512), b("di", 128, 256), -32.0, O.add, 32.0, O.mult)
        ts(B("hwf", 5, 6), B("hwf", 3, 4), -0.5, O.add, 4096.0, O.mult)
        ts(B("hwf", 5, 6), B("hwf", 5, 6), c1("pf", 8), O.add, c1("pf", 7), O.add)
        ts(KT, b("jf", 0, 4), 16.0, O.mult, B("hwf", 5, 6), O.add)
        lane = lambda z, l: b(z, 16 - l, 144 - l)

        def hashes(p):
            iw = lambda i, n=1: B("iw", 64 * i, 64 * (i + n))
            hn = B("hn", 64 * p, 64 * p + 64)
            C, w = B("C2", 0, 64) if p else E2, lambda i: B("WW", 128 * i, 128 * i + 128)
            for i in range(2):
                mm(B("bM", 192 + 64 * i, 256 + 64 * i), w(i), C)
            for i in range(2):
                ts(iw(i), B("bM", 192 + 64 * i, 256 + 64 * i), B("hwf", 6 + i, 7 + i), O.add)
            for j, (i, v) in enumerate(((3, b("m2k", 0, 64)), (2, b("m2k", 0, 64)), (3, C), (2, C))):
                mm(B("bM", 320, 384), w(i), v, j == 0, j == 3)
            ts(iw(2, 2), iw(0, 2), 4095, O.bitwise_and)
            tt(iw(4), iw(2), iw(3), O.mult)
            ts(iw(5), iw(4), 5, O.arith_shift_right)
            tt(iw(6), iw(5), B("bM", 320, 384), O.add)
            ts(hn, iw(6), 4095, O.bitwise_and)
            if p == 0:
                cp(B("hl", 0, 64), hn)
            for c in range(4 * p):
                cp(comb("hl", c), block("hn", c, 64))

        def search(p):
            key = B("bK", 64 * p, 64 * p + 64)
            mm(key, b("Ih"), b("KC", 64 * p, 64 * p + 64), True, False)
            sums, fillp, e16s = [0], {"bE": 0, "bF": 0}, []
            for lo, hi, e, bank in CAND:
                e16s.append(B(bank, fillp[bank], fillp[bank] + hi - lo))
                fillp[bank] += hi - lo
                if p == 0 and lo >= SUB:
                    mm(e16s[-1], B("ET", p=(0, 64)), b("EXP", lo, hi, p=(0, 64)))
            if SUB:
                mm(B("bF", 0, SUB), B("ET", p=(0, 64)), b("EXP", 0, SUB, p=(0, 64)), True, False)
            for (lo, hi, e, bank), e16 in zip(CAND, e16s):
                if hi <= FUSE:
                    if p == 0:
                        act(B("Ga", lo, hi), e16, F.Copy)
                    tt(B("V", lo, hi), B("hl", lo // 16, hi // 16), B("Ga", lo, hi), O.subtract, win=table)
                    if RELU:
                        ts(B("A", lo, hi), B("V", lo, hi), 0.0, O.min)
                        for l in range(lo // 64, hi // 64):
                            mm(key, lane("ZV", l), B("V", 64 * l, 64 * l + 64), False, sums)
                    else:
                        act(B("A", lo, hi), B("V", lo, hi), F.Abs)
                    for l in range(lo // 64, hi // 64):
                        mm(key, lane("ZA" if RELU else "ZV", l), B("A", 64 * l, 64 * l + 64), False, sums)
                    continue
                gather(e, B("V", lo, hi), table, B("hl", lo // 16, hi // 16))
                if lo < SUB:
                    mm(e16, b("IN"), B("V", lo, hi), False, hi == SUB)
                    if hi == SUB:
                        act(B("A", 0, SUB), B("bF", 0, SUB), F.Abs)
                        for l in range(SUB // 64):
                            mm(key, lane("ZV", l), B("A", 64 * l, 64 * l + 64), False, sums)
                    continue
                for l in range(lo // 64, hi // 64):
                    mm(key, lane("ZV", l), B("V", 64 * l, 64 * l + 64), False, sums)
                tt(B("A", lo, hi), B("V", lo, hi), e16, O.min)
                for l in range(lo // 64, hi // 64):
                    mm(key, lane("ZA", l), B("A", 64 * l, 64 * l + 64), False, sums)
            scan(B("km", 0, 64), b("d0k", 0, 64), key, O.max, O.min)

        for t in range(RO):
            now = P if t else B("bE", 0, 64)
            ts(B("offs", 0, 64), now, 2048.0, O.min, 2048.0, O.add)
            mm(B("bF", 0, 256), b("BD"), b("NH", 0, 256), True, False)
            if TURN == "V":
                for d in range(4):
                    ts(comb("Pm", d), B(now[0][:-1], now[1] + 16 * d * now[3], now[1] + (16 * d + 15) * now[3] + 1, now[3]), EMPTY, O.min, c1("cx", t), O.max)
            else:
                ts(Pm, now, EMPTY, O.min, c1("cx", t), O.max)
            for h in range(3):
                if TURN == "V":
                    mm(B("bK", 256 + 64 * h, 320 + 64 * h), b("SH", 128 * h, 128 * h + 128), Pm)
                for d in range(4 * (TURN == "T")):
                    mm(comb("bK", d, 256 + 64 * h), b("SH", 128 * h, 128 * h + 128), block("Pm", d))
            act(B("Wn", 128, 256), B("bK", 256, 384), F.Copy)
            act(B("Pr", 0, 64), B("bK", 384, 448), F.Identity, scale=-1.0, bias=4096.0)
            ts(B("Pr", 64, 128), B("bK", 384, 448), 3000.0, O.min)
            for lo, hi, e in MID:
                gather(e, B("Gv", lo, hi), table, B("offs", lo // 16, hi // 16))
            for lo, hi, again in ABS:
                if again:
                    act(B("Ga", lo, hi), B("offs", lo // 16, hi // 16), F.Abs, win=table)
                else:
                    act(B("Ga", lo, hi), B("Gv", lo, hi), F.Abs)
            part = lambda nm, d: B(nm, 4 * ((d - 1 - t) % N) + 3, 1024, 16)
            shift = lambda d: b("I2", 128 - 32 * d, 256 - 32 * d)
            for lo, hi, e in MID:
                scan(B("Hi", lo, hi), b("d0h", 0, hi - lo), B("Gv", lo, hi), O.min, O.max)
            m = part("Hi", 0)
            for d in range(1, 4):
                mm(B("bE", 64 * d, 64 * d + 64), shift(d), part("Hi", d))
            for d in range(1, 4):
                tt(B("HL", 64 * d - 64, 64 * d), B("bE", 64 * d, 64 * d + 64), m, O.max)
                m = B("HL", 64 * d - 64, 64 * d)
            for lo, hi, again in ABS:
                scan(B("Lo", lo, hi), b("d0l", 0, hi - lo), B("Ga", lo, hi), O.max, O.min)
            sums = [0]
            for d in range(4):
                mm(B("bF", d, 256, 4), Ib, m, False, sums)
                mm(B("bF", d, 256, 4), shift(d), part("Lo", d), False, sums)
            scan(B("E2", 0, 256), b("d04", 0, 256), B("bF", 0, 256), O.max, O.min)
            mm(B("bK", 256, 384, p=(0, 64)), E2, b("HI"))
            act(B("ET", p=(0, 64)), B("bK", 256, 384, p=(0, 64)), F.Identity, bias=-1024.0)
            hashes(0)
            if FUSE:
                mm(B("bM", 0, 64), b("HI"), b("m2k", 64, 128), True, False)
                for c in range(4):
                    mm(B("bM", 16 * c, 16 * c + FUSE // 64), b("HI"), B("E2", 4 * c + 3, FUSE // 4, 16), False, False)
            for c in range(4):
                mm(block("bM", c), b("HI"), B("E2", 4 * c + 3, 256, 16), not FUSE, c == 3 or not FUSE)
            act(B("Epl", 0, 64), B("bM", 0, 64), F.Identity, bias=1023.5)
            search(0)
            th = B("bK", 128, 132)
            mm(th, b("If"), KT, True, False)
            for l in range((SUB + FUSE) // 64, 16):
                mm(th, lane("ZE", l), B("E2", 16 * l + 3, 16 * l + 16, 4), False, l == 15)
            k4 = B("km", 15, 64, 16)
            if COLS:
                ts(B("km", 68, 72), k4, M12, O.add, -M12, O.add)
                for c in range(4):
                    ts(B("lz", c, c + 1), B("km", 16 * c + 15, 16 * c + 16), B("km", 68 + c, 69 + c), O.subtract)
            else:
                cp(B("ki", 0, 4), k4)
                ts(B("ki", 4, 8), B("ki", 0, 4), 1023, O.bitwise_and)
                cp(B("lz", 0, 4), B("ki", 4, 8))
            tt(B("C2", 0, 64), B("lz", 0, 4), B("Epl", 0, 64), O.add, win=B("V", 0, 1024))
            tt(B("km", 64, 68), k4, th, O.min)
            hashes(1)
            if t == 0:
                seeds()
            search(1)
            for bank in ("bE", "bF"):
                mm(B(bank, 0, 260), Ib, b("MB", 260 * (t % 3), 260 * (t % 3) + 260), True, False)
            tt(B("ki", 0, 4), k4, B("km", 64, 68), O.min)
            ts(B("ki", 4, 8), B("ki", 0, 4), 4, O.arith_shift_right, 255, O.bitwise_and)
            ts(B("ki", 8, 12), B("ki", 0, 4), 15, O.bitwise_and)
            cp(B("lz", 4, 12), B("ki", 4, 12))
            ts(B("pd", 64, 128), B("lz", 4, 8), -2048.0, O.add, win=B("hn", 0, 192))
            pd = B("pd", 0, 64)
            tt(pd, B("lz", 8, 12), B("pd", 64, 128), O.mult, win=b("OHW", 0, 16))
            for i, bank in enumerate(("bE", "bF")):
                for h in range(2):
                    n = 8 * t + 4 * h + 2 * i
                    mm(B(bank, 256, 258, p=(64 * h, 64 * h + 64)), pd, b("nS", n, n + 2), False, False)
                for j in range(4):
                    u = 2 * ((2 * i + j // 2 + 1 + t) % N) + j % 2
                    mm(B(bank, 64 * j, 64 * j + 64), b("GO", 128 * u, 128 * u + 128), pd, False, j == 3)
            sx = lane("Z1", XL[t])
            mm(B("bM", 384, 448), sx, b("m384", 0, 64), True, False)
            if TURN == "V":
                mm(B("bM", 384, 448), b("Ih"), Pm, False, False)
            for c in range(4 * (TURN == "T")):
                mm(comb("bM", c, 384), b("Ih"), block("Pm", c), False, False)
            for c in range(4):
                mm(block("bM", c, 384), sx, comb("pd", c), False, c == 3)
            ys = [B("bM" if r // 2 else "bK", 448 + r, 449 + r) for r in range(N)]
            for r in range(N):
                xr_, bank = B("X", 128 * r, 128 * r + 128), "bF" if r // 2 else "bE"
                ts(xr_, B(bank, 128 * (r % 2), 128 * (r % 2) + 128), B(bank, 256 + r % 2, 257 + r % 2), O.is_equal)
                mm(ys[r], xr_, c1("w2", 0))
            for c in range(4):
                mm(B("bE", c, c + 1), B("X", c, 512, 4), c1("w2", 0))
            for r in range(N):
                ts(B("M", 128 * r, 128 * r + 128), b("IW"), ys[r], O.is_equal)
            mm(B("bK", 200, 208), Ib, b("zb", 0, 8), True, False)
            for c in range(4):
                mm(B("bK", 200 + c, 201 + c), B("X", c, 512, 4), c1("w2", 0), False, False)
            act(Pw, B("bM", 384, 448), F.Copy)
            LB, L, LA = B("lz", 12, 16), B("lz", 16, 20), B("lz", 20, 24)
            ts(LB, B("bE", 0, 4), 256.0, O.min)
            for c in range(4):
                mm(B("bK", 200 + c, 208, 4), B("M", c, 512, 4), b("w2", 0, 2), False, c == 3)
            win = B("Wn", 0, 272)
            tt(B("fw", 0, 64), LB, B("Sd", 64 * (t % 3), 64 * (t % 3) + 64), O.max, win=b("F1", 0, 272))
            act(B("gg", 128, 192), LB, F.Copy, win=b("F2", 0, 272))
            ts(B("lz", 16, 24), B("bK", 200, 208), 256.0, O.min)
            tt(B("gg", 0, 64), L, B("Pr", 0, 64), O.is_lt, win=win)
            tt(B("gg", 64, 128), L, B("Pr", 64, 128), O.is_equal, win=win)
            tt(B0, LA, B("fw", 0, 64), O.min, win=win)
            mm(B("bF"), Ib, b("CC"), True, False)
            sums = [0]
            for c, w, i, v, o in ((0, "cAB", 4, "gg", 128), (0, "cAB", 0, "gg", 0), (1, "cAB", 2, "gg", 0), (0, "cAB", 1, "gg", 64),
                                  (1, "cAB", 3, "gg", 64), (1, "PERM", 0, "B0", 0)):
                mm(B("bF", c, 128, 2), b(w, 128 * i, 128 * i + 128), B(v, o, o + 64), False, sums)
            scan(B("P"), B("fw", 64, 192), B("bF"), O.max, O.min)
        ts(Pm, P, 2047.0, O.min)
        ts(B("pd", 0, 64), P, 2048.0, O.is_ge, -4096.0, O.mult)
        mm(B("bK", 0, 64), Ib, b("NH", 256, 320), True, False)
        for v in ("Pm", "pd"):
            mm(B("bK", 0, 64), b("OUTP"), B(v, 0, 64), False, v == "pd")
        cp(B("yo", 0, 64), B("bK", 0, 64))
        send([([T.cores[d] for d in others], B("yo", 0, 64), b("yl", 64 * grp, 64 * grp + 64), "y%d" % grp)], 0.0)
        mine = (32 * rank, 32 * rank + 32)
        op("Y", [], [B("yo", 0, 64)], lambda: g.sync.dma_start(rows("yp", grp), ap(B("yo", 0, 64, p=mine))).then_inc(T.sem.st, 16), 50.0, raw=True)
        for i, q in enumerate(others[::-1]):
            gq = 2 * q + s
            e, en = (g.scalar, "S") if i == 1 and s == 1 else (g.sync, "Y")

            def home(gq=gq, e=e):
                e.wait_ge(T.sem["y%d" % gq], eo)
                e.dma_start(rows("yp", gq), ap(b("yl", 64 * gq, 64 * gq + 64, p=mine))).then_inc(T.sem.st, 16)
            op(en, [], [B("yo", 0, 64)], home, 50.0, raw=True)

    for s in range(2):
        i0 = len(ops)
        stream(s)
        for o in ops[i0:len(ops) - LAST]:
            o["lead"] = LEAD * (1 - s)
    ops2 = order(ops)
    if report is not None:
        report.extend(ops2)
    issue(g, T, ops2)
    g.sync.wait_ge(T.sem.st, 128)
    g.wait_ge(T.sem.lsem, local[0])
